import numpy as np, ml_dtypes
CORES = [3,11,19,27,35,43]
N = 6
BF = ml_dtypes.bfloat16
def gentries(a):
    return np.ascontiguousarray(a.reshape(8, 16, -1).transpose(0, 2, 1)).reshape(8, -1)
def gtable(e):
    e = np.asarray(e); return np.ascontiguousarray(e.reshape(8, -1, 16).transpose(0, 2, 1)).reshape(128, -1).astype(np.int32)
V, B, T, S, LH = 3072, 384, 256, 6, 3
M = V + T * S
def rows_of(rng, u):
    y = np.sort((u * (V - 15)).astype(np.int64), axis=-1) + np.arange(16)
    return rng.permuted(y, axis=-1)
def homes(rng, sb):
    he = rng.integers(0, B, (N, 8, V))
    for r in range(N):
        for g in range(8):
            o = rng.permutation(16 * B); he[r, g, sb[r, g].reshape(-1)[o]] = o >> 4
    return he
def parts(rng):
    sb = rows_of(rng, rng.random((N, 8, B, 16))); he = homes(rng, sb)
    x = rng.integers(0, 64, (N, 8, 16, V)); z = rng.integers(0, 64, (N, 8, 16, T))
    pe = (B * rng.random((N, 8, V)) ** 2).astype(np.int64); bx = (B * rng.random((N, 8, T)) ** 2).astype(np.int64)
    lim = np.stack([rng.integers(100, 450, (N, 8)), rng.integers(180, 320, (N, 8))], axis=-1)
    return x, sb, pe, he, bx, z, lim
def pack(x, sb, pe, he, bx, z, lim):
    w = lambda a: np.ascontiguousarray(a).astype(np.int32)
    return {"xs": x.reshape(N, 128, V).astype(np.float32).astype(BF), "sb": np.stack([gtable(a.reshape(8, -1)) for a in sb]), "pe": w(pe), "he": w(he),
            "bx": w(bx), "zs": z.reshape(N, 128, T).astype(np.float32).astype(BF), "lim": w(lim)}
def setup_inputs(rng):
    return pack(*parts(rng))
def setup_inputs_spread(rng):
    x, sb, pe, he, bx, z, lim = parts(rng)
    sb = rows_of(rng, rng.random((N, 8, B, 16)) ** rng.choice(np.array([1.0, 2.0, 4.0]), (N, 8, 1, 1))); he = homes(rng, sb)
    x = (64 * rng.random(x.shape) * np.exp2(-rng.integers(0, 6, (N, 8, 1, V)))).astype(np.int64)
    z = (64 * rng.random(z.shape) * np.exp2(-rng.integers(0, 6, (N, 8, 1, T)))).astype(np.int64)
    bx = (B * rng.random((N, 8, T)) ** rng.choice(np.array([1.0, 2.0, 4.0]), (N, 8, 1))).astype(np.int64)
    lim = np.minimum((np.exp2(10 * rng.random((N, 8, 2)))).astype(np.int64), 1023); lim[:, 0, 0] = 0; lim[:, 1, 0] = 1023; lim[:, 2, 1] = 0; lim[:, 3, 1] = 1023
    return pack(x, sb, pe, he, bx, z, lim)
def setup_inputs_ends(rng):
    base = np.concatenate([np.arange(8), np.arange(V - 8, V)])
    sb = rng.permuted(np.broadcast_to(base, (N, 8, B, 16)).copy(), axis=-1)
    pe = (B - 1) * rng.integers(0, 2, (N, 8, V)); he = (B - 1) * rng.integers(0, 2, (N, 8, V)); bx = (B - 1) * rng.integers(0, 2, (N, 8, T))
    m = rng.integers(0, 3, (N, 8, 1, V)); x = 63 * np.where(m == 2, rng.integers(0, 2, (N, 8, 16, V)), m)
    m = rng.integers(0, 3, (N, 8, 1, T)); z = 63 * np.where(m == 2, rng.integers(0, 2, (N, 8, 16, T)), m)
    x[:, 2][:, :, base] = 63; z[:, 2] = 63
    for g in (3, 7):
        x[:, g][:, :, base] = 0; z[:, g] = 63
    for g in (1, 5):
        x[:, g][:, :, base] = 63; x[:, g][:, :, V - 1] = 0; z[:, g] = 0; he[:, g][:, base] = B - 1
    he[:, 7][:, base] = B - 1
    for g in (4, 7):
        bx[:, g] = 0; bx[:, g, T - 1] = B - 1
    h = (np.arange(8)[None, :] + N - 1 - np.arange(N)[:, None]) & 7
    lim = 1023 * np.stack([h & 1, (h >> 1) & 1], axis=-1)
    return pack(x, sb, pe, he, bx, z, lim)
def setup_inputs_corners(rng):
    x, sb, pe, he, bx, z, lim = parts(rng)
    for r in range(N):
        for g in range(8):
            k = g & 3
            if k == 0:
                m = int(rng.integers(100, 400)); extra = (rng.random(V) < 0.85).astype(np.int64)
                x[r, g] = (m >> 4) + (np.argsort(rng.random((16, V)), axis=0) < (m & 15) + extra[None, :])
                z[r, g] = 0; lim[r, g] = (1000, m)
            elif k == 1:
                i, j = rng.permutation(16)[:2]; x[r, g] = 20; x[r, g, i] += rng.integers(0, 16, V); x[r, g, j] += rng.integers(0, 16, V)
                z[r, g] = 20; lim[r, g] = (int(rng.integers(4, 9)), 1023)
            elif k == 2:
                sec = np.concatenate([np.array([0, V - 1]), 1 + rng.permutation(V - 2)[:14]])
                sb[r, g] = rng.permuted(np.tile(sec, (B, 1)), axis=-1)
                for j in range(8):
                    sb[r, g, B - 1 - j] = np.concatenate([sec[2 * j:2 * j + 2], rng.permutation(np.delete(sec, [2 * j, 2 * j + 1]))])
                he[r, g, sec] = B - 1 - (np.arange(16) >> 1)
                if r % 2 == 0: he[r, g, sec[2:]] = np.arange(14)
                x[r, g][:, sec] = 31; bx[r, g] = rng.integers(0, B, T); o = rng.permutation(T)[:32]; bx[r, g, o] = B - 1 - (np.arange(32) & 7)
                lim[r, g] = (1023, 1023)
            else:
                pe[r, g] = np.where(rng.random(V) < 0.5, he[r, g], pe[r, g])
                x[r, g] = 63 * rng.integers(0, 2, (1, V)); z[r, g] = 63 * rng.integers(0, 2, (1, T))
                bx[r, g] = rng.choice(np.array([0, 1, B - 2, B - 1]), T)
                lim[r, g] = (int(rng.choice(np.array([1, 8, 1023]))), int(rng.choice(np.array([0, 1007, 1008, 1023]))))
    return pack(x, sb, pe, he, bx, z, lim)
def setup_inputs_crowd(rng):
    x, sb, pe, he, bx, z, lim = parts(rng)
    at = (0, B - 1, B >> 1, B - 1, 5, B - 2, 1, B - 1)
    for r in range(N):
        for g in range(8):
            a = at[g]; bx[r, g] = a
            if g != 6: z[r, g] = z[r, g, :, :1]
            if g == 2: bx[r, g, 0] = 0
            if g == 3: bx[r, g, T - 1] = 3
            if g in (4, 5):
                sb[r, g, a - 1] = rng.permutation(sb[r, g, a])
                if g == 4: bx[r, g, rng.permutation(T)[:T >> 1]] = a - 1
                else: bx[r, g, int(rng.integers(0, T))] = a - 1
            if g == 6: bx[r, g] = rng.integers(0, 4, T)
            if g == 7:
                x[r, g][:, sb[r, g, a]] = x[r, g][:, sb[r, g, a, :1]] & 3; z[r, g] = z[r, g] & 3
                far = rng.permutation(sb[r, g, a])[2 * S - 2:]; x[r, g][:, far] = rng.integers(40, 64, (16, far.size))
                pe[r, g, sb[r, g, a]] = a
            he[r, g, sb[r, g, a]] = a; lim[r, g, 0] = (300, 500, 700, 1000)[g & 3]
            if g != 0: lim[r, g, 1] = int(rng.integers(250, 500))
    return pack(x, sb, pe, he, bx, z, lim)
def setup_inputs_busy(rng):
    x, sb, pe, he, bx, z, lim = parts(rng); K = V >> 4; z = 0 * z + 8
    for g in range(8):
        H = rng.permutation(B)[:K]
        for r in range(N):
            o = rng.permutation(V); own = o.reshape(K, 16); he[r, g, o] = np.repeat(H, 16)
            nx = np.arange(K); nx[0:8:2] += 1; nx[1:8:2] -= 1
            if g & 1:
                src = np.concatenate([np.arange(1, 8, 2), np.arange(8, K)]); nx[src] = rng.permutation(nx[src])
            pe[r, g, o] = np.repeat(H[nx], 16)
            sb[r, g, H] = own; sb[r, g, H[1:8:2], 0] = own[0:8:2, 1]
            far = (np.arange(K) >= 16) & (rng.random(K) < 0.25)
            w = np.where(far, rng.integers(14, 51, K), 0); c = np.where(far, 3, rng.integers(0, 7, K)); c[:16] = 0
            x[r, g][:, o] = 8 + np.repeat(w, 16) * rng.integers(0, 2, (16, V)) + (rng.random((16, V)) * (np.repeat(c, 16) + 1)).astype(np.int64)
            first = np.arange(1, K)
            if S & 1: first = np.delete(first, 7)
            mid = np.concatenate([first, np.arange(16, K)])[:T - 2]
            bx[r, g] = H[np.concatenate([np.array([0]), rng.permutation(mid), np.array([8 if S & 1 else 0])])]
            lim[r, g] = (int(rng.integers(97, 130)), 300 if g == 5 else 1023)
    H = rng.permutation(B)[:K]
    for r in range(N):
        o = rng.permutation(V); own = o.reshape(K, 16); sb[r, 6, H] = own
        ex = np.concatenate([31 + rng.permutation(31), rng.permutation(31), np.arange(62, K)])
        ho = np.concatenate([np.arange(62), np.roll(np.arange(62, K), 1)])
        pe[r, 6, o] = np.repeat(H[ex], 16); he[r, 6, o] = np.repeat(H[ho], 16)
        x[r, 6] = rng.integers(0, 64, (16, V))
        x[r, 6][:, own[:31].reshape(-1)] = rng.integers(8, 10, (16, 31 * 16))
        x[r, 6][:, own[31:62].reshape(-1)] = rng.integers(40, 64, (16, 31 * 16))
        two = np.argsort(rng.random((31, 16)), axis=1)[:, :2]; b = 31 + np.arange(31)
        m = int(lim[r, 6, 0]) + 240 + rng.permutation(31) - 8
        x[r, 6][:, own[b, two[:, 0]]] = 8
        x[r, 6][:, own[b, two[:, 1]]] = 8 + (m >> 4) + (np.argsort(rng.random((16, 31)), axis=0) < (m & 15))
        i = rng.permutation(T); bx[r, 6, i[:31]] = H[:31]; bx[r, 6, i[31:]] = H[rng.integers(62, K, T - 31)]
        z[r, 6] = rng.integers(0, 64, (16, T)); z[r, 6][:, i[:31]] = 8
    return pack(x, sb, pe, he, bx, z, lim)
def check_inputs(d):
    bad = []
    for k, lo, hi in (("xs", 0, 63), ("sb", 0, V - 1), ("pe", 0, B - 1), ("he", 0, B - 1), ("bx", 0, B - 1), ("zs", 0, 63), ("lim", 0, 1023)):
        v = np.asarray(d[k]).astype(np.float64)
        if not (np.min(v) >= lo and np.max(v) <= hi): bad.append("range of " + k)
        elif np.any(v != np.floor(v)): bad.append("whole numbers in " + k)
    w = np.sort(np.stack([gentries(a) for a in np.asarray(d["sb"])]).reshape(N, 8, B, 16), axis=-1)
    if np.any(w[..., 1:] == w[..., :-1]): bad.append("16 different entries of every box in sb")
    return bad
def reference(xs, sb, pe, he, bx, zs, lim):
    X = np.zeros((N, 8, 16, M), np.int64); X[..., :V] = xs.astype(np.float32).astype(np.int64).reshape(N, 8, 16, V)
    rows = np.stack([gentries(a) for a in sb]).astype(np.int64).reshape(N, 8, B, 16)
    P = np.zeros((N, 8, M), np.int64); Q = np.zeros((N, 8, M), np.int64); P[..., :V] = pe; Q[..., :V] = he
    J = np.zeros((N, 8, V), np.int64) + np.arange(V); till = np.full((N, 8, M), -1, np.int64)
    b = bx.astype(np.int64); z = zs.astype(np.float32).astype(np.int64).reshape(N, 8, 16, T); back = np.zeros((N, 8, T), np.int64)
    L = lim.astype(np.int64); A = np.zeros((N, 8), np.int64); BIG = 2 ** 20
    for t in range(S):
        for q in range(N):
            o = (q - t) % N
            for g in range(8):
                act = np.flatnonzero(back[o, g] <= t)
                if act.size == 0: continue
                x = X[q, g]; a = b[o, g, act]; zz = z[o, g][:, act]
                s = rows[q, g][a]; c = J[q, g][s]
                void = (c >= V) & (Q[q, g][s] == a[:, None]); held = till[q, g][c] >= t; free = ~void & ~held
                D = np.add.reduce(np.abs(x[:, c] - zz[:, :, None]), axis=0)
                key = np.where(free, D * 16 + np.arange(16), BIG); two = np.argsort(key, axis=1, kind="stable")[:, :2]
                kk = np.take_along_axis(key, two, 1); ef = np.take_along_axis(c, two, 1); e = ef[:, 0]; f = ef[:, 1]
                some = kk[:, 0] < BIG; pair = kk[:, 1] < BIG; xe = x[:, e]; xf = x[:, f]
                claim = np.flatnonzero(some); tk = claim[np.unique(e[claim], return_index=True)[1]]
                wait = some.copy(); wait[tk] = False
                ms = np.unique(a, return_index=True)[1]
                split = ~some | ((kk[:, 0] >> 4) > L[q, g, 1])
                apart = np.add.reduce(np.abs(xe - xf), axis=0)
                join = pair & ~split & (e < V) & (f < V) & (Q[q, g][e] == a) & (Q[q, g][f] == a) & (apart < L[q, g, 0] + 8 * (A[q, g] & 31))
                sp = ms[split[ms]]; jo = ms[join[ms]]; et = e[tk]; i = act[tk]
                b[o, g, i] = np.where(a[tk] == P[q, g][et], Q[q, g][et], P[q, g][et])
                stay = np.where(et >= V, LH, 1); till[q, g, et] = t + stay; back[o, g, i] = t + stay + 1
                back_s = s[sp][void[sp] & ~held[sp]]; J[q, g, back_s] = back_s
                n = V + T * t + act[jo]; J[q, g, e[jo]] = n; J[q, g, f[jo]] = n
                P[q, g, n] = P[q, g][e[jo]]; Q[q, g, n] = P[q, g][f[jo]]; A[q, g] += jo.size
                x[:, n] = np.maximum(xe, xf)[:, jo]; x[:, et] = zz[:, tk]
                z[o, g][:, i] = (zz[:, tk] + xe[:, tk]) >> 1
                z[o, g][:, act[wait]] = np.abs(zz - xe)[:, wait]
    return {"yj": J.astype(np.float32), "yx": X.reshape(N, 128, M).astype(np.float32).astype(BF), "yb": b.astype(np.float32), "yz": z.reshape(N, 128, T).astype(np.float32).astype(BF)}

@@ -1,0 +1,807 @@
+from concourse.mybir import AluOpType as ALU, AxisListType, ActivationFunctionType as ACT
+
+N, V, B, TR, S = 6, 3072, 384, 256, 6
+LG = TR * S
+WD = LG + V
+KOFF = 49152.0
+CAP = 65536.0
+HELD = 100000.0
+NONE = 8192.0
+VG = (1, 5)
+ABSH = (1,)
+CYC, GAT, SCA, FIX, PEC, PEF, LAT, LAT0, DMA, HOP = 1.04, 1.3, 3.15, 60.0, 0.52, 15.0, 80.0, 80.0, 2200.0, 3300.0
+ROUNDS, SEED = 8000, 1
+PLACED = {}
+DENSE = True
+BOXB = ("PB", "PE", None, None, "PB", None, None, None)
+
+F32, BF, F16, I32, U16 = "float32", "bfloat16", "float16", "int32", "uint16"
+SCRATCH = {}
+for _n, _c, _d in [
+    ("xsb", V, BF), ("sbt", B, I32), ("pq", 384, I32), ("pqd", 768, BF), ("pqr", V, BF),
+    ("bxi", TR, I32), ("limi", 16, I32), ("limb", 16, I32),
+    ("W", WD + TR, F32), ("XE", V, F32), ("G", 4096 + 16, F32), ("DP", 4096, BF), ("RL", 4096, BF),
+    ("R1", V, F16), ("KM", V, F16), ("IOS", V, I32), ("HEL", 192, U16), ("HAS", 192, F16), ("SLI", 192, F32),
+    ("JO", 192, F32), ("JU", 192, U16), ("JH", B + TR, F32), ("YO", WD + TR, BF), ("YJ", 192, F32), ("YT", 192, F32),
+    ("COL", TR, F32), ("D3", B, F32), ("D2", B, F32), ("CF", B, F32), ("CG", B, F32), ("GV", 128, F32),
+    ("EV", 512, F32), ("E32", 512, BF), ("PI", 8, I32), ("PF", 8, F32), ("PC", 96, F32), ("OH", 16, F32),
+    ("IB", 128, BF), ("NIB", 128, BF), ("N64", 128, BF), ("HIB", 128, BF), ("INJ", 128, BF), ("IH", 128, F16),
+    ("ONE", 128, BF), ("O8", 128, F16), ("ZH", 144, F16), ("ZQ", 144, F16), ("ZB", 144, BF), ("EX", 128, F16),
+    ("EZ", 128, F16), ("SEL", 128, BF), ("S1", 128, BF), ("S2", 128, BF), ("W8", 40, BF), ("WF", 80, BF), ("BG", 256, BF),
+    ("C17", TR, BF), ("I17", 128, BF), ("B17", 128, BF), ("C384", 128, BF), ("RST", TR, F32), ("KEEP", TR, F32),
+    ("B0", 512, BF), ("FBT", B, F32), ("C1", TR, F32), ("CB", 18, F32), ("CT", 18, F32), ("J16", 16, F16),
+    ("OFF", TR, U16), ("ZT", TR, BF), ("INA", TR, BF), ("JK", TR, F32), ("VK", TR, BF), ("FX", TR, BF),
+    ("LB0", TR, BF), ("LB1", TR, BF), ("PM", TR, I32), ("M2", TR, F32), ("PM2", TR, I32),
+    ("TP", (2, 128), F16), ("TQ", (2, 128), F16), ("T2", TR, F16), ("T3", TR, F16),
+    ("GE", TR, F32), ("GF", TR, F32), ("XA", TR, BF), ("XB", TR, BF), ("FE", TR, BF), ("FF", TR, BF),
+    ("LE0", TR, BF), ("LE1", TR, BF), ("JNK", 8 * B, BF), ("AA", TR, BF), ("BV", TR, BF), ("AB", TR, BF),
+    ("TZ", TR, F32), ("TH", TR, F32), ("SE", TR, BF), ("W1", TR, F32), ("W2", TR, F32), ("NL", TR, F32),
+    ("PV0", TR, F32), ("PV1", TR, F32), ("ZI", TR, I32),
+    ("SM", 16 * 40, F32), ("SI", 16 * 4, I32), ("SU", 16 * 6, U16),
+    ("zin", (S + 1, TR), BF), ("bin", (S, 16), U16), ("zout", (S, TR), BF), ("bout", (S, 16), U16),
+    ("bfi", 16, F32), ("bfo", 16, F32),
+]:
+    SCRATCH[_n] = ("sbuf", [128] + (list(_c) if isinstance(_c, tuple) else [_c]), _d)
+BANKS = ("P0", "P1", "P2", "PK", "PA", "PB", "PE", "PD")
+for _n in BANKS:
+    SCRATCH[_n] = ("psum", [128, 512], F32)
+
+SEMAPHORES = (["sv", "ss", "sp", "sg", "sent"] + ["d%d" % k for k in range(24)]
+              + ["az%d" % k for k in range(S)] + ["ab%d" % k for k in range(S)])
+WHOLE = {"TP": "TP0 TP1 TP2 TP3 TP4 TP5", "TQ": "TQ0 TQ1 TQ2 TQ3 TQ4", "Ws": " ".join("W%d" % m for m in range(12)),
+         "W": "Wl Wd " + " ".join("W%d" % m for m in range(12)), "G": "G0 G1 G2 G3 G4 G5 G6 G7 Gs",
+         "ce": " ".join("ce%d" % k for k in range(16)), "cb": " ".join("cb%d" % k for k in range(16)),
+         "pqr": "pqr0 pqr1 pqr2 pqr3", "XE": "XE0 XE1 XE2 XE3 XE4 XE5", "YO": "YO0 YO1 YO2 YOd"}
+
+
+def names(text):
+    return " ".join(WHOLE.get(x, x) for x in text.split()).split()
+
+
+def put_in_order(ops):
+    wrote, read, deps = {}, {}, []
+    for n, (ways, R, Wr) in enumerate(ops):
+        d = set()
+        for r in R:
+            if r in wrote:
+                d.add(wrote[r])
+            if r in BANKS:
+                d.update(read.get(r, ()))
+        for r in Wr:
+            if r in wrote:
+                d.add(wrote[r])
+            d.update(read.get(r, ()))
+        d.discard(n)
+        deps.append(d)
+        for r in R:
+            read.setdefault(r, []).append(n)
+        for r in Wr:
+            wrote[r] = n
+            read[r] = []
+    if "place" not in PLACED:
+        PLACED["place"] = shorten([[w[:3] for w in o[0]] for o in ops], [sorted(d) for d in deps], [kind_of(o) for o in ops])
+    place = PLACED["place"]
+    return [(n, ops[n][0][place[n][0]], deps[n]) for n in sorted(range(len(ops)), key=lambda k: (place[k][1], k))]
+
+
+def kind_of(o):
+    return "".join(x for x in (o[2] or ["out"])[0] + "<" + (o[1] or [""])[0] if not x.isdigit())
+
+
+def place_calls(ops, deps, order, fixed, back):
+    busy, place = {q: [] for q in "vspgy"}, [None] * len(ops)
+    for n in order:
+        best = None
+        for k in (range(len(ops[n])) if fixed[n] is None else (fixed[n],)):
+            w = ops[n][k]
+            t = 0.0
+            for d in deps[n]:
+                e = place[d][2]
+                if w[0] != "p" or ops[d][0][0] != "p":
+                    e += LAT
+                if e > t:
+                    t = e
+            if back:
+                t += w[2] - w[1]
+            lst = busy[w[0]]
+            lo, hi = 0, len(lst)
+            while lo < hi:
+                mid = (lo + hi) // 2
+                if lst[mid][1] <= t:
+                    lo = mid + 1
+                else:
+                    hi = mid
+            while lo < len(lst) and t + w[1] > lst[lo][0]:
+                t = max(t, lst[lo][1])
+                lo += 1
+            e = t + (w[1] if back else w[2])
+            if best is None or e < best[2]:
+                best = (k, t, e, lo)
+        place[n] = best
+        w = ops[n][best[0]]
+        busy[w[0]].insert(best[3], (best[1], best[1] + w[1]))
+    return place
+
+
+def shorten(ops, deps, kinds):
+    n_ = len(ops)
+    succ = [[] for _ in ops]
+    level = [0.0] * n_
+    for n in range(n_ - 1, -1, -1):
+        level[n] += min(w[2] for w in ops[n]) + LAT
+        for d in deps[n]:
+            succ[d].append(n)
+            level[d] = max(level[d], level[n])
+    seed = [SEED]
+
+    def draw(k):
+        seed[0] = (seed[0] * 1103515245 + 12345) % 2147483648
+        return (seed[0] >> 8) % k
+
+    free = [n for n in range(n_) if len(ops[n]) > 1]
+    cur = place_calls(ops, deps, sorted(range(n_), key=lambda k: (-level[k], k)), [None] * n_, False)
+    best, cs = cur, max(x[2] for x in cur)
+    bs = cs
+    for it in range(ROUNDS):
+        fixed = [x[0] for x in cur]
+        if draw(4):
+            ends = {(ops[n][x[0]][0], round(x[1] + ops[n][x[0]][1])): n for n, x in enumerate(cur)}
+            n = max(range(n_), key=lambda k: cur[k][2])
+            waits = []
+            while n is not None:
+                m = ends.get((ops[n][cur[n][0]][0], round(cur[n][1])))
+                if m is not None and m not in deps[n]:
+                    waits.append((n, m))
+                    n = m
+                else:
+                    n = max(deps[n], key=lambda k: cur[k][2]) if deps[n] else None
+            key = [x[1] for x in cur]
+            for _ in range(1 + draw(2)):
+                n, m = waits[draw(len(waits))]
+                way_ = draw(4)
+                if way_ == 0 and len(ops[m]) > 1:
+                    fixed[m] = 1 - fixed[m]
+                elif way_ == 1 and len(ops[n]) > 1:
+                    fixed[n] = 1 - fixed[n]
+                elif way_ == 2:
+                    key[m] = min([key[d] for d in succ[m]] + [key[n] + 1.0 + draw(1500)]) - 0.5
+                else:
+                    key[n] = max([key[d] for d in deps[n]] + [key[m] - 1.0 - draw(1500)]) + 0.5
+            new = place_calls(ops, deps, sorted(range(n_), key=lambda k: (key[k], k)), fixed, False)
+            s_ = max(x[2] for x in new)
+            if s_ < cs + 150.0 * (1.0 - it / ROUNDS):
+                cur, cs = new, s_
+                if s_ < bs:
+                    best, bs = new, s_
+            continue
+        if draw(4) == 0:
+            kind, k = kinds[free[draw(len(free))]], draw(2)
+            for n in free:
+                if kinds[n] == kind:
+                    fixed[n] = k
+        else:
+            for _ in range((0, 1, 3, 8)[draw(4)]):
+                fixed[free[draw(len(free))]] = draw(2)
+        b = place_calls(ops, succ, sorted(range(n_), key=lambda k: (-cur[k][2], -k)), fixed, True)
+        key = [-x[2] for x in b]
+        for _ in range((0, 5, 30)[draw(3)]):
+            n = draw(n_)
+            lo = max([key[d] for d in deps[n]] or [key[n] - 2000.0])
+            hi = min([key[d] for d in succ[n]] or [key[n] + 2000.0])
+            key[n] = lo + (hi - lo) * (1 + draw(999)) / 1001.0
+        new = place_calls(ops, deps, sorted(range(n_), key=lambda k: (key[k], k)), fixed, False)
+        s_ = max(x[2] for x in new)
+        if s_ < cs + 400.0 * (1.0 - it / ROUNDS):
+            cur, cs = new, s_
+            if s_ < bs:
+                best, bs = new, s_
+    return best
+
+
+def rank_program(g, core, T, topo):
+    rank = T.rank_of(core)
+    if rank is None:
+        return
+    Q = {"v": g.vector, "s": g.scalar, "p": g.tensor, "g": g, "y": g.sync}
+    own = {"v": "sv", "s": "ss", "p": "sp", "g": "sg"}
+    ops = []
+
+    def nel(ap):
+        n = 1
+        for x in list(ap.shape)[1:]:
+            n *= int(x)
+        return n
+
+    def two(*aps):
+        return all("16" in str(x.dtype) for x in aps)
+
+    def op(ways, R, Wr):
+        ops.append((ways, names(R), names(Wr)))
+
+    def way(q, c, fn):
+        return (q, c, c, fn, "c")
+
+    def plain(n, k=1.0):
+        return FIX + max(64.0, n * k) * CYC
+
+    def vtime(out, a, ind, k):
+        if ind == "g":
+            return 55 + nel(out) * GAT
+        if ind == "s":
+            return 50 + nel(a) * SCA
+        return plain(nel(a), k)
+
+    def dma(q, R, Wr, out, in_, nbytes=0):
+        op([(q, 100.0, DMA + nbytes / 200.0, lambda: Q[q].dma_start(out, in_), "d")], R, Wr)
+
+    def mms(R, Wr, groups, first=True, last=True):
+        def fn():
+            for items in groups:
+                for n, (o, l, r) in enumerate(items):
+                    ins = g.tensor.matmul(o, l, r, first and n == 0, last and n == len(items) - 1)
+            return ins
+        op([way("p", sum(PEF + max(min(64, nel(l)), nel(r)) * PEC for it in groups for o, l, r in it), fn)], R, Wr)
+
+    def mm(R, Wr, items, first=True, last=True):
+        mms(R, Wr, [items], first, last)
+
+    def ts_way(out, a, s1, o1, s2, o2, ind):
+        c = vtime(out, a, ind, 0.5 if ind is None and two(out, a) else 1.0)
+        if o2 is None:
+            return way("v", c, lambda: g.vector.tensor_scalar(out, a, s1, None, o1))
+        return way("v", c, lambda: g.vector.tensor_scalar(out, a, s1, s2, o1, o2))
+
+    def ts(R, Wr, out, a, s1, o1, s2=None, o2=None, ind=None):
+        op([ts_way(out, a, s1, o1, s2, o2, ind)], R, Wr)
+
+    def tt(R, Wr, out, a, b, o, ind=None):
+        k = 1.0 if any(x in BANKS for x in R.split()) else 2.0
+        op([way("v", vtime(out, a, ind, k), lambda: g.vector.tensor_tensor(out, a, b, o))], R, Wr)
+
+    def cp_way(out, a, ind):
+        return way("v", vtime(out, a, ind, 0.5 if ind is None and two(out, a) else 1.0), lambda: g.vector.tensor_copy(out, a))
+
+    def cp(R, Wr, out, a, ind=None):
+        op([cp_way(out, a, ind)], R, Wr)
+
+    def ms(Wr, out, c):
+        op([way("v", plain(nel(out), 0.5 if two(out) else 1.0), lambda: g.vector.memset(out, c))], "", Wr)
+
+    def act_way(out, a, f, ind, kw):
+        return way("s", vtime(out, a, ind, 1.0) + 20 * ("accum_out" in kw), lambda: g.scalar.activation(out, a, f, **kw))
+
+    def act(R, Wr, out, a, f, ind=None, **kw):
+        op([act_way(out, a, f, ind, kw)], R, Wr)
+
+    add, sub, mul, mx, mn = ALU.add, ALU.subtract, ALU.mult, ALU.max, ALU.min
+    eq, ge, gt, le, lt = ALU.is_equal, ALU.is_ge, ALU.is_gt, ALU.is_le, ALU.is_lt
+    band, shr = ALU.bitwise_and, ALU.arith_shift_right
+
+    def lin2(R, Wr, out, a, scale=None, bias=None, ind=None):
+        if scale is None and bias is None:
+            op([act_way(out, a, ACT.Copy, ind, {}), cp_way(out, a, ind)], R, Wr)
+            return
+        s_, b_ = 1.0 if scale is None else scale, 0.0 if bias is None else bias
+        op([act_way(out, a, ACT.Identity, ind, {"scale": s_, "bias": b_}), ts_way(out, a, s_, mul, b_, add, ind)], R, Wr)
+
+    def scan(R, Wr, out, d0, d1, o0, o1):
+        op([way("v", plain(nel(d0)), lambda: g.vector.tensor_tensor_scan(out, d0, d1, 0.0, o0, o1))], R, Wr)
+
+    def iota(Wr, out, pat, base, cm, flt=True):
+        kw = {"allow_small_or_imprecise_dtypes": True} if flt else {}
+        op([way("g", 130 + 2 * nel(out) * CYC, lambda: g.iota(out, pat, base, cm, **kw))], "", Wr)
+
+    slots = {}
+
+    def sm(name, a=0, b=16, st=1, pool="SM"):
+        d = slots.setdefault(pool, {})
+        k = d.setdefault(name, len(d))
+        return T[pool][:, 16 * k + a:16 * k + b:st]
+
+    def si(name):
+        return sm(name, pool="SI")
+
+    def su(name):
+        return sm(name, pool="SU")
+
+    nxt = T.cores[(rank + 1) % N]
+    rid, pid = topo.addr(nxt)[:2]
+    emask = topo.mask(core, nxt)
+    neng = len(topo.engines(core, nxt))
+
+    def send(R, Wr, out, in_, sem):
+        op([("g", 600.0, HOP + 4.0 * nel(out), lambda: g.remote_dma(out, in_, T.sem[sem], T.sem.sent, pid, rid, emask), sem)], R, Wr)
+
+    dma("y", "", "pq0", T.pq[:, 0:192], T.pe[:], 98304)
+    dma("s", "", "pq1", T.pq[:, 192:384], T.he[:], 98304)
+    dma("y", "", "xsb0", T.xsb[:, 0:1536], T.xs[:, 0:1536], 600000)
+    dma("s", "", "bxi", T.bxi[0:8, :], T.bx[:])
+    dma("y", "", "xsb1", T.xsb[:, 1536:V], T.xs[:, 1536:V], 800000)
+    dma("s", "", "sbt", T.sbt[:], T.sb[:], 196608)
+    dma("y", "", "zin0", T.zin[:, 0, :], T.zs[:], 65536)
+    dma("y", "", "limi", T.limi[0:1, :], T.lim[:])
+
+    iota("PI0", T.PI[:, 0:1], [[0, 1]], 0, 1, False)
+    iota("COL", T.COL[:], [[1, TR]], 0, 0)
+    iota("D3", T.D3[:], [[0, 24], [1, 16]], 0, 0)
+    iota("D2", T.D2[:], [[1, 24], [0, 16]], -12, 0)
+    iota("EV", T.EV[:], [[1, 32], [0, 16]], 0, 0)
+    iota("GV", T.GV[:], [[16, 8], [0, 16]], 0, 0)
+    op([way("g", 300.0, lambda: g.partition_broadcast(T.limb[:], T.limi[0:1, :], 128))], "limi", "limb")
+    iota("IOS", T.IOS[:], [[1, V]], 0, 0, False)
+    iota("ONE", T.ONE[:], [[0, 128]], 1, 0)
+    iota("JH", T.JH[:], [[0, B + TR]], int(NONE), 0)
+    iota("TZ", T.TZ[:], [[0, TR]], 0, 0)
+    iota("RST", T.RST[:], [[0, TR]], 0, 0)
+    iota("KEEP", T.KEEP[:], [[0, TR]], 1, 0)
+    iota("Wl", T.W[:, 0:LG], [[0, LG]], 0, 0)
+    iota("Wd", T.W[:, WD:WD + TR], [[0, TR]], 0, 0)
+    iota("YOd", T.YO[:, WD:WD + TR], [[0, TR]], 0, 0)
+    ms("TP", T.TP[:], 0.0)
+    ms("TQ", T.TQ[:], 0.0)
+    ms("RST", T.RST[:, 0:TR:16], CAP)
+    ms("KEEP", T.KEEP[:, 0:TR:16], 0.0)
+    ms("AI", si("AI"), 0)
+    for k, (sh, mk) in enumerate(((0, 15), (0, 112), (0, 31), (0, 7), (3, 3), (4, 1), (3, 1))):
+        ts("PI0", "PI%d" % (k + 1), T.PI[:, k + 1:k + 2], T.PI[:, 0:1], sh, shr, mk, band)
+    cp(" ".join("PI%d" % k for k in range(8)), "PF", T.PF[:], T.PI[:])
+    pc, rc, gc, p32, q7, q3, par, q8 = [T.PF[:, k:k + 1] for k in range(8)]
+    ts("COL PF", "OH", T.OH[:], T.COL[:, 0:16], rc, eq)
+    cp("pq0 pq1", "pqh", T.pqd[:, 0:384], T.pq[:])
+    tt("pq0 pq1 pqh", "pql", T.pqd[:, 384:768], T.pq[:], T.pqd[:, 0:384], sub)
+    for f, (c0, nm) in enumerate(((0, "pqh"), (384, "pql"), (192, "pqh"), (576, "pql"))):
+        dma("y", nm, "pqr%d" % f, T.pqr[8 * f:8 * f + 8, :], T.pqd[:, c0:c0 + 192], 49152)
+
+    pcn = [0]
+
+    def col():
+        pcn[0] += 1
+        return T.PC[:, pcn[0] - 1:pcn[0]], "pc%d" % pcn[0]
+
+    def lin(a, an, s, b, bn=""):
+        c, n = col()
+        lin2(an + " " + bn, n, c, a, s, b)
+        return c, n
+
+    def rows(spec, prev=None):
+        for r, w in spec:
+            prev = lin(T.OH[:, r:r + 1], "OH", float(w), 0.0 if prev is None else prev[0], "" if prev is None else prev[1])
+        return prev
+
+    z7, z7n = lin(q7, "PF", 16.0, 15.0)
+    ts("COL PF", "IB", T.IB[:], T.COL[:, 0:128], pc, eq)
+    ts("COL " + z7n, "ZQ", T.ZQ[:], T.COL[:, 0:144], z7, eq)
+    cp("bxi", "T2", T.T2[0:8, :], T.bxi[0:8, :])
+
+    def to_list(R, src, row, k, bank_, c0, extra=None, flat=False):
+        items = [] if extra is None else [extra]
+        for r in range(16):
+            rhs = src[row:row + k, 16 * r:16 * r + 16] if flat else src[row:row + k, r:TR:16]
+            items.append((T[bank_][:, c0:c0 + 16], T.ZQ[row:row + k, 15 - r:143 - r], rhs))
+        mm(R + " ZQ", bank_, items)
+
+    to_list("T2", T.T2, 0, 8, "PE", 0)
+    cp("PE", "bin0", T.bin[:, 0, :], T.PE[:, 0:16])
+    l1, l1n = rows([(2, 1.0 / 512)])
+    l2, l2n = rows([(5, 1.0 / 512)])
+    m1, m1n = rows([(1, 1.0 / 512)])
+    m2, m2n = rows([(4, 1.0 / 512)])
+    lin2("D3 %s %s" % (l1n, l2n), "CF", T.CF[:], T.D3[:], l2, l1)
+    lin2("D2 %s %s" % (m1n, m2n), "CG", T.CG[:], T.D2[:], m2, m1)
+    tt("CF D3", "CF", T.CF[:], T.CF[:], T.D3[:], mul)
+    tt("CG D2", "CG", T.CG[:], T.CG[:], T.D2[:], mul)
+    tt("CF CG", "B0", T.B0[:, 0:256], T.CF[:, 64:320], T.CG[:, 64:320], add)
+    lin2("B0", "B0b", T.B0[:, 256:512], T.B0[:, 0:256])
+    k0, k0n = rows([(13, 0.25)])
+    lin2("CF B0 " + k0n, "CF", T.CF[:], T.CF[:], None, k0)
+    tt("CF CG", "FBT", T.FBT[:], T.CF[:], T.CG[:], add)
+    s7, s7n = lin(q3, "PF", 1.0, z7, z7n)
+    ts("COL " + s7n, "SEL", T.SEL[:], T.COL[:, 8:136], s7, eq, 1.0 / 1024, mul)
+    a0, a0n = rows([(0, 1.0 / 512), (3, -8.0 / 512)])
+    b0, b0n = rows([(3, 1.0 / 512)])
+    l0, l0n = rows([(12, 0.125)], (k0, k0n))
+    n0, n0n = rows([(12, -0.125)], lin(k0, k0n, 1.0, 128.0))
+    lin2("COL %s %s" % (a0n, b0n), "CT", T.CT[:], T.COL[:, 0:18], b0, a0)
+    lin2("COL", "CB", T.CB[:], T.COL[:, 0:18], None, -8.0)
+    tt("CT CB", "CT", T.CT[:], T.CB[:], T.CT[:], mul)
+    lin2("CT CB " + l0n, "CBa", T.CB[:, 0:6], T.CT[:, 0:6], None, l0)
+    lin2("CT " + n0n, "CB", T.CB[:, 6:18], T.CT[:, 6:18], None, n0)
+    ts("EV PF", "E32", T.E32[:], T.EV[:], p32, eq)
+
+    for m, bk in enumerate(("P0", "P1", "P2", "PB", "PD", "PA")):
+        sl = slice(512 * m, 512 * m + 512)
+        mm("IB xsb%d B0 B0b" % (m // 3), bk, [(T[bk][:], T.IB[:], T.xsb[:, sl]), (T[bk][:], T.IB[:], T.B0[:])], last=False)
+        mm("SEL pqr", bk, [(T[bk][:], T.SEL[0:32, :], T.pqr[0:32, sl])], first=False)
+        for u in range(2):
+            c0 = LG + 512 * m + 256 * u
+            lin2(bk + " CB", "W%d" % (2 * m + u), T.W[:, c0:c0 + 256], T[bk][:, 256 * u:256 * u + 256], None,
+                 T.CB[:, 6 + 2 * m + u:7 + 2 * m + u])
+
+    npar, nparn = lin(par, "PF", -1.0, 1.0)
+    sq = rows([(3, 2.0 ** 30), (4, 2.0 ** 30), (5, 2.0 ** 30)])
+    bc, bcn = rows([(6, 2.0 ** 23)], sq)
+    j0, j0n = rows([(6, 1.0 / 1024)])
+    sc, scn = col()
+    ts("PF", scn, sc, rc, 3.0, lt, -2.0 ** 40, mul)
+    LS = []
+    for u, (pp, ppn) in enumerate(((npar, nparn), (par, "PF"))):
+        a, an = lin(sc, scn, pp, 0.0, ppn)
+        b, bn = lin(bc, bcn, pp, 0.0, ppn)
+        LS.append((a, b, an + " " + bn))
+        ts("ONE " + ppn, "BG%d" % u, T.BG[:, 128 * u:128 * u + 128], T.ONE[:], pp, mul, 2.0 ** 22, mul)
+    lin2("COL " + j0n, "C1", T.C1[:], T.COL[:], j0)
+    lin2("IB", "I17", T.I17[:], T.IB[:], 20480.0)
+    lin2("IB PF", "C17", T.C17[:, 0:128], T.IB[:], rc)
+    lin2("IB PF", "C17b", T.C17[:, 128:256], T.IB[:], rc)
+    lin2("ONE", "C384", T.C384[:], T.ONE[:], KOFF / 128)
+    ts("GV PF", "B17", T.B17[:], T.GV[:], gc, eq, 8192.0, mul)
+    ts("GV PF", "BLK", T.W8[:, 0:8], T.GV[:, 0:128:16], gc, eq)
+    BLK, W8P, W8N, W8I, W8A = [T.W8[:, 8 * k:8 * k + 8] for k in range(5)]
+    for nm, ap, w in (("W8P", W8P, 32.0), ("W8N", W8N, -16.0), ("W8I", W8I, 2.0 ** 23), ("W8A", W8A, 16.0)):
+        lin2("BLK", nm, ap, BLK, w)
+
+    def wf(f):
+        return T.WF[:, 8 * f:8 * f + 8]
+
+    def weights(f, spec, prev=None):
+        c, n = rows(spec, prev)
+        lin2("BLK " + n, "WF%d" % f, wf(f), BLK, c)
+
+    low = rows([(1, 8192.0), (2, 512.0)])
+    weights(0, [(6, 2.0 ** 23), (11, 2.0 ** 33)], lin(sq[0], sq[1], -1.0, 0.0))
+    weights(2, [(13, 768.0)], low)
+    weights(1, [(0, 131072.0), (13, 8704.0)], low)
+    weights(3, [(7, -1024.0), (8, -1024.0)])
+    weights(4, [(9, -1024.0), (10, -1024.0)])
+    weights(5, [(12, 512.0)])
+    weights(6, [(9, 2.0 ** -13), (10, 2.0 ** -13), (12, 2.0 ** -11), (13, 2.0 ** -12)])
+    lin2("WF6", "WF7", wf(7), wf(6), 2048.0)
+    lin2("WF2", "WF8", wf(8), wf(2), -2.0 ** -23)
+    lin2("WF2", "WF9", wf(9), wf(2), -2.0 ** -12)
+    spc, spcn = rows([(3, 0.25), (11, 0.25), (9, -1.0 / 1024)])
+    lin2("ONE " + spcn, "Gs", T.G[:, 4096:4112], T.ONE[:, 0:16], spc, 128.0)
+    lin2("IB", "IH", T.IH[:], T.IB[:])
+    lin2("IB", "NIB", T.NIB[:], T.IB[:], -1.0)
+    lin2("IB", "N64", T.N64[:], T.IB[:], -64.0)
+    lin2("IB", "HIB", T.HIB[:], T.IB[:], 0.5)
+    lin2("ONE", "O8", T.O8[:], T.ONE[:], 8.0)
+    lin2("GV PF", "DL", sm("DL", 0, 8), T.GV[:, 0:128:16], None, rc)
+    lin2("DL", "DLb", sm("DL", 8, 16), sm("DL", 0, 8), None, 128.0)
+    lin2("DL DLb", "J16", T.J16[:], sm("DL"), 16.0)
+    lin2("DL DLb", "DM", sm("DM"), sm("DL"), None, float(WD))
+    for h in range(2):
+        lin2("ONE PF", "DW%d" % h, sm("DW", 8 * h, 8 * h + 8), T.ONE[:, 0:8], pc, float(WD + 128 * h))
+        cp("limb", "L0%d" % h, sm("L0", 8 * h, 8 * h + 8), T.limb[:, 0:16:2])
+        ts("limb", "SL%d" % h, sm("SL", 8 * h, 8 * h + 8), T.limb[:, 1:16:2], 16.0, mul, KOFF + 16.0, add)
+    lin2("DW0 DW1", "DB", sm("DB"), sm("DW"), None, float(B - WD))
+    pv_, pvn_ = lin(pc, "PF", 1.0, -NONE)
+    lin2("COL " + pvn_, "VC", sm("VC"), T.COL[:, 0:16], 128.0, pv_)
+    lin2("VC", "VL", sm("VL"), sm("VC"), None, NONE + 1.0)
+    q16, q16n = lin(q7, "PF", 16.0, 0.0)
+    ez, ezn = lin(q8, "PF", 513.0, -512.0)
+    ts("GV " + q16n, "EX", T.EX[:], T.GV[:], q16, eq)
+    lin2("EX " + ezn, "EZ", T.EZ[:], T.EX[:], ez)
+    nj, njn = lin(T.OH[:, 6:7], "OH", -1.0, 1.0)
+    lin2("IB " + njn, "INJ", T.INJ[:], T.IB[:], nj)
+    m78, m78n = rows([(7, 1.0), (8, 1.0)])
+    lin2("IB " + m78n, "S1", T.S1[:], T.IB[:], m78)
+    p2, p2n = lin(pc, "PF", 1.0, 2.0)
+    g15, g15n = lin(gc, "PF", 1.0, 15.0)
+    lin2("ZQ PF", "ZB", T.ZB[:], T.ZQ[:], par)
+    r0, r0n = lin(rc, "PF", 1.0, float(LG))
+    lin2("COL " + r0n, "SLI", T.SLI[:], T.COL[:, 0:192], 16.0, r0)
+    r192, r192n = lin(rc, "PF", 192.0, 0.0)
+    lin2("COL " + r192n, "YJ", T.YJ[:], T.COL[:, 0:192], None, r192)
+    ts("COL %s %s" % (p2n, m78n), "S2", T.S2[:], T.COL[:, 0:128], p2, eq, m78, mul)
+    ts("COL " + g15n, "ZH", T.ZH[:], T.COL[:, 0:144], g15, eq)
+
+    def homes(part):
+        if part == 0:
+            mm("ZB pqr", "PE", [(T.PE[:, 0:192], T.ZB[0:32, 15 - r:143 - r], T.pqr[0:32, r:V:16]) for r in range(16)])
+            cp("PE", "HEL", T.HEL[:], T.PE[:, 0:192])
+            for u in range(6):
+                sl = slice(512 * u, 512 * u + 512)
+                tt("sbt HEL IOS", "KM%d" % u, T.KM[:, sl], T.sbt[:].indirect(T.HEL[:, 32 * u:32 * u + 32]), T.IOS[:, sl], eq, "g")
+        else:
+            mm("ZH KM0 KM1 KM2 KM3 KM4 KM5", "P2", [(T.P2[:, 0:192], T.ZH[:, 15 - r:143 - r], T.KM[:, r:V:16]) for r in range(16)])
+            lin2("P2", "HAS", T.HAS[:], T.P2[:, 0:192], -NONE, NONE)
+
+    homes(0)
+
+    def fld(n, bk="PA"):
+        return T[bk][:, 256 + 16 * n:272 + 16 * n]
+
+    def fields(R, spec, bk="PA"):
+        groups = []
+        for n, parts in spec:
+            for h in range(2):
+                o = T[bk][:, 256 + 16 * n + 8 * h:264 + 16 * n + 8 * h]
+                groups.append([(o, src[:, 128 * h:128 * h + 128], w) for src, w in parts])
+        mms(R, bk, groups)
+
+    rot = [0]
+
+    def bank():
+        rot[0] += 1
+        return "P%d" % (rot[0] % 3)
+
+    def pairs(gq, L, ln, rhs, rn_, ina, bn, cn, onv, bk=None):
+        bk = bk or bank()
+        a, u = 32 * (gq // 2), gq % 2
+        groups = []
+        for h, (c0, n) in enumerate(((0, 128), (128, 256))):
+            it = [(T[bk][:, c0:c0 + n], L[u][a:a + 32, 128 * h:128 * h + 128], rhs[a:a + 32, 0:n])]
+            if ina:
+                it.append((T[bk][:, c0:c0 + n], T.BG[a:a + 32, 128 * u:128 * u + 128], T.INA[a:a + 32, 0:n]))
+            groups.append(it)
+        mms("%s%d %s" % (ln, u, rn_) + (" INA BG0 BG1" if ina else ""), bk, groups)
+        for h, (c0, n) in enumerate(((0, 128), (128, 256))):
+            k = 8 * h + gq
+            o, src = sm(cn, k, k + 1), T[bk][:, c0:c0 + n]
+            if onv:
+                op([way("v", plain(n), lambda o=o, src=src: g.vector.tensor_reduce(o, src, AxisListType.X, mn))], bk, "%s%d" % (cn, k))
+            else:
+                act(bk + " " + bn, "%s%d JNK%d" % (cn, k, k), T.JNK[:, B * gq + c0:B * gq + c0 + n], src, ACT.Relu,
+                    bias=sm(bn, k, k + 1), scale=-1.0, accum_out=o)
+        if onv:
+            both = "%s%d %s%d" % (cn, gq, cn, gq + 8)
+            tt(bn + " " + both, both, sm(cn, gq, 16, 8), sm(bn, gq, 16, 8), sm(cn, gq, 16, 8), sub)
+
+    def turn(src, sn, dst, dn, bk="PD"):
+        mms(sn + " IH", bk, [[(T[bk][:, 128 * h:128 * h + 128], src[:, h, :], T.IH[:])] for h in range(2)])
+        lin2(bk, dn, dst[:], T[bk][:, 0:TR])
+
+    def slot(buf, k, lo=0):
+        return buf[:, :, 32 * k + lo:32 * k + lo + 8]
+
+    LB, LE = (T.LB0, T.LB1), (T.LE0, T.LE1)
+    best, best2 = T.PM[:, 15:TR:16], T.PM2[:, 15:TR:16]
+    j16 = (T.PE[:, 0:16], T.IH[:], T.J16[:])
+
+    for t in range(S):
+        last = t == S - 1
+        Z, zn = T.zin[:, t, :], "zin%d" % t
+        BI, bn_ = T.bin[:, t, :], "bin%d" % t
+        win, wn = (T.W[:, LG:WD], "Ws") if t == 0 else (T.XE[:], "XE")
+        cp("sbt " + bn_, "OFF", T.OFF[:], T.sbt[:].indirect(BI), "g")
+        mms(zn + " IB", "PD", [[(T.PD[:, 128 * h:128 * h + 128], T.zin[:, t, 128 * h:128 * h + 128], T.IB[:])] for h in range(2)])
+        lin2("PD", "ZT", T.ZT[:], T.PD[:, 0:TR], None, -64.0)
+        tt("FBT C1 " + bn_, "FX", T.FX[:], T.FBT[:].indirect(BI), T.C1[:], add, "g")
+        ts("JH " + bn_, "VK", T.VK[:], T.JH[:, 0:B].indirect(BI), 4096.0, lt, ind="g")
+        ts(zn, "INA", T.INA[:], Z, 64.0, ge)
+        if last:
+            lin2("JH", "CF", T.CF[:], T.JH[:, 0:B], None, 1.0)
+            ts("JH", "CG", T.CG[:], T.JH[:, 0:B], 4096.0, lt)
+            tt("CF CG", "JH", T.JH[:, 0:B], T.CF[:], T.CG[:], mul)
+        lin2("JH " + bn_, "JK", T.JK[:], T.JH[:, 0:B].indirect(BI), ind="g")
+        for u in range(2):
+            lin2("FX " + LS[u][2], "LB%d" % u, LB[u][:], T.FX[:], LS[u][0], LS[u][1])
+        items = [(T.PK[:, 0:TR], T.ONE[:], T.C17[:])]
+        for h in range(2):
+            o = T.PK[:, 128 * h:128 * h + 128]
+            items += [(o, T.VK[:, 128 * h:128 * h + 128], T.I17[:]), (o, T.INA[:, 128 * h:128 * h + 128], T.B17[:])]
+            if h in ABSH:
+                items.append((o, T.ONE[:], T.C384[:]))
+        mm("ONE C17 C17b C384 VK INA I17 B17", "PK", items, last=False)
+        fields("FX INA W8I WF0 WF2", [(0, [(T.FX, wf(0)), (T.INA, W8I)]), (1, [(T.FX, wf(2))])])
+        lin2("PA", "BB", sm("BB"), fld(0))
+        lin2("PA", "a", sm("a"), fld(1))
+
+        def dpass(h, src, sn, wt, fin):
+            mm(sn + " W8P W8N W8A", "PK", [(T.PK[:, 128 * h + k:128 * h + 128:16], src[:, 2048 * h + k:2048 * h + 2048:16], wt)
+                                           for k in range(16)], first=False, last=fin)
+
+        for c in range(8):
+            sl = slice(512 * c, 512 * c + 512)
+            h, a, bk = c // 4, 32 * (c % 4), bank()
+            lin2("OFF " + wn, "G%d" % c, T.G[:, sl], win.indirect(T.OFF[:, 32 * c:32 * c + 32]), ind="g")
+            mm("ZT E32", bk, [(T[bk][:], T.ZT[a:a + 32, 128 * h:128 * h + 128], T.E32[a:a + 32, :])])
+            tt("G%d %s" % (c, bk), "DP%d" % c, T.DP[:, sl], T.G[:, sl], T[bk][:], sub)
+            if h in ABSH:
+                act("DP%d" % c, "RL%d" % c, T.RL[:, sl], T.DP[:, sl], ACT.Abs, bias=-192.0)
+            else:
+                ts("DP%d" % c, "RL%d" % c, T.RL[:, sl], T.DP[:, sl], 192.0, mx)
+            if c % 4 == 3:
+                if h not in ABSH:
+                    dpass(h, T.DP, " ".join("DP%d" % x for x in range(c - 3, c + 1)), W8N, False)
+                dpass(h, T.RL, " ".join("RL%d" % x for x in range(c - 3, c + 1)), W8A if h in ABSH else W8P, h == 1)
+        for gq in range(8):
+            pairs(gq, LB, "LB", T.FX, "FX", True, "BB", "cb", False, BOXB[gq])
+        scan("RST PK", "PM", T.PM[:], T.RST[:], T.PK[:, 0:TR], mx, mn)
+        ts("PM", "K1", si("K1"), best, 65551, band)
+        ts("K1", "TP0", slot(T.TP, 0), si("K1"), 4096.0, mn)
+        turn(T.TP, "TP", T.T2, "T2")
+        to_list("T2 IH J16", T.T2, 0, 8, "PE", 0, j16)
+        ts("PE", "OE", su("OE"), T.PE[:, 0:16], 4096.0, mn)
+        tt("G OE C1", "GE", T.GE[:], T.G[:].indirect(su("OE")), T.C1[:], add, "g")
+        lin2("GE", "XA", T.XA[:], T.GE[:])
+        tt("GE XA", "FE", T.FE[:], T.GE[:], T.XA[:], sub)
+        tt("PK PM", "M2", T.M2[:, 1:TR], T.PK[:, 1:TR], T.PM[:, 0:TR - 1], mx)
+        ms("M2", T.M2[:, 0:TR:16], CAP)
+        scan("RST M2", "PM2", T.PM2[:], T.RST[:], T.M2[:], mx, mn)
+        ts("PM2", "K2", si("K2"), best2, 65551, band)
+        ts("K2", "TQ0", slot(T.TQ, 0), si("K2"), 4096.0, mn)
+        turn(T.TQ, "TQ", T.T3, "T3")
+        to_list("T3 IH J16", T.T3, 0, 8, "PE", 0, j16)
+        ts("PE", "OF", su("OF"), T.PE[:, 0:16], 4096.0, mn)
+        lin2("G OF", "GF", T.GF[:], T.G[:].indirect(su("OF")), ind="g")
+        lin2("GF", "XB", T.XB[:], T.GF[:])
+        tt("GF XB", "FF", T.FF[:], T.GF[:], T.XB[:], sub)
+        mm("IB NIB XA XB", "PE", [(T.PE[:, TR:], T.IB[:], T.XA[:]), (T.PE[:, TR:], T.NIB[:], T.XB[:])])
+        act("PE", "AB", T.AB[:], T.PE[:, TR:], ACT.Abs)
+        for u in range(2):
+            lin2("FE " + LS[u][2], "LE%d" % u, LE[u][:], T.FE[:], LS[u][0], LS[u][1])
+        fields("FE WF0", [(2, [(T.FE, wf(0))])])
+        lin2("PA", "BE", sm("BE"), fld(2))
+        fields("FE FX WF1 WF2 WF3 WF4 WF5", [(4, [(T.FE, wf(3)), (T.FX, wf(2))]), (5, [(T.FE, wf(4)), (T.FX, wf(2))]),
+                                             (6, [(T.FE, wf(5))]), (3, [(T.FE, wf(1))])])
+        for gq in range(8):
+            pairs(gq, LE, "LE", T.FE, "FE", False, "BE", "ce", gq in VG, "P%d" % (gq % 2))
+        mms("IB NIB N64 XA INA " + zn, "PB",
+            [[(T.PB[:, 0:TR], T.IB[:], Z), (T.PB[:, 0:TR], T.NIB[:], T.XA[:]), (T.PB[:, 0:TR], T.N64[:], T.INA[:])],
+             [(T.PB[:, TR:], T.IB[:], Z), (T.PB[:, TR:], T.IB[:], T.XA[:])]])
+        act("PB", "AA", T.AA[:], T.PB[:, 0:TR], ACT.Abs, bias=128.0)
+        lin2("PB", "BV", T.BV[:], T.PB[:, TR:], 0.5, 63.75)
+        ts("PA", "e1", sm("e1"), fld(4), 0.0, eq)
+        lin2("PA", "TP1", slot(T.TP, 0, 8), fld(6))
+        lin2("PA", "c", sm("c"), fld(3))
+        tt("PA e1", "e1", sm("e1"), sm("e1"), fld(5), mul)
+        tt("PA e1", "e1", sm("e1"), sm("e1"), fld(4), add)
+        tt("a e1", "TP2", slot(T.TP, 2), sm("a"), sm("e1"), sub)
+        ts("ce", "TP0", slot(T.TP, 0), sm("ce"), 0.0, gt)
+        tt("TP0 e1", "TP3", slot(T.TP, 2, 8), slot(T.TP, 0), sm("e1"), mul)
+        tt("ce DW0 DW1", "cd", sm("cd"), sm("ce"), sm("DW"), mn)
+        tt("c cd", "cd", sm("cd"), sm("cd"), sm("c"), mx)
+        lin2("cd", "TP4", slot(T.TP, 1), sm("cd"))
+        tt("cd TP4", "TP5", slot(T.TP, 1, 8), sm("cd"), slot(T.TP, 1), sub)
+        turn(T.TP, "TP", T.T2, "T2")
+        to_list("T2", T.T2, 32, 16, "PD", 256)
+        cp("PD", "CU", su("CU"), T.PD[:, 256:272])
+        mm("T2 EZ IB BV", "PB", [(T.PB[:, 0:TR], T.IB[:], T.BV[:]), (T.PB[:, 0:TR], T.EZ[0:16, :], T.T2[0:16, :])])
+        to_list("T2", T.T2, 64, 16, "PE", 0, None, last)
+        zo, zon = T.zout[:, t, :], "zout%d" % t
+        tt("PB AA", zon, zo, T.PB[:, 0:TR], T.AA[:], mx)
+        if last:
+            cp(zon, "ZI", T.ZI[:], zo)
+            ts("ZI", "ZI", T.ZI[:], T.ZI[:], 63, band)
+            cp("ZI", zon, zo, T.ZI[:])
+            lin2("PE", "bfo", T.bfo[:], T.PE[:, 0:16])
+            send("bfo", "bfi", T.bfi[:], T.bfo[:], "ab%d" % t)
+        else:
+            cp("PE", "bout%d" % t, T.bout[:, t, :], T.PE[:, 0:16])
+            send("bout%d" % t, "bin%d" % (t + 1), T.bin[:, t + 1, :], T.bout[:, t, :], "ab%d" % t)
+        send(zon, "zin%d" % (t + 1), T.zin[:, t + 1, :], zo, "az%d" % t)
+
+        fields("FE FF FX AB BLK WF6 WF7 WF8 WF9",
+               [(7, [(T.FE, wf(6)), (T.FF, wf(7)), (T.FX, wf(8)), (T.FX, wf(9))]), (8, [(T.AB, BLK)])], "PK")
+        tt("PM SL0 SL1", "sp", sm("sp"), best, sm("SL"), ge)
+        lin2("sp", "sp", sm("sp"), sm("sp"), HELD)
+        tt("cb DB", "ad", sm("ad"), sm("cb"), sm("DB"), mn)
+        tt("a ad", "TQ1", slot(T.TQ, 1), sm("a"), sm("ad"), mx)
+        tt("cb sp", "m", sm("m"), sm("cb"), sm("sp"), mx)
+        jl, jln = (sm("L0"), "L00 L01") if t == 0 else (sm("JL"), "JL")
+        tt("PK " + jln, "j3", sm("j3"), fld(8, "PK"), jl, ge)
+        tt("j3 m", "m", sm("m"), sm("m"), sm("j3"), mx)
+        tt("PK m", "j", sm("j"), sm("m"), fld(7, "PK"), eq)
+        tt("j PM2", "j3", sm("j3"), sm("j"), best2, mul)
+        tt("j3 sp", "TZ", T.TZ[:, 0:TR:16], sm("j3"), sm("sp"), mx)
+        for h in range(2):
+            k = 2 * t + h
+            lin2("j VC VL", "TQ%d" % (2 + h), T.TQ[:, h, 64:72], sm("j", 8 * h, 8 * h + 8),
+                 sm("VL" if last else "VC", k, k + 1), 0.0 if last else NONE)
+        lin2("j", "TQ4", slot(T.TQ, 3), sm("j"))
+        scan("KEEP TZ", "TH", T.TH[:], T.KEEP[:], T.TZ[:], mul, add)
+        tt("PK TH", "SE", T.SE[:], T.PK[:, 0:TR], T.TH[:], le)
+        if t == 0:
+            homes(1)
+        turn(T.TQ, "TQ", T.T3, "T3", "P2")
+        mms("T3 EX SE IB", "P2", [[(T.P2[:, 0:TR], T.EX[64:72, :], T.T3[64:72, :])]]
+            + [[(T.P2[:, TR + 128 * h:TR + 128 * h + 128], T.SE[:, 128 * h:128 * h + 128], T.IB[:])] for h in range(2)])
+        to_list("T3", T.T3, 32, 8, "PK", 0)
+        tt("P2 JK", "W1", T.W1[:], T.P2[:, 0:TR], T.JK[:], sub)
+        tt("P2 W1", "W2", T.W2[:], T.P2[:, TR:], T.W1[:], mul)
+        cp("PK", "OB", su("OB"), T.PK[:, 0:16])
+        tt("W2 JK OB JH", "JH", T.JH[:].indirect(su("OB")), T.W2[:], T.JK[:], add, "s")
+        pv, pvn = (T.PV1, "PV1") if t == 1 else (T.PV0, "PV0")
+        half = [(T.P1[:, TR:], T.HIB[:], x[:]) for x in (T.XA, T.XB, T.AB)]
+        if last:
+            mm("HIB XA XB AB", "P1", half)
+            lin2("P1", "NL", T.NL[:], T.P1[:, TR:], None, -128.0)
+        else:
+            mms("IB INJ HIB XA XB AB B0 S1 S2 FE FF " + zn, "P1",
+                [[(T.P1[:, 0:TR], T.IB[:], Z), (T.P1[:, 0:TR], T.INJ[:], T.FE[:])],
+                 half + [(T.P1[:, TR:], T.IB[:], T.B0[:, 0:TR]), (T.P1[:, TR:], T.S1[:], T.FE[:]), (T.P1[:, TR:], T.S2[:], T.FF[:])]])
+            lin2("P1", pvn, pv[:], T.P1[:, 0:TR])
+            lin2("P1 CBa", "NL", T.NL[:], T.P1[:, TR:], None, T.CB[:, t:t + 1])
+        mm("T3 EX", "P0", [(T.P0[:, 0:TR], T.EX[96:104, :], T.T3[96:104, :])])
+
+        def pass1(u, n):
+            sl = slice(n * u, n * u + n)
+            tt("JH HEL KM0 KM1 KM2 KM3 KM4 KM5", "R1%d" % u, T.R1[:, sl],
+               T.JH[:, 0:B].indirect(T.HEL[:, n // 16 * u:n // 16 * (u + 1)]), T.KM[:, sl], mul, "g")
+
+        if last:
+            for u in range(3):
+                for x in range(3):
+                    sl = slice(1536 * u + 512 * x, 1536 * u + 512 * x + 512)
+                    nm = "Y%d%d" % (u, x)
+                    act("W", nm, T.YO[:, sl], T.W[:, sl], ACT.Abs)
+                    op([ts_way(T.YO[:, sl], T.YO[:, sl], -128.0, add, 0.0, mx, None),
+                        act_way(T.YO[:, sl], T.YO[:, sl], ACT.Relu, None, {"bias": -128.0})], nm, nm)
+            ally = " ".join("Y%d%d" % (u, x) for u in range(3) for x in range(3))
+            tt("P0 NL Y02", "Y02", T.YO[:, TR * t:TR * t + TR], T.P0[:, 0:TR], T.NL[:], mul)
+            cp("YOd CU %s %s" % (ally, zn), ally, T.YO[:].indirect(su("CU")), Z, "s")
+            dma("y", ally, "", T.yx[:, 0:V], T.YO[:, LG:WD], 800000)
+            dma("y", ally, "", T.yx[:, V:WD], T.YO[:, 0:LG], 1200000)
+            for u in range(4):
+                pass1(u, 768)
+                mm("ZH R1%d" % u, "PB", [(T.PB[:, 0:192], T.ZH[:, 15 - r:143 - r], T.R1[:, 192 * r:192 * r + 192])
+                                         for r in range(4 * u, 4 * u + 4)], first=u == 0, last=u == 3)
+            ts("PB", "YT", T.YT[:], T.PB[:, 0:192], 4096.0, mul, float(V - 1), mn)
+            tt("PB YT", "YT", T.YT[:], T.PB[:, 0:192], T.YT[:], add)
+            tt("YT YJ", "YJ", T.YJ[:], T.YJ[:], T.YT[:], mx)
+            dma("y", "YJ", "", T.yj[:], T.YJ[:], 98304)
+            break
+
+        if t and DENSE:
+            for u in range(12):
+                sl = slice(LG + 256 * u, LG + 256 * u + 256)
+                act("W%d" % u, "W%d" % u, T.W[:, sl], T.W[:, sl], ACT.Abs)
+        tt("P0 NL", "Wl", T.W[:, TR * t:TR * t + TR], T.P0[:, 0:TR], T.NL[:], mul)
+        if t == 4:
+            ts("PV1 UL W", "W", T.W[:].indirect(su("UL")), T.PV1[:], 1.0, mul, 128.0, add, "s")
+        ts(pvn + " CU W", "W", T.W[:].indirect(su("CU")), pv[:], -1.0, mul, -128.0, add, "s")
+        for nm, cmp_, when in (("US", lt, () if DENSE else (1, 2, 3)), ("UL", ge, (1,))):
+            if t in when:
+                ts("PD", "UT", sm("UT"), T.PD[:, 256:272], float(LG), cmp_)
+                tt("UT DM", "UT", sm("UT"), sm("UT"), sm("DM"), mul)
+                tt("UT PD", "UT", sm("UT"), sm("UT"), T.PD[:, 256:272], mx)
+                cp("UT", nm, su(nm), sm("UT"))
+        for u, bk in enumerate(("P2", "PK", "P2")):
+            pass1(u, 1024)
+            sl = slice(64 * u, 64 * u + 64)
+            o = T[bk][:, 0:64]
+            mm("ZH IH HAS R1%d" % u, bk, [(o, T.IH[:], T.HAS[:, sl])]
+               + [(o, T.ZH[:, 15 - r:143 - r], T.R1[:, 1024 * u + r:1024 * u + 1024:16]) for r in range(16)])
+            tt(bk + " SLI", "JO%d" % u, T.JO[:, sl], o, T.SLI[:, sl], mn)
+            cp("JO%d" % u, "JU%d" % u, T.JU[:, sl], T.JO[:, sl])
+            for x in range(2 * u, 2 * u + 2):
+                lin2("W JU%d" % u, "XE%d" % x, T.XE[:, 512 * x:512 * x + 512],
+                     T.W[:, 0:WD].indirect(T.JU[:, 32 * x:32 * x + 32]), ind="g")
+        if t < 4 and not DENSE:
+            us = "US" if t else "CU"
+            ts("%s %s W" % (pvn, us), "W", T.W[:].indirect(su(us)), pv[:], 1.0, mul, 128.0, add, "s")
+        mms("O8 TQ4", "PA", [[(T.PA[:, 400 + 8 * u:408 + 8 * u], T.O8[:], T.TQ[:, h, 96:104]) for h in range(2)] for u in range(2)])
+        tt("PA AI", "AI", si("AI"), fld(9), si("AI"), add)
+        ts("AI", "AM", si("AM"), si("AI"), 248, band)
+        tt("AM L00 L01", "JL", sm("JL"), si("AM"), sm("L0"), add)
+
+    dma("y", "bfi", "", T.yb[:], T.bfi[:])
+    dma("y", "zin6", "", T.yz[:], T.zin[:, S, :], 65536)
+
+    count, seen, token, nd = {}, {}, {}, 0
+    for n, (q, c0, c1, fn, kind), deps in put_in_order(ops):
+        want = {}
+        for d in deps:
+            sem, val = token[d]
+            if not (q == "p" and sem == "sp"):
+                want[sem] = max(want.get(sem, 0), val)
+        for sem, val in want.items():
+            if seen.get((q, sem), 0) < val:
+                Q[q].wait_ge(T.sem[sem], val)
+                seen[(q, sem)] = val
+        ins = fn()
+        if kind == "c":
+            sem, inc = own[q], 1
+        elif kind == "d":
+            sem, inc = "d%d" % nd, 16
+            nd += 1
+        else:
+            sem, inc = kind, neng
+            count["sent"] = count.get("sent", 0) + neng
+        if kind in ("c", "d"):
+            ins.then_inc(T.sem[sem], inc)
+        count[sem] = count.get(sem, 0) + inc
+        token[n] = (sem, count[sem])
+    for sem, val in count.items():
+        g.wait_ge(T.sem[sem], val)

@@ -1,57 +1,60 @@
 from concourse.mybir import AluOpType as ALU, AxisListType, ActivationFunctionType as ACT
 
 N, V, B, TR, S = 6, 3072, 384, 256, 6
-LG = TR * S
-WD = LG + V
-KOFF = 49152.0
-CAP = 65536.0
-HELD = 100000.0
+WD = V + TR * S
+U = 131072.0
+CAP = 32304.0
+HELD = 85000.0
 NONE = 8192.0
-VG = (1, 5)
-ABSH = (1,)
-CYC, GAT, SCA, FIX, PEC, PEF, LAT, LAT0, DMA, HOP = 1.04, 1.3, 3.15, 60.0, 0.52, 15.0, 80.0, 80.0, 2200.0, 3300.0
+BW = 392
+BIG = 8192.0
+CYC, GAT, SCA, FIX, PEC, PEF, LAT, DMA, HOP = 1.04, 1.3, 3.15, 60.0, 0.52, 15.0, 80.0, 2200.0, 3300.0
 ROUNDS, SEED = 8000, 1
+PARTS = (("P2", 0, 2), ("PK", 2, 4), ("P2", 4, 6))
 PLACED = {}
-DENSE = True
-BOXB = ("PB", "PE", None, None, "PB", None, None, None)
 
 F32, BF, F16, I32, U16 = "float32", "bfloat16", "float16", "int32", "uint16"
 SCRATCH = {}
 for _n, _c, _d in [
-    ("xsb", V, BF), ("sbt", B, I32), ("pq", 384, I32), ("pqd", 768, BF), ("pqr", V, BF),
-    ("bxi", TR, I32), ("limi", 16, I32), ("limb", 16, I32),
-    ("W", WD + TR, F32), ("XE", V, F32), ("G", 4096 + 16, F32), ("DP", 4096, BF), ("RL", 4096, BF),
-    ("R1", V, F16), ("KM", V, F16), ("IOS", V, I32), ("HEL", 192, U16), ("HAS", 192, F16), ("SLI", 192, F32),
-    ("JO", 192, F32), ("JU", 192, U16), ("JH", B + TR, F32), ("YO", WD + TR, BF), ("YJ", 192, F32), ("YT", 192, F32),
-    ("COL", TR, F32), ("D3", B, F32), ("D2", B, F32), ("CF", B, F32), ("CG", B, F32), ("GV", 128, F32),
-    ("EV", 512, F32), ("E32", 512, BF), ("PI", 8, I32), ("PF", 8, F32), ("PC", 96, F32), ("OH", 16, F32),
-    ("IB", 128, BF), ("NIB", 128, BF), ("N64", 128, BF), ("HIB", 128, BF), ("INJ", 128, BF), ("IH", 128, F16),
-    ("ONE", 128, BF), ("O8", 128, F16), ("ZH", 144, F16), ("ZQ", 144, F16), ("ZB", 144, BF), ("EX", 128, F16),
-    ("EZ", 128, F16), ("SEL", 128, BF), ("S1", 128, BF), ("S2", 128, BF), ("W8", 40, BF), ("WF", 80, BF), ("BG", 256, BF),
-    ("C17", TR, BF), ("I17", 128, BF), ("B17", 128, BF), ("C384", 128, BF), ("RST", TR, F32), ("KEEP", TR, F32),
-    ("B0", 512, BF), ("FBT", B, F32), ("C1", TR, F32), ("CB", 18, F32), ("CT", 18, F32), ("J16", 16, F16),
-    ("OFF", TR, U16), ("ZT", TR, BF), ("INA", TR, BF), ("JK", TR, F32), ("VK", TR, BF), ("FX", TR, BF),
-    ("LB0", TR, BF), ("LB1", TR, BF), ("PM", TR, I32), ("M2", TR, F32), ("PM2", TR, I32),
-    ("TP", (2, 128), F16), ("TQ", (2, 128), F16), ("T2", TR, F16), ("T3", TR, F16),
-    ("GE", TR, F32), ("GF", TR, F32), ("XA", TR, BF), ("XB", TR, BF), ("FE", TR, BF), ("FF", TR, BF),
-    ("LE0", TR, BF), ("LE1", TR, BF), ("JNK", 8 * B, BF), ("AA", TR, BF), ("BV", TR, BF), ("AB", TR, BF),
-    ("TZ", TR, F32), ("TH", TR, F32), ("SE", TR, BF), ("W1", TR, F32), ("W2", TR, F32), ("NL", TR, F32),
-    ("PV0", TR, F32), ("PV1", TR, F32), ("ZI", TR, I32),
-    ("SM", 16 * 40, F32), ("SI", 16 * 4, I32), ("SU", 16 * 6, U16),
-    ("zin", (S + 1, TR), BF), ("bin", (S, 16), U16), ("zout", (S, TR), BF), ("bout", (S, 16), U16),
-    ("bfi", 16, F32), ("bfo", 16, F32),
+    ("xsb", V, BF), ("sb3", 3 * BW, I32), ("pq", 384, I32), ("pqh", 384, F16), ("pqr", V, F16),
+    ("bxi", TR, I32), ("bxh", TR, F16), ("limi", 16, I32), ("limb", 16, I32),
+    ("W", WD + TR, F32), ("XE", V, F32), ("DP", 17 * TR, F32), ("RL", 4096, BF),
+    ("R1", V, F16), ("KM", V, F16), ("IOS", V, I32), ("HEL", 192, U16), ("HS", 192, U16), ("C3K", 192, F16), ("SLI", 384, F32),
+    ("JF", 17 * B, F32), ("ZK", 144, F16),
+    ("JO", 192, F32), ("JU", 192, U16), ("JH", 648, F32), ("YO", WD + TR, BF), ("YL", TR, BF), ("YJ", 192, F32),
+    ("COL", TR, F32), ("D3", 400, F32), ("D2", 400, F32), ("FBT", 400, F32), ("GV", 128, F32), ("GW", 200, F32),
+    ("PI", 8, I32), ("PF", 8, F32), ("PC", 96, F32), ("PH", 16, BF), ("OH", 16, F32),
+    ("MB", 128 * 17, BF), ("MH", 128 * 14, F16), ("EG", 1024, F16), ("GW8", 1024, BF), ("D8", 128, BF), ("MF", 128 * 5, F32), ("W8", 48, BF), ("W8H", 96, F16), ("W8F", 8, F32),
+    ("ZH", 144, F16), ("ZB", 144, F16), ("EH", 328, F16), ("CL", 200, F32), ("CLH", 200, F16), ("BIG", 200, BF),
+    ("RW", 1408, BF), ("CF", 16 * 12, F32), ("C17", TR, BF), ("C1", TR, BF), ("C96", TR, BF), ("DG", TR, BF),
+    ("RST", TR + 16, F32), ("KEEP", TR, F32), ("MASK", TR, BF), ("MASK2", TR, BF), ("BI", 288, I32), ("BC", 288, F32),
+    ("B8", TR, BF), ("CB", 32, F32),
+    ("OT", TR, I32), ("OU", TR, I32), ("OFF", TR, U16), ("INA", TR, BF), ("ZC", TR, F32), ("JK", TR, F32), ("FX", TR, F16),
+    ("H", 656, BF), ("MS", 200, F32), ("LK", TR, BF), ("PM", TR, I32), ("M2", TR, F32), ("PM2", TR, I32),
+    ("SK", TR, F16), ("SF", TR, F16), ("SN", TR, F16), ("SO", TR, F16), ("SC", TR, F32), ("LS", TR, BF),
+    ("XD", TR, BF), ("XF", TR, BF), ("FE", TR, F16), ("FF", TR, F16), ("LE0", TR, F16), ("LE1", TR, F16),
+    ("JNK", 8 * B, BF), ("AA", TR, BF), ("HB", TR, BF), ("AB", TR, BF), ("TZ", TR, F32), ("TH", TR, F32),
+    ("SE", TR, BF), ("UU", TR, BF), ("X", TR, F32), ("PV0", TR, F32), ("PV1", TR, F32), ("SG", TR, F32), ("ZM", TR, BF),
+    ("SM", 16 * 40, F32), ("SI", 16 * 8, I32), ("SU", 16 * 10, U16), ("SH", 16 * 12, F16),
+    ("zin", (S + 1) * TR, BF), ("zout", S * TR, BF), ("lin", S * 32, U16), ("lout", S * 32, U16),
+    ("stin", S * 48, I32), ("stout", S * 48, I32), ("Y3", 48, F32), ("T3", 48, F32), ("bfi", 16, F32), ("bfo", 16, F32),
 ]:
-    SCRATCH[_n] = ("sbuf", [128] + (list(_c) if isinstance(_c, tuple) else [_c]), _d)
+    SCRATCH[_n] = ("sbuf", [128, _c], _d)
 BANKS = ("P0", "P1", "P2", "PK", "PA", "PB", "PE", "PD")
 for _n in BANKS:
     SCRATCH[_n] = ("psum", [128, 512], F32)
 
-SEMAPHORES = (["sv", "ss", "sp", "sg", "sent"] + ["d%d" % k for k in range(24)]
-              + ["az%d" % k for k in range(S)] + ["ab%d" % k for k in range(S)])
-WHOLE = {"TP": "TP0 TP1 TP2 TP3 TP4 TP5", "TQ": "TQ0 TQ1 TQ2 TQ3 TQ4", "Ws": " ".join("W%d" % m for m in range(12)),
-         "W": "Wl Wd " + " ".join("W%d" % m for m in range(12)), "G": "G0 G1 G2 G3 G4 G5 G6 G7 Gs",
-         "ce": " ".join("ce%d" % k for k in range(16)), "cb": " ".join("cb%d" % k for k in range(16)),
-         "pqr": "pqr0 pqr1 pqr2 pqr3", "XE": "XE0 XE1 XE2 XE3 XE4 XE5", "YO": "YO0 YO1 YO2 YOd"}
+SEMAPHORES = (["sv", "ss", "sp", "sg", "sent"] + ["d%d" % k for k in range(40)]
+              + ["a%s%d" % (x, k) for x in "zlsp" for k in range(S)])
+
+
+def many(x, n, lo=0):
+    return " ".join("%s%d" % (x, k) for k in range(lo, n))
+
+
+WHOLE = {"Ws": many("W", 12), "W": "Wl Wd " + many("W", 12), "DP": many("DP", 17), "ce": many("ce", 16), "XE": many("XE", 6),
+         "KM": many("KM", 6), "sb3": many("sb", 8), "pqr": "pqr0 pqr1", "YO": many("YO", 5) + " YOd", "PF": many("PF", 1),
+         "JF": many("JF", 4), "RW": many("RW", 4)}
 
 
 def names(text):
@@ -60,8 +63,10 @@ def names(text):
 
 def put_in_order(ops):
     wrote, read, deps = {}, {}, []
+    soft = PLACED.setdefault("soft", set())
     for n, (ways, R, Wr) in enumerate(ops):
         d = set()
+        fed = {wrote[r] for r in R + Wr if r in wrote and r[0] != "~"}
         for r in R:
             if r in wrote:
                 d.add(wrote[r])
@@ -73,13 +78,15 @@ def put_in_order(ops):
             d.update(read.get(r, ()))
         d.discard(n)
         deps.append(d)
+        soft.update((x, n) for x in d if x not in fed and ways[0][4] == "c" and ops[x][0][0][4] == "c")
         for r in R:
             read.setdefault(r, []).append(n)
         for r in Wr:
             wrote[r] = n
             read[r] = []
     if "place" not in PLACED:
-        PLACED["place"] = shorten([[w[:3] for w in o[0]] for o in ops], [sorted(d) for d in deps], [kind_of(o) for o in ops])
+        PLACED["place"] = shorten([[w[:3] for w in o[0]] for o in ops], [sorted(d) for d in deps], [kind_of(o) for o in ops], None, ROUNDS)
+        PLACED["ops"] = [(o[1], o[2], [w[:3] for w in o[0]], sorted(d)) for o, d in zip(ops, deps)]
     place = PLACED["place"]
     return [(n, ops[n][0][place[n][0]], deps[n]) for n in sorted(range(len(ops)), key=lambda k: (place[k][1], k))]
 
@@ -89,7 +96,7 @@ def kind_of(o):
 
 
 def place_calls(ops, deps, order, fixed, back):
-    busy, place = {q: [] for q in "vspgy"}, [None] * len(ops)
+    busy, place, soft = {q: [] for q in "vspgy"}, [None] * len(ops), PLACED["soft"]
     for n in order:
         best = None
         for k in (range(len(ops[n])) if fixed[n] is None else (fixed[n],)):
@@ -97,7 +104,7 @@ def place_calls(ops, deps, order, fixed, back):
             t = 0.0
             for d in deps[n]:
                 e = place[d][2]
-                if w[0] != "p" or ops[d][0][0] != "p":
+                if w[0] != ops[d][place[d][0]][0] or (w[0] != "p" and ((n, d) if back else (d, n)) not in soft):
                     e += LAT
                 if e > t:
                     t = e
@@ -123,7 +130,7 @@ def place_calls(ops, deps, order, fixed, back):
     return place
 
 
-def shorten(ops, deps, kinds):
+def shorten(ops, deps, kinds, cur=None, ROUNDS=None, SEED=1):
     n_ = len(ops)
     succ = [[] for _ in ops]
     level = [0.0] * n_
@@ -139,7 +146,7 @@ def shorten(ops, deps, kinds):
         return (seed[0] >> 8) % k
 
     free = [n for n in range(n_) if len(ops[n]) > 1]
-    cur = place_calls(ops, deps, sorted(range(n_), key=lambda k: (-level[k], k)), [None] * n_, False)
+    cur = cur or place_calls(ops, deps, sorted(range(n_), key=lambda k: (-level[k], k)), [None] * n_, False)
     best, cs = cur, max(x[2] for x in cur)
     bs = cs
     for it in range(ROUNDS):
@@ -167,6 +174,9 @@ def shorten(ops, deps, kinds):
                     key[m] = min([key[d] for d in succ[m]] + [key[n] + 1.0 + draw(1500)]) - 0.5
                 else:
                     key[n] = max([key[d] for d in deps[n]] + [key[m] - 1.0 - draw(1500)]) + 0.5
+            for n in range(n_):
+                for d in deps[n]:
+                    key[n] = max(key[n], key[d])
             new = place_calls(ops, deps, sorted(range(n_), key=lambda k: (key[k], k)), fixed, False)
             s_ = max(x[2] for x in new)
             if s_ < cs + 150.0 * (1.0 - it / ROUNDS):
@@ -240,7 +250,7 @@ def rank_program(g, core, T, topo):
                 for n, (o, l, r) in enumerate(items):
                     ins = g.tensor.matmul(o, l, r, first and n == 0, last and n == len(items) - 1)
             return ins
-        op([way("p", sum(PEF + max(min(64, nel(l)), nel(r)) * PEC for it in groups for o, l, r in it), fn)], R, Wr)
+        op([way("p", sum(PEF + max(min(64, nel(l)), nel(r)) * PEC * (1 if two(l) else 4) for it in groups for o, l, r in it), fn)], R, Wr)
 
     def mm(R, Wr, items, first=True, last=True):
         mms(R, Wr, [items], first, last)
@@ -284,6 +294,9 @@ def rank_program(g, core, T, topo):
         s_, b_ = 1.0 if scale is None else scale, 0.0 if bias is None else bias
         op([act_way(out, a, ACT.Identity, ind, {"scale": s_, "bias": b_}), ts_way(out, a, s_, mul, b_, add, ind)], R, Wr)
 
+    def relu2(R, Wr, out, a, bias, ind=None):
+        op([act_way(out, a, ACT.Relu, ind, {"bias": bias}), ts_way(out, a, bias, add, 0.0, mx, ind)], R, Wr)
+
     def scan(R, Wr, out, d0, d1, o0, o1):
         op([way("v", plain(nel(d0)), lambda: g.vector.tensor_tensor_scan(out, d0, d1, 0.0, o0, o1))], R, Wr)
 
@@ -293,16 +306,36 @@ def rank_program(g, core, T, topo):
 
     slots = {}
 
-    def sm(name, a=0, b=16, st=1, pool="SM"):
+    def sm(name, a=0, b=16, st=1, pool="SM", w=16, rows=None):
         d = slots.setdefault(pool, {})
         k = d.setdefault(name, len(d))
-        return T[pool][:, 16 * k + a:16 * k + b:st]
+        if rows is not None:
+            return T[pool][rows[0]:rows[1], w * k + a:w * k + b:st]
+        return T[pool][:, w * k + a:w * k + b:st]
 
     def si(name):
         return sm(name, pool="SI")
 
     def su(name):
         return sm(name, pool="SU")
+
+    def sh(name, a=0, b=16, st=1):
+        return sm(name, a, b, st, pool="SH")
+
+    def mb(name, rows=None):
+        return sm(name, 0, 128, pool="MB", w=128, rows=rows)
+
+    def mh(name, rows=None, b=128):
+        return sm(name, 0, b, pool="MH", w=128, rows=rows)
+
+    def mf(name, rows=None):
+        return sm(name, 0, 128, pool="MF", w=128, rows=rows)
+
+    def w8(name):
+        return sm(name, 0, 8, pool="W8", w=8)
+
+    def wh(name):
+        return sm(name, 0, 8, pool="W8H", w=8)
 
     nxt = T.cores[(rank + 1) % N]
     rid, pid = topo.addr(nxt)[:2]
@@ -317,40 +350,56 @@ def rank_program(g, core, T, topo):
     dma("y", "", "xsb0", T.xsb[:, 0:1536], T.xs[:, 0:1536], 600000)
     dma("s", "", "bxi", T.bxi[0:8, :], T.bx[:])
     dma("y", "", "xsb1", T.xsb[:, 1536:V], T.xs[:, 1536:V], 800000)
-    dma("s", "", "sbt", T.sbt[:], T.sb[:], 196608)
-    dma("y", "", "zin0", T.zin[:, 0, :], T.zs[:], 65536)
+    dma("s", "", "sb0", T.sb3[:, 0:B], T.sb[:], 196608)
+    dma("y", "", "sb1", T.sb3[16:128, BW:BW + B], T.sb[0:112, :], 196608)
+    dma("y", "", "sb2", T.sb3[0:112, 2 * BW:2 * BW + B], T.sb[16:128, :], 196608)
+    dma("y", "", "sb3a", T.sb3[0:16, BW:BW + B], T.sb[0:16, :])
+    dma("y", "", "sb4", T.sb3[112:128, 2 * BW:2 * BW + B], T.sb[0:16, :])
+    dma("y", "", "zraw ZM", T.ZM[:], T.zs[:], 65536)
     dma("y", "", "limi", T.limi[0:1, :], T.lim[:])
+    for k in range(3):
+        ms("sb%d" % (5 + k), T.sb3[:, BW * k + B:BW * k + BW], 0)
 
     iota("PI0", T.PI[:, 0:1], [[0, 1]], 0, 1, False)
     iota("COL", T.COL[:], [[1, TR]], 0, 0)
-    iota("D3", T.D3[:], [[0, 24], [1, 16]], 0, 0)
-    iota("D2", T.D2[:], [[1, 24], [0, 16]], -12, 0)
-    iota("EV", T.EV[:], [[1, 32], [0, 16]], 0, 0)
     iota("GV", T.GV[:], [[16, 8], [0, 16]], 0, 0)
+    iota("ONE", mb("ONE"), [[0, 128]], 1, 0)
+    iota("D3", T.D3[:], [[0, 25], [1, 16]], 0, 0)
+    iota("D8", T.D8[:], [[0, 16], [1, 8]], 0, 0)
+    iota("GW8", T.GW8[:], [[-16, 8], [1, 128]], 0, 0)
+    for k, c in ((0, 192), (3, 3583.5), (4, 192.0 * (5.0 + 5.0 / 512) + 3840.0)):
+        iota("CF%d" % k, T.CF[0:1, 16 * k:16 * k + 16], [[0, 16]], int(8 * c), 0)
+    iota(many("CF", 5 + S, 5), T.CF[0:1, 80:80 + 16 * S], [[-4096, S], [0, 16]], int(8 * (BIG - 1 - 192 - 512 * 3)), 0)
+    iota("D2", T.D2[:], [[1, 25], [0, 16]], 1024, 0)
+    iota("BC1", T.BC[:, TR:TR + 12], [[256, 12]], 0, 0)
+    iota("BC2", T.BC[:, TR + 12:TR + 32], [[256, 20]], 0, 0)
+    iota("GW", T.GW[:], [[16, 8], [0, 25]], 0, 0)
+    iota("CL", T.CL[0:1, :], [[0, 8], [-1, 25]], -1024, 0)
     op([way("g", 300.0, lambda: g.partition_broadcast(T.limb[:], T.limi[0:1, :], 128))], "limi", "limb")
+    iota("JH", T.JH[:], [[0, 648]], -int(NONE), 0)
+    iota("JF0", T.JF[:, 0:1632], [[0, 1632]], -int(NONE), 0)
+    for k in range(1, 4):
+        dma("y", "JF0", "JF%d" % k, T.JF[:, 1632 * k:1632 * k + 1632], T.JF[:, 0:1632], 840000 * k)
+    iota("RST", T.RST[:], [[0, TR + 16]], 0, 0)
     iota("IOS", T.IOS[:], [[1, V]], 0, 0, False)
-    iota("ONE", T.ONE[:], [[0, 128]], 1, 0)
-    iota("JH", T.JH[:], [[0, B + TR]], int(NONE), 0)
-    iota("TZ", T.TZ[:], [[0, TR]], 0, 0)
-    iota("RST", T.RST[:], [[0, TR]], 0, 0)
-    iota("KEEP", T.KEEP[:], [[0, TR]], 1, 0)
-    iota("Wl", T.W[:, 0:LG], [[0, LG]], 0, 0)
+    iota("RW0", T.RW[:, 0:TR], [[-1, TR]], 0, 0)
+    iota("RW1", T.RW[0:1, TR:2 * TR], [[0, TR]], 256, 0)
+    iota("RW2", T.RW[0:1, 512:640], [[0, 128]], 2048, 0)
+    iota("RW3", T.RW[0:1, 640:1408], [[-2048, S], [0, 128]], 224 * 2048, 0)
+    iota("Wl", T.W[:, V:WD], [[0, WD - V]], 0, 0)
     iota("Wd", T.W[:, WD:WD + TR], [[0, TR]], 0, 0)
-    iota("YOd", T.YO[:, WD:WD + TR], [[0, TR]], 0, 0)
-    ms("TP", T.TP[:], 0.0)
-    ms("TQ", T.TQ[:], 0.0)
-    ms("RST", T.RST[:, 0:TR:16], CAP)
-    ms("KEEP", T.KEEP[:, 0:TR:16], 0.0)
-    ms("AI", si("AI"), 0)
-    for k, (sh, mk) in enumerate(((0, 15), (0, 112), (0, 31), (0, 7), (3, 3), (4, 1), (3, 1))):
-        ts("PI0", "PI%d" % (k + 1), T.PI[:, k + 1:k + 2], T.PI[:, 0:1], sh, shr, mk, band)
-    cp(" ".join("PI%d" % k for k in range(8)), "PF", T.PF[:], T.PI[:])
-    pc, rc, gc, p32, q7, q3, par, q8 = [T.PF[:, k:k + 1] for k in range(8)]
+    iota("YOd", T.YO[:, WD - TR:WD + TR], [[0, 2 * TR]], 0, 0)
+    ms("JH", T.JH[:, B:B + 1], 0.0)
+    ms("RST", T.RST[:, 0:TR + 16:16], CAP)
+    for k, (sh_, mk) in enumerate(((0, 15), (0, 112), (4, 7), (0, 7), (4, 1), (3, 1))):
+        ts("PI0", "PI%d" % (k + 1), T.PI[:, k + 1:k + 2], T.PI[:, 0:1], sh_, shr, mk, band)
+    cp(many("PI", 7), "PF", T.PF[:, 0:7], T.PI[:, 0:7])
+    pc, rc, gc, xg, q7, par, q8 = [T.PF[:, k:k + 1] for k in range(7)]
+    lin2("PF", "PI7", T.PF[:, 7:8], q8, 8.0)
     ts("COL PF", "OH", T.OH[:], T.COL[:, 0:16], rc, eq)
-    cp("pq0 pq1", "pqh", T.pqd[:, 0:384], T.pq[:])
-    tt("pq0 pq1 pqh", "pql", T.pqd[:, 384:768], T.pq[:], T.pqd[:, 0:384], sub)
-    for f, (c0, nm) in enumerate(((0, "pqh"), (384, "pql"), (192, "pqh"), (576, "pql"))):
-        dma("y", nm, "pqr%d" % f, T.pqr[8 * f:8 * f + 8, :], T.pqd[:, c0:c0 + 192], 49152)
+    cp("pq0 pq1", "pqh", T.pqh[:], T.pq[:])
+    for f in range(2):
+        dma("ys"[f], "pqh", "pqr%d" % f, T.pqr[8 * f:8 * f + 8, :], T.pqh[:, 192 * f:192 * f + 192], 49152)
 
     pcn = [0]
 
@@ -363,428 +412,444 @@ def rank_program(g, core, T, topo):
         lin2(an + " " + bn, n, c, a, s, b)
         return c, n
 
+    def test(a, c, o, s):
+        x, n = col()
+        ts("PF", n, x, a, c, o, s, mul)
+        return x, n
+
     def rows(spec, prev=None):
         for r, w in spec:
             prev = lin(T.OH[:, r:r + 1], "OH", float(w), 0.0 if prev is None else prev[0], "" if prev is None else prev[1])
         return prev
 
-    z7, z7n = lin(q7, "PF", 16.0, 15.0)
-    ts("COL PF", "IB", T.IB[:], T.COL[:, 0:128], pc, eq)
-    ts("COL " + z7n, "ZQ", T.ZQ[:], T.COL[:, 0:144], z7, eq)
-    cp("bxi", "T2", T.T2[0:8, :], T.bxi[0:8, :])
-
-    def to_list(R, src, row, k, bank_, c0, extra=None, flat=False):
-        items = [] if extra is None else [extra]
-        for r in range(16):
-            rhs = src[row:row + k, 16 * r:16 * r + 16] if flat else src[row:row + k, r:TR:16]
-            items.append((T[bank_][:, c0:c0 + 16], T.ZQ[row:row + k, 15 - r:143 - r], rhs))
-        mm(R + " ZQ", bank_, items)
-
-    to_list("T2", T.T2, 0, 8, "PE", 0)
-    cp("PE", "bin0", T.bin[:, 0, :], T.PE[:, 0:16])
-    l1, l1n = rows([(2, 1.0 / 512)])
-    l2, l2n = rows([(5, 1.0 / 512)])
-    m1, m1n = rows([(1, 1.0 / 512)])
-    m2, m2n = rows([(4, 1.0 / 512)])
-    lin2("D3 %s %s" % (l1n, l2n), "CF", T.CF[:], T.D3[:], l2, l1)
-    lin2("D2 %s %s" % (m1n, m2n), "CG", T.CG[:], T.D2[:], m2, m1)
-    tt("CF D3", "CF", T.CF[:], T.CF[:], T.D3[:], mul)
-    tt("CG D2", "CG", T.CG[:], T.CG[:], T.D2[:], mul)
-    tt("CF CG", "B0", T.B0[:, 0:256], T.CF[:, 64:320], T.CG[:, 64:320], add)
-    lin2("B0", "B0b", T.B0[:, 256:512], T.B0[:, 0:256])
-    k0, k0n = rows([(13, 0.25)])
-    lin2("CF B0 " + k0n, "CF", T.CF[:], T.CF[:], None, k0)
-    tt("CF CG", "FBT", T.FBT[:], T.CF[:], T.CG[:], add)
-    s7, s7n = lin(q3, "PF", 1.0, z7, z7n)
-    ts("COL " + s7n, "SEL", T.SEL[:], T.COL[:, 8:136], s7, eq, 1.0 / 1024, mul)
-    a0, a0n = rows([(0, 1.0 / 512), (3, -8.0 / 512)])
-    b0, b0n = rows([(3, 1.0 / 512)])
-    l0, l0n = rows([(12, 0.125)], (k0, k0n))
-    n0, n0n = rows([(12, -0.125)], lin(k0, k0n, 1.0, 128.0))
-    lin2("COL %s %s" % (a0n, b0n), "CT", T.CT[:], T.COL[:, 0:18], b0, a0)
-    lin2("COL", "CB", T.CB[:], T.COL[:, 0:18], None, -8.0)
-    tt("CT CB", "CT", T.CT[:], T.CB[:], T.CT[:], mul)
-    lin2("CT CB " + l0n, "CBa", T.CB[:, 0:6], T.CT[:, 0:6], None, l0)
-    lin2("CT " + n0n, "CB", T.CB[:, 6:18], T.CT[:, 6:18], None, n0)
-    ts("EV PF", "E32", T.E32[:], T.EV[:], p32, eq)
-
-    for m, bk in enumerate(("P0", "P1", "P2", "PB", "PD", "PA")):
-        sl = slice(512 * m, 512 * m + 512)
-        mm("IB xsb%d B0 B0b" % (m // 3), bk, [(T[bk][:], T.IB[:], T.xsb[:, sl]), (T[bk][:], T.IB[:], T.B0[:])], last=False)
-        mm("SEL pqr", bk, [(T[bk][:], T.SEL[0:32, :], T.pqr[0:32, sl])], first=False)
-        for u in range(2):
-            c0 = LG + 512 * m + 256 * u
-            lin2(bk + " CB", "W%d" % (2 * m + u), T.W[:, c0:c0 + 256], T[bk][:, 256 * u:256 * u + 256], None,
-                 T.CB[:, 6 + 2 * m + u:7 + 2 * m + u])
-
+    IB, ONE = mb("IB"), mb("ONE")
+    ts("COL PF", "IB", IB, T.COL[:, 0:128], pc, eq)
+    for nm, w in (("UI", U), ("NIB", -1.0), ("N64", 64.0 * U), ("HIB", 0.5), ("UH", U / 2), ("N512", -512.0 * U),
+                  ("IU", 1.0 / U)):
+        lin2("IB", nm, mb(nm), IB, w)
+    for t in range(S):
+        lin2("IB", "IT%d" % t, mb("IT%d" % t), IB, NONE + 256.0 * t)
+    lin2("IB", "IH", mh("IH"), IB)
+    lin2("ONE", "ONEH", mh("ONEH"), ONE)
+    for nm, w in (("I4", 4.0), ("NI", 1.0), ("NI3", 5.0 + 5.0 / 512)):
+        lin2("IB", nm, mf(nm), IB, w)
+    ts("GV PF", "B1K", mf("B1K"), T.GV[:], gc, eq, 1024.0, mul)
+    lin2("ONE", "O2K", mf("O2K", (0, 1)), mb("ONE", (0, 1)), 0.125)
+    ts("GV PF", "BLK", w8("BLK"), T.GV[:, 0:128:16], gc, eq)
+    BLK = w8("BLK")
+    lin2("BLK", "W8A", w8("W8A"), BLK, 32.0 / U)
+    lin2("BLK", "BLKF", T.W8F[:], BLK)
+    ts("D3 PF", "MASK", T.MASK[:], T.D3[:, 0:TR], rc, eq)
+    cp("COL", "SPR", su("SPR"), T.COL[:, 0:16])
+    r16, r16n = lin(rc, "PF", 16.0, 0.0)
+    ts("COL " + r16n, "PERM", su("PERM"), T.COL[:, 0:16], r16, add)
+    lin2("COL PF", "J16", sh("J16"), T.COL[:, 0:16], 16.0, rc)
     npar, nparn = lin(par, "PF", -1.0, 1.0)
-    sq = rows([(3, 2.0 ** 30), (4, 2.0 ** 30), (5, 2.0 ** 30)])
-    bc, bcn = rows([(6, 2.0 ** 23)], sq)
-    j0, j0n = rows([(6, 1.0 / 1024)])
-    sc, scn = col()
-    ts("PF", scn, sc, rc, 3.0, lt, -2.0 ** 40, mul)
-    LS = []
-    for u, (pp, ppn) in enumerate(((npar, nparn), (par, "PF"))):
-        a, an = lin(sc, scn, pp, 0.0, ppn)
-        b, bn = lin(bc, bcn, pp, 0.0, ppn)
-        LS.append((a, b, an + " " + bn))
-        ts("ONE " + ppn, "BG%d" % u, T.BG[:, 128 * u:128 * u + 128], T.ONE[:], pp, mul, 2.0 ** 22, mul)
-    lin2("COL " + j0n, "C1", T.C1[:], T.COL[:], j0)
-    lin2("IB", "I17", T.I17[:], T.IB[:], 20480.0)
-    lin2("IB PF", "C17", T.C17[:, 0:128], T.IB[:], rc)
-    lin2("IB PF", "C17b", T.C17[:, 128:256], T.IB[:], rc)
-    lin2("ONE", "C384", T.C384[:], T.ONE[:], KOFF / 128)
-    ts("GV PF", "B17", T.B17[:], T.GV[:], gc, eq, 8192.0, mul)
-    ts("GV PF", "BLK", T.W8[:, 0:8], T.GV[:, 0:128:16], gc, eq)
-    BLK, W8P, W8N, W8I, W8A = [T.W8[:, 8 * k:8 * k + 8] for k in range(5)]
-    for nm, ap, w in (("W8P", W8P, 32.0), ("W8N", W8N, -16.0), ("W8I", W8I, 2.0 ** 23), ("W8A", W8A, 16.0)):
-        lin2("BLK", nm, ap, BLK, w)
+    lin2("IB " + nparn, "P00", mh("P00"), IB, npar)
+    lin2("IB PF", "P11", mh("P11"), IB, par)
+    up, upn = lin(pc, "PF", 1.0, 16.0)
+    dn, dnn = lin(pc, "PF", 1.0, -16.0)
+    ts("COL %s %s" % (upn, nparn), "P10", mh("P10"), T.COL[:, 0:128], up, eq, npar, mul)
+    ts("COL PF " + dnn, "P01", mh("P01"), T.COL[:, 0:128], dn, eq, par, mul)
+    ts("ONE PF", "VO0", sh("VO", 0, 16, 2), T.MB[:, 0:8], par, mul, float(BW), mul)
+    ts("ONE " + nparn, "VO1", sh("VO", 1, 16, 2), T.MB[:, 0:8], npar, mul, 2.0 * BW, mul)
 
-    def wf(f):
-        return T.WF[:, 8 * f:8 * f + 8]
+    def spread(R, Wr, out, src, mask="MASK"):
+        tt(R + " SPR " + mask, Wr, out[:], src.indirect(su("SPR")), T[mask][:], mul, "g")
 
-    def weights(f, spec, prev=None):
-        c, n = rows(spec, prev)
-        lin2("BLK " + n, "WF%d" % f, wf(f), BLK, c)
-
-    low = rows([(1, 8192.0), (2, 512.0)])
-    weights(0, [(6, 2.0 ** 23), (11, 2.0 ** 33)], lin(sq[0], sq[1], -1.0, 0.0))
-    weights(2, [(13, 768.0)], low)
-    weights(1, [(0, 131072.0), (13, 8704.0)], low)
-    weights(3, [(7, -1024.0), (8, -1024.0)])
-    weights(4, [(9, -1024.0), (10, -1024.0)])
-    weights(5, [(12, 512.0)])
-    weights(6, [(9, 2.0 ** -13), (10, 2.0 ** -13), (12, 2.0 ** -11), (13, 2.0 ** -12)])
-    lin2("WF6", "WF7", wf(7), wf(6), 2048.0)
-    lin2("WF2", "WF8", wf(8), wf(2), -2.0 ** -23)
-    lin2("WF2", "WF9", wf(9), wf(2), -2.0 ** -12)
-    spc, spcn = rows([(3, 0.25), (11, 0.25), (9, -1.0 / 1024)])
-    lin2("ONE " + spcn, "Gs", T.G[:, 4096:4112], T.ONE[:, 0:16], spc, 128.0)
-    lin2("IB", "IH", T.IH[:], T.IB[:])
-    lin2("IB", "NIB", T.NIB[:], T.IB[:], -1.0)
-    lin2("IB", "N64", T.N64[:], T.IB[:], -64.0)
-    lin2("IB", "HIB", T.HIB[:], T.IB[:], 0.5)
-    lin2("ONE", "O8", T.O8[:], T.ONE[:], 8.0)
-    lin2("GV PF", "DL", sm("DL", 0, 8), T.GV[:, 0:128:16], None, rc)
-    lin2("DL", "DLb", sm("DL", 8, 16), sm("DL", 0, 8), None, 128.0)
-    lin2("DL DLb", "J16", T.J16[:], sm("DL"), 16.0)
-    lin2("DL DLb", "DM", sm("DM"), sm("DL"), None, float(WD))
-    for h in range(2):
-        lin2("ONE PF", "DW%d" % h, sm("DW", 8 * h, 8 * h + 8), T.ONE[:, 0:8], pc, float(WD + 128 * h))
-        cp("limb", "L0%d" % h, sm("L0", 8 * h, 8 * h + 8), T.limb[:, 0:16:2])
-        ts("limb", "SL%d" % h, sm("SL", 8 * h, 8 * h + 8), T.limb[:, 1:16:2], 16.0, mul, KOFF + 16.0, add)
-    lin2("DW0 DW1", "DB", sm("DB"), sm("DW"), None, float(B - WD))
-    pv_, pvn_ = lin(pc, "PF", 1.0, -NONE)
-    lin2("COL " + pvn_, "VC", sm("VC"), T.COL[:, 0:16], 128.0, pv_)
-    lin2("VC", "VL", sm("VL"), sm("VC"), None, NONE + 1.0)
-    q16, q16n = lin(q7, "PF", 16.0, 0.0)
-    ez, ezn = lin(q8, "PF", 513.0, -512.0)
-    ts("GV " + q16n, "EX", T.EX[:], T.GV[:], q16, eq)
-    lin2("EX " + ezn, "EZ", T.EZ[:], T.EX[:], ez)
-    nj, njn = lin(T.OH[:, 6:7], "OH", -1.0, 1.0)
-    lin2("IB " + njn, "INJ", T.INJ[:], T.IB[:], nj)
-    m78, m78n = rows([(7, 1.0), (8, 1.0)])
-    lin2("IB " + m78n, "S1", T.S1[:], T.IB[:], m78)
-    p2, p2n = lin(pc, "PF", 1.0, 2.0)
-    g15, g15n = lin(gc, "PF", 1.0, 15.0)
-    lin2("ZQ PF", "ZB", T.ZB[:], T.ZQ[:], par)
-    r0, r0n = lin(rc, "PF", 1.0, float(LG))
-    lin2("COL " + r0n, "SLI", T.SLI[:], T.COL[:, 0:192], 16.0, r0)
-    r192, r192n = lin(rc, "PF", 192.0, 0.0)
-    lin2("COL " + r192n, "YJ", T.YJ[:], T.COL[:, 0:192], None, r192)
-    ts("COL %s %s" % (p2n, m78n), "S2", T.S2[:], T.COL[:, 0:128], p2, eq, m78, mul)
-    ts("COL " + g15n, "ZH", T.ZH[:], T.COL[:, 0:144], g15, eq)
-
-    def homes(part):
-        if part == 0:
-            mm("ZB pqr", "PE", [(T.PE[:, 0:192], T.ZB[0:32, 15 - r:143 - r], T.pqr[0:32, r:V:16]) for r in range(16)])
-            cp("PE", "HEL", T.HEL[:], T.PE[:, 0:192])
-            for u in range(6):
-                sl = slice(512 * u, 512 * u + 512)
-                tt("sbt HEL IOS", "KM%d" % u, T.KM[:, sl], T.sbt[:].indirect(T.HEL[:, 32 * u:32 * u + 32]), T.IOS[:, sl], eq, "g")
+    def to_list(sn, c0, blk, bn, extra=None, bk="PE"):
+        its = [(T[bk][:, c0 + 8 * h:c0 + 8 * h + 8], T[sn][:, 128 * h:128 * h + 128], blk) for h in range(2)]
+        if extra is None:
+            mms(sn + " " + bn, bk, [[x] for x in its])
         else:
-            mm("ZH KM0 KM1 KM2 KM3 KM4 KM5", "P2", [(T.P2[:, 0:192], T.ZH[:, 15 - r:143 - r], T.KM[:, r:V:16]) for r in range(16)])
-            lin2("P2", "HAS", T.HAS[:], T.P2[:, 0:192], -NONE, NONE)
+            mm("%s %s IH %s" % (sn, bn, extra), bk, [(T[bk][:, c0:c0 + 16], mh("IH"), sh(extra))] + its)
 
-    homes(0)
+    def as_list(R, sn, src, c0, mask, extra=None, bk="PE"):
+        tt("%s SP8 %s" % (R, mask), sn, T[sn][:, 0:128], src.indirect(sm("SP8", 0, 8, pool="SU")), mh(mask), mul, "g")
+        o = T[bk][:, c0:c0 + 16]
+        mm("%s EG IH %s" % (sn, extra or ""), bk, ([(o, mh("IH"), sh(extra))] if extra else [])
+           + [(o, T.EG[:, 128 * q:128 * q + 128], T[sn][:, 16 * q:16 * q + 16]) for q in range(8)])
+
+    ts("GW8 PF", "EG", T.EG[:], T.GW8[:], rc, eq)
+    lin2("PI7 COL", "UT", sm("UT", 0, 8), T.COL[:, 0:8], None, T.PF[:, 7:8])
+    cp("UT", "SP8", sm("SP8", 0, 8, pool="SU"), sm("UT", 0, 8))
+    ts("D8 PF", "MN", mh("MN"), T.D8[:], xg, eq, -1.0, mul)
+    ts("D8 PF", "M256", mh("M256"), T.D8[:], xg, eq, 256.0, mul)
+
+    def pair_lists(out, on, both=False):
+        as_list("af", "SN", sm("af"), 32, "MN")
+        lin2("PE", "BH", sh("BH"), T.PE[:, 32:48])
+        mm("BH IH VO0 VO1 P00 P01 P10 P11", "PE", [(T.PE[:, 48:64], mh("IH"), sh("VO"))]
+           + [(T.PE[:, 48 + v:64:2], mh("P%d%d" % (u, v)), sh("BH", u, 16, 2)) for u in range(2) for v in range(2)])
+        cp("PE", on, out, T.PE[:, 32 if both else 48:64])
+
+    cp("bxi", "bxh", T.bxh[0:8, :], T.bxi[0:8, :])
+    mms("bxh IH", "PA", [[(T.PA[:, 8 * h:8 * h + 8], T.bxh[0:8, 128 * h:128 * h + 128], mh("IH", (0, 8), 8))] for h in range(2)])
+    ts("PA", "stin0", T.stin[:, 16:32], T.PA[:, 0:16], -1.0, mul, BIG - 1, add)
+    lin2("PA", "af", sm("af"), T.PA[:, 0:16], -1.0)
+    pair_lists(T.lin[:, 0:32], "lin0 pin0", True)
+    lin2("zraw", "zin0", T.zin[:, 0:TR], T.ZM[:], U)
+    ts("ONE PF", "SP3", su("SP3"), T.MB[:, 0:16], rc, mul)
+    for t in range(S):
+        iota("sx%d" % t, T.stin[:, 48 * t + 32:48 * t + 48], [[128, 2], [0, 8]], WD, 1, False)
+    ms("Y0", T.Y3[:, 0:16], -float(B))
+
+    LN2 = 0.6931471805599453
+    act("PF", "PH0", T.PH[:, 0:1], rc, ACT.Exp, scale=-LN2)
+    act("PF", "PH1", T.PH[:, 1:2], rc, ACT.Exp, scale=LN2, bias=-LN2)
+    lin2("COL PF", "TI", sm("TI", 0, 2), T.COL[:, 0:2], 128.0, pc)
+    act("TI", "PH2", T.PH[:, 2:4], sm("TI", 0, 2), ACT.Exp, scale=-0.4 * LN2, bias=51.2 * LN2)
+    for h in range(2):
+        ts("ONE PH2", "TB%d" % h, sm("THB", 8 * h, 8 * h + 8), T.MB[:, 0:8], T.PH[:, 2 + h:3 + h], mul, T.PH[:, 2 + h:3 + h], mul)
+    lin2("TB0 TB1", "THB", sm("THB"), sm("THB"), 2.57 * 1024)
+    sr, srn = lin(T.PH[:, 0:1], "PH0", 1.0, 0.0)
+    sb_, sbn = lin(T.PH[:, 0:1], "PH0", 0.5, -0.5)
+    lin2("COL", "BC0", T.BC[:, 0:TR], T.COL[:])
+    ts("BC0 BC1 BC2 %s %s" % (srn, sbn), "BI", T.BI[:], T.BC[:], sr, mul, sb_, add)
+    ts("BI", "BI", T.BI[:], T.BI[:], 1, band)
+    a2, a2n = test(rc, 8.0, lt, 2.0)
+    a1, a1n = test(rc, 8.0, lt, -1.0)
+    ts("BI %s %s" % (a2n, a1n), "B8", T.B8[:], T.BI[:, 0:TR], a2, mul, a1, add)
+    b2, b2n = test(rc, 12.0, lt, 2.0)
+    lin2("%s %s" % (b2n, a2n), b2n, b2, a2, -1.0, b2)
+    bs_, bsn = rows([(12, -1.0), (13, -192.0), (14, -192.0)], lin(b2, b2n, -0.5, 64.0 * U))
+    bl_, bln = rows([(12, 1.0)], lin(b2, b2n, -0.5, 0.0))
+    ts("BI %s %s" % (b2n, bsn), "CB", T.CB[:, 0:12], T.BI[:, TR:TR + 12], b2, mul, bs_, add)
+    ts("BI %s %s" % (b2n, bln), "CBa", T.CB[:, 12:18], T.BI[:, TR + 12:TR + 18], b2, mul, bl_, add)
+    s7, s7n = lin(q7, "PF", 16.0, 13.0)
+    s8, s8n = lin(q8, "PF", 1.0, s7, s7n)
+    ts("COL " + s8n, "SEL", mh("SEL"), T.COL[:, 0:128], s8, eq)
+
+    for m, bk in enumerate(("P0", "P1", "P2", "PB", "PD", "PK")):
+        sl = slice(512 * m, 512 * m + 512)
+        mm("UI IB xsb%d B8" % (m // 3), bk, [(T[bk][:], mb("UI"), T.xsb[:, sl])]
+           + [(T[bk][:, TR * u:TR * u + TR], IB, T.B8[:]) for u in range(2)], last=False)
+        mm("SEL pqr", bk, [(T[bk][:], mh("SEL", (0, 16)), T.pqr[0:16, sl])], first=False)
+        for u in range(2):
+            c0 = 512 * m + TR * u
+            lin2(bk + " CB", "W%d" % (2 * m + u), T.W[:, c0:c0 + TR], T[bk][:, TR * u:TR * u + TR], None,
+                 T.CB[:, 2 * m + u:2 * m + u + 1])
+
+    ts("D3 PF", "FBT", T.FBT[:], T.D3[:], rc, eq)
+    tt("FBT D2", "FBT", T.FBT[:], T.FBT[:], T.D2[:], mul)
+    ts("GV PF", "S12", mh("S12"), T.GV[:], gc, eq)
+    tt("IB S12", "EH0", T.EH[:, 0:128], IB, mh("S12"), sub)
+    lin2("S12 OH EH0", "S12", mh("S12"), mh("S12"), T.OH[:, 12:13])
+    ts("GW PF", "EH1", T.EH[:, 128:328], T.GW[:], gc, eq)
+    lin2("CL", "CLH", T.CLH[0:1, :], T.CL[0:1, :])
+    ms("BIG", T.BIG[0:1, :], 0.0)
+    ms("BIG", T.BIG[0:1, 24:200:25], 2.0 ** 55)
+    ms("BIGR", mb("BIGR", (0, 1)), 2.0 ** 55)
+    lo_, lon = lin(xg, "PF", 25.0, -0.46875)
+    spc, spcn = rows([(11, -1.0)], lin(T.OH[:, 12:13], "OH", 1.0, 64.0 * U))
+    rq, rqn = lin(rc, "PF", 1.0, -0.25)
+    for h in range(2):
+        lin2("IB " + rqn, "C17%d" % h, T.C17[:, 128 * h:128 * h + 128], IB, rq)
+        lin2("IB TI", "DG%d" % h, T.DG[:, 128 * h:128 * h + 128], IB, sm("TI", h, h + 1))
+    ms("C96", T.C96[0:1, :], -96.0 * U)
+    l13, l13n = test(rc, 13.0, lt, 256.0)
+    LS_ = [lin(l13, l13n, pp, 0.0, ppn) for pp, ppn in ((npar, nparn), (par, "PF"))]
+
+    def weights(nm, spec, prev=None):
+        c, n = rows(spec, prev)
+        lin2("BLK " + n, nm, wh(nm), BLK, c)
+
+    w12, w12n = test(rc, 12.0, lt, 1.0)
+    weights("Wc", [(12, 1536.0)], lin(T.PH[:, 1:2], "PH1", w12, 0.0, w12n))
+    weights("Wp", [(13, 1.0)])
+    weights("Wh", [(13, 1.0), (14, -1.0)])
+    weights("Wn", [(13, -1.0), (12, -512.0)])
+    weights("We", [(14, 5.0 / 512), (12, 1280.0)])
+    weights("Wf", [(14, 5.0), (12, 2560.0)])
+    lin2("IB OH", "S1", mh("S1"), IB, T.OH[:, 13:14])
+    p1, p1n = lin(pc, "PF", 1.0, 1.0)
+    ts("COL OH " + p1n, "S2", mh("S2"), T.COL[:, 0:128], p1, eq, T.OH[:, 13:14], mul)
+    lin2("ONE", "O8", mh("O8"), ONE, 8.0)
+    for h in range(2):
+        lin2("ONE TI", "DB%d" % h, sm("DB", 8 * h, 8 * h + 8), T.MB[:, 0:8], sm("TI", h, h + 1), -3328.0)
+        ts("limb", "L0%d" % h, sh("L0", 8 * h, 8 * h + 8), T.limb[:, 0:16:2], -1.0, mul)
+        ts("limb", "SL%d" % h, sm("SL", 8 * h, 8 * h + 8), T.limb[:, 1:16:2], 32.0, mul, 32.0, add)
+    ts("SL0 SL1", "SL0 SL1", sm("SL"), sm("SL"), CAP, mn)
+    lin2("DB0 DB1", "TX", sm("TX"), sm("DB"), BIG)
+    lin2("DB0 DB1", "DB0 DB1", sm("DB"), sm("DB"), -1.0, -3328.0 - B - 1)
+    lin2("J16", "DM", sm("DM"), sh("J16"), None, float(WD))
+    z7, z7n = lin(q7, "PF", 16.0, 15.0)
+    ts("COL PF " + z7n, "ZB", T.ZB[:], T.COL[:, 0:144], z7, eq, q8, mul)
+    g15, g15n = lin(gc, "PF", 1.0, 15.0)
+    ts("COL OH " + g15n, "ZH", T.ZH[:], T.COL[:, 0:144], g15, eq, T.OH[:, 0:1], mul)
+    kb, kbn = lin(rc, "PF", float(B), -16.0 * B)
+    ts("COL %s %s" % (g15n, kbn), "ZK", T.ZK[:], T.COL[:, 0:144], g15, eq, kb, mul)
+    ms("C3K", T.C3K[0:1, :], float(V))
+    lin2("COL PF", "SLI0", T.SLI[:, 0:192], T.COL[:, 0:192], 16.0, rc)
+    r192, r192n = lin(rc, "PF", 192.0, 0.0)
+    lin2("COL " + r192n, "SLI1", T.SLI[:, 192:384], T.COL[:, 0:192], None, r192)
+    x8, x8n = lin(xg, "PF", 1.0, 8.0)
+    for h, (c, cn) in enumerate(((xg, "PF"), (x8, x8n))):
+        ts("D3 " + cn, "MASK2" if h else "MASK2a", T.MASK2[:, 128 * h:128 * h + 128], T.D3[:, 0:128], c, eq)
+    lin2("OH", "OHH", sh("OHH"), T.OH[:], -1.0)
+
+    mm("ZB pqr", "PE", [(T.PE[:, 256:448], T.ZB[0:16, 15 - r:143 - r], T.pqr[0:16, r:V:16]) for r in range(16)])
+    cp("PE", "HEL", T.HEL[:], T.PE[:, 256:448])
+    for u in range(6):
+        sl = slice(512 * u, 512 * u + 512)
+        tt("sb0 HEL IOS", "KM%d" % u, T.KM[:, sl], T.sb3[:, 0:B].indirect(T.HEL[:, 32 * u:32 * u + 32]), T.IOS[:, sl], eq, "g")
+
+    def home_places():
+        mm("ZK KM ZB pqr", "P2", [(T.P2[:, 256:448], T.ZK[:, 15 - r:143 - r], T.KM[:, r:V:16]) for r in range(16)]
+           + [(T.P2[:, 256:448], T.ZB[0:16, 15 - r:143 - r], T.pqr[0:16, r:V:16]) for r in range(16)])
+        ts("P2", "HS", T.HS[:], T.P2[:, 256:448], 16.0 * B, add)
 
     def fld(n, bk="PA"):
-        return T[bk][:, 256 + 16 * n:272 + 16 * n]
+        return T[bk][:, 16 * n:16 * n + 16]
 
-    def fields(R, spec, bk="PA"):
-        groups = []
-        for n, parts in spec:
-            for h in range(2):
-                o = T[bk][:, 256 + 16 * n + 8 * h:264 + 16 * n + 8 * h]
-                groups.append([(o, src[:, 128 * h:128 * h + 128], w) for src, w in parts])
-        mms(R, bk, groups)
-
-    rot = [0]
-
-    def bank():
-        rot[0] += 1
-        return "P%d" % (rot[0] % 3)
-
-    def pairs(gq, L, ln, rhs, rn_, ina, bn, cn, onv, bk=None):
-        bk = bk or bank()
-        a, u = 32 * (gq // 2), gq % 2
-        groups = []
-        for h, (c0, n) in enumerate(((0, 128), (128, 256))):
-            it = [(T[bk][:, c0:c0 + n], L[u][a:a + 32, 128 * h:128 * h + 128], rhs[a:a + 32, 0:n])]
-            if ina:
-                it.append((T[bk][:, c0:c0 + n], T.BG[a:a + 32, 128 * u:128 * u + 128], T.INA[a:a + 32, 0:n]))
-            groups.append(it)
-        mms("%s%d %s" % (ln, u, rn_) + (" INA BG0 BG1" if ina else ""), bk, groups)
-        for h, (c0, n) in enumerate(((0, 128), (128, 256))):
-            k = 8 * h + gq
-            o, src = sm(cn, k, k + 1), T[bk][:, c0:c0 + n]
-            if onv:
-                op([way("v", plain(n), lambda o=o, src=src: g.vector.tensor_reduce(o, src, AxisListType.X, mn))], bk, "%s%d" % (cn, k))
+    def field(n, bk, parts, whole=()):
+        its = [(fld(n, bk), l, r) for l, r in whole]
+        out = [] if not its else [its]
+        for h in range(2):
+            half = [(T[bk][:, 16 * n + 8 * h:16 * n + 8 * h + 8], src[:, 128 * h:128 * h + 128], w) for src, w in parts]
+            if its:
+                its += half
             else:
-                act(bk + " " + bn, "%s%d JNK%d" % (cn, k, k), T.JNK[:, B * gq + c0:B * gq + c0 + n], src, ACT.Relu,
-                    bias=sm(bn, k, k + 1), scale=-1.0, accum_out=o)
-        if onv:
-            both = "%s%d %s%d" % (cn, gq, cn, gq + 8)
-            tt(bn + " " + both, both, sm(cn, gq, 16, 8), sm(bn, gq, 16, 8), sm(cn, gq, 16, 8), sub)
+                out.append(half)
+        return out
 
-    def turn(src, sn, dst, dn, bk="PD"):
-        mms(sn + " IH", bk, [[(T[bk][:, 128 * h:128 * h + 128], src[:, h, :], T.IH[:])] for h in range(2)])
-        lin2(bk, dn, dst[:], T[bk][:, 0:TR])
+    def cf(k):
+        return (mf("O2K", (0, 1)), T.CF[0:1, 16 * k:16 * k + 16])
 
-    def slot(buf, k, lo=0):
-        return buf[:, :, 32 * k + lo:32 * k + lo + 8]
-
-    LB, LE = (T.LB0, T.LB1), (T.LE0, T.LE1)
+    LE = (T.LE0, T.LE1)
     best, best2 = T.PM[:, 15:TR:16], T.PM2[:, 15:TR:16]
-    j16 = (T.PE[:, 0:16], T.IH[:], T.J16[:])
 
     for t in range(S):
         last = t == S - 1
-        Z, zn = T.zin[:, t, :], "zin%d" % t
-        BI, bn_ = T.bin[:, t, :], "bin%d" % t
-        win, wn = (T.W[:, LG:WD], "Ws") if t == 0 else (T.XE[:], "XE")
-        cp("sbt " + bn_, "OFF", T.OFF[:], T.sbt[:].indirect(BI), "g")
-        mms(zn + " IB", "PD", [[(T.PD[:, 128 * h:128 * h + 128], T.zin[:, t, 128 * h:128 * h + 128], T.IB[:])] for h in range(2)])
-        lin2("PD", "ZT", T.ZT[:], T.PD[:, 0:TR], None, -64.0)
-        tt("FBT C1 " + bn_, "FX", T.FX[:], T.FBT[:].indirect(BI), T.C1[:], add, "g")
-        ts("JH " + bn_, "VK", T.VK[:], T.JH[:, 0:B].indirect(BI), 4096.0, lt, ind="g")
-        ts(zn, "INA", T.INA[:], Z, 64.0, ge)
-        if last:
-            lin2("JH", "CF", T.CF[:], T.JH[:, 0:B], None, 1.0)
-            ts("JH", "CG", T.CG[:], T.JH[:, 0:B], 4096.0, lt)
-            tt("CF CG", "JH", T.JH[:, 0:B], T.CF[:], T.CG[:], mul)
-        lin2("JH " + bn_, "JK", T.JK[:], T.JH[:, 0:B].indirect(BI), ind="g")
-        for u in range(2):
-            lin2("FX " + LS[u][2], "LB%d" % u, LB[u][:], T.FX[:], LS[u][0], LS[u][1])
-        items = [(T.PK[:, 0:TR], T.ONE[:], T.C17[:])]
-        for h in range(2):
-            o = T.PK[:, 128 * h:128 * h + 128]
-            items += [(o, T.VK[:, 128 * h:128 * h + 128], T.I17[:]), (o, T.INA[:, 128 * h:128 * h + 128], T.B17[:])]
-            if h in ABSH:
-                items.append((o, T.ONE[:], T.C384[:]))
-        mm("ONE C17 C17b C384 VK INA I17 B17", "PK", items, last=False)
-        fields("FX INA W8I WF0 WF2", [(0, [(T.FX, wf(0)), (T.INA, W8I)]), (1, [(T.FX, wf(2))])])
-        lin2("PA", "BB", sm("BB"), fld(0))
-        lin2("PA", "a", sm("a"), fld(1))
-
-        def dpass(h, src, sn, wt, fin):
-            mm(sn + " W8P W8N W8A", "PK", [(T.PK[:, 128 * h + k:128 * h + 128:16], src[:, 2048 * h + k:2048 * h + 2048:16], wt)
-                                           for k in range(16)], first=False, last=fin)
-
-        for c in range(8):
-            sl = slice(512 * c, 512 * c + 512)
-            h, a, bk = c // 4, 32 * (c % 4), bank()
-            lin2("OFF " + wn, "G%d" % c, T.G[:, sl], win.indirect(T.OFF[:, 32 * c:32 * c + 32]), ind="g")
-            mm("ZT E32", bk, [(T[bk][:], T.ZT[a:a + 32, 128 * h:128 * h + 128], T.E32[a:a + 32, :])])
-            tt("G%d %s" % (c, bk), "DP%d" % c, T.DP[:, sl], T.G[:, sl], T[bk][:], sub)
-            if h in ABSH:
-                act("DP%d" % c, "RL%d" % c, T.RL[:, sl], T.DP[:, sl], ACT.Abs, bias=-192.0)
-            else:
-                ts("DP%d" % c, "RL%d" % c, T.RL[:, sl], T.DP[:, sl], 192.0, mx)
-            if c % 4 == 3:
-                if h not in ABSH:
-                    dpass(h, T.DP, " ".join("DP%d" % x for x in range(c - 3, c + 1)), W8N, False)
-                dpass(h, T.RL, " ".join("RL%d" % x for x in range(c - 3, c + 1)), W8A if h in ABSH else W8P, h == 1)
-        for gq in range(8):
-            pairs(gq, LB, "LB", T.FX, "FX", True, "BB", "cb", False, BOXB[gq])
-        scan("RST PK", "PM", T.PM[:], T.RST[:], T.PK[:, 0:TR], mx, mn)
-        ts("PM", "K1", si("K1"), best, 65551, band)
-        ts("K1", "TP0", slot(T.TP, 0), si("K1"), 4096.0, mn)
-        turn(T.TP, "TP", T.T2, "T2")
-        to_list("T2 IH J16", T.T2, 0, 8, "PE", 0, j16)
-        ts("PE", "OE", su("OE"), T.PE[:, 0:16], 4096.0, mn)
-        tt("G OE C1", "GE", T.GE[:], T.G[:].indirect(su("OE")), T.C1[:], add, "g")
-        lin2("GE", "XA", T.XA[:], T.GE[:])
-        tt("GE XA", "FE", T.FE[:], T.GE[:], T.XA[:], sub)
+        Z, zn = T.zin[:, TR * t:TR * t + TR], "zin%d" % t
+        BL, B2, ln_ = T.lin[:, 32 * t:32 * t + 16], T.lin[:, 32 * t + 16:32 * t + 32], "lin%d" % t
+        st, stn = T.stin[:, 48 * t + 16:48 * t + 32], "stin%d" % t
+        win, wn = (T.W[:, 0:V], "Ws") if t == 0 else (T.XE[:], "XE")
+        cp("sb3 sb3a pin%d" % t, "OT", T.OT[:], T.sb3[:].indirect(B2), "g")
+        op([way("v", plain(TR), lambda: g.vector.transpose(T.OU[:], T.OT[:]))], "OT", "OU")
+        cp("OU PERM", "OFF", T.OFF[:], T.OU[:].indirect(su("PERM")), "g")
+        if t:
+            ts(zn, "INA", T.INA[:], Z, 64.0 * U, ge)
+            mm("NIB N64 INA " + zn, "PD", [(T.PD[:, 0:TR], mb("NIB"), Z), (T.PD[:, 0:TR], mb("N64"), T.INA[:])])
+            lin2("PD " + spcn, "DP16", T.DP[:, 4096:4352], T.PD[:, 0:TR], None, spc)
+        else:
+            lin2(zn + " " + spcn, "DP16", T.DP[:, 4096:4352], Z, -1.0, spc)
+        relu2("JH " + ln_, "JK", T.JK[:], T.JH[:, 0:BW].indirect(BL), NONE, "g")
+        mm("ONE C170 C171 JK I4", "PK", [(T.PK[:, 0:TR], ONE, T.C17[:])]
+           + [(T.PK[:, 128 * h:128 * h + 128], T.JK[:, 128 * h:128 * h + 128], mf("I4")) for h in range(2)], last=False)
+        for k in range(16):
+            tt("OFF %s %s" % (zn, wn), "DP%d ~DP" % k, T.DP[:, TR * k:TR * k + TR], win.indirect(T.OFF[:, 16 * k:16 * k + 16]), Z, sub, "g")
+        for lo, hi in ((0, 2), (2, 4), (4, 6), (6, 8), (8, 10), (10, 12), (12, 14), (14, 15), (15, 16)):
+            act(many("DP", hi, lo), many("RL", hi, lo) + " ~RL", T.RL[:, TR * lo:TR * hi], T.DP[:, TR * lo:TR * hi], ACT.Abs, bias=-64.0 * U)
+            mm(many("RL", hi, lo) + " W8A", "PK",
+               [(T.PK[:, 128 * h + k:128 * h + 128:16], T.RL[:, TR * k + 128 * h:TR * k + 128 * h + 128], w8("W8A"))
+                for k in range(lo, hi) for h in range(2)], first=False, last=hi == 16)
+        if t:
+            ts(stn, "a", si("a"), st, 511, band)
+            ts("a", "af", sm("af"), si("a"), -511.0, add)
+        if not last:
+            po = T.lout[:, 32 * t + 16:32 * t + 32]
+            pair_lists(po, "pout%d" % t)
+            send("pout%d" % t, "pin%d" % (t + 1), T.lin[:, 32 * t + 48:32 * t + 64], po, "ap%d" % t)
+        lin2("FBT " + ln_, "FX", T.FX[:], T.FBT[:].indirect(BL), ind="g")
+        ts("%s %s" % (ln_, lon), "LO", su("LO"), BL, 0.0625, mul, lo_, add)
+        for h, bk in enumerate(("P0", "P1")):
+            mm("FX EH0 EH1 ONEH CLH", bk, [(T[bk][:, 0:328], T.FX[:, 128 * h:128 * h + 128], T.EH[:]),
+                                           (T[bk][:, 128:328], mh("ONEH", (0, 1)), T.CLH[0:1, :])])
+            ts(bk + " PH2", "H%d" % h, T.H[:, 328 * h:328 * h + 328], T[bk][:, 0:328], 0.0, eq, T.PH[:, 2 + h:3 + h], mul)
+        mm("H0 H1 BIG BIGR", "P0", [(T.P0[:, 0:200], mb("BIGR", (0, 1)), T.BIG[0:1, :])]
+           + [(T.P0[:, 0:200], T.H[:, 328 * h:328 * h + 128], T.H[:, 328 * h + 128:328 * h + 328]) for h in range(2)])
+        lin2("P0", "MS", T.MS[:], T.P0[:, 0:200])
+        tt("MS LO FX", "LK", T.LK[:], T.MS[:].indirect(su("LO")), T.FX[:], mul, "g")
+        mms("LK BLK", "P1", field(0, "P1", [(T.LK, BLK)]))
+        tt("P1 THB", "nsw", sm("nsw"), fld(0, "P1"), sm("THB"), ge)
+        tt("nsw DB0 DB1", "ob", sm("ob"), sm("nsw"), sm("DB"), mul)
+        tt("ob af", "ob", sm("ob"), sm("ob"), sm("af"), mn)
+        as_list("ob", "SO", sm("ob"), 64, "MN", bk="P2")
+        cp("P2", "OB", su("OB"), T.P2[:, 64:80])
+        ts(stn, "q", sm("q"), st, BIG - 1 - 512 * (t + 2), le, -float(B), mul)
+        tt("q af", "sq%d" % t, T.stin[:, 48 * t:48 * t + 16], sm("q"), sm("af"), mn)
+        scan("RST PK", "PM", T.PM[:], T.RST[:, 0:TR], T.PK[:, 0:TR], mx, mn)
+        ts("PM", "K1", si("K1"), best, 31, band)
+        as_list("K1", "SK", si("K1"), 0, "M256", "J16")
+        cp("PE", "OE", su("OE"), T.PE[:, 0:16])
+        lin2("DP OE", "XD", T.XD[:], T.DP[:].indirect(su("OE")), ind="g")
+        tt("DP OE XD", "FE", T.FE[:], T.DP[:].indirect(su("OE")), T.XD[:], sub, "g")
         tt("PK PM", "M2", T.M2[:, 1:TR], T.PK[:, 1:TR], T.PM[:, 0:TR - 1], mx)
-        ms("M2", T.M2[:, 0:TR:16], CAP)
-        scan("RST M2", "PM2", T.PM2[:], T.RST[:], T.M2[:], mx, mn)
-        ts("PM2", "K2", si("K2"), best2, 65551, band)
-        ts("K2", "TQ0", slot(T.TQ, 0), si("K2"), 4096.0, mn)
-        turn(T.TQ, "TQ", T.T3, "T3")
-        to_list("T3 IH J16", T.T3, 0, 8, "PE", 0, j16)
-        ts("PE", "OF", su("OF"), T.PE[:, 0:16], 4096.0, mn)
-        lin2("G OF", "GF", T.GF[:], T.G[:].indirect(su("OF")), ind="g")
-        lin2("GF", "XB", T.XB[:], T.GF[:])
-        tt("GF XB", "FF", T.FF[:], T.GF[:], T.XB[:], sub)
-        mm("IB NIB XA XB", "PE", [(T.PE[:, TR:], T.IB[:], T.XA[:]), (T.PE[:, TR:], T.NIB[:], T.XB[:])])
-        act("PE", "AB", T.AB[:], T.PE[:, TR:], ACT.Abs)
+        scan("RST M2", "PM2", T.PM2[:, 1:TR], T.RST[:, 16:TR + 15], T.M2[:, 1:TR], mx, mn)
+        ts("PM2", "K2", si("K2"), best2, 31, band)
+        as_list("K2", "SF", si("K2"), 16, "M256", "J16")
+        cp("PE", "OF", su("OF"), T.PE[:, 16:32])
+        lin2("DP OF", "XF", T.XF[:], T.DP[:].indirect(su("OF")), ind="g")
+        tt("DP OF XF", "FF", T.FF[:], T.DP[:].indirect(su("OF")), T.XF[:], sub, "g")
+        mm("IB NIB XD XF", "PD", [(T.PD[:, TR:], IB, T.XD[:]), (T.PD[:, TR:], mb("NIB"), T.XF[:])])
+        act("PD", "AB", T.AB[:], T.PD[:, TR:], ACT.Abs, scale=1.0 / U)
         for u in range(2):
-            lin2("FE " + LS[u][2], "LE%d" % u, LE[u][:], T.FE[:], LS[u][0], LS[u][1])
-        fields("FE WF0", [(2, [(T.FE, wf(0))])])
-        lin2("PA", "BE", sm("BE"), fld(2))
-        fields("FE FX WF1 WF2 WF3 WF4 WF5", [(4, [(T.FE, wf(3)), (T.FX, wf(2))]), (5, [(T.FE, wf(4)), (T.FX, wf(2))]),
-                                             (6, [(T.FE, wf(5))]), (3, [(T.FE, wf(1))])])
+            lin2("FE " + LS_[u][1], "LE%d" % u, LE[u][:], T.FE[:], LS_[u][0])
+        ts("K1", "tx", sm("tx"), si("K1"), 16.0, ge, 4096.0 * BIG, mul)
+        tt("tx TX", "tx", sm("tx"), sm("tx"), sm("TX"), add)
         for gq in range(8):
-            pairs(gq, LE, "LE", T.FE, "FE", False, "BE", "ce", gq in VG, "P%d" % (gq % 2))
-        mms("IB NIB N64 XA INA " + zn, "PB",
-            [[(T.PB[:, 0:TR], T.IB[:], Z), (T.PB[:, 0:TR], T.NIB[:], T.XA[:]), (T.PB[:, 0:TR], T.N64[:], T.INA[:])],
-             [(T.PB[:, TR:], T.IB[:], Z), (T.PB[:, TR:], T.IB[:], T.XA[:])]])
-        act("PB", "AA", T.AA[:], T.PB[:, 0:TR], ACT.Abs, bias=128.0)
-        lin2("PB", "BV", T.BV[:], T.PB[:, TR:], 0.5, 63.75)
-        ts("PA", "e1", sm("e1"), fld(4), 0.0, eq)
-        lin2("PA", "TP1", slot(T.TP, 0, 8), fld(6))
-        lin2("PA", "c", sm("c"), fld(3))
-        tt("PA e1", "e1", sm("e1"), sm("e1"), fld(5), mul)
-        tt("PA e1", "e1", sm("e1"), sm("e1"), fld(4), add)
-        tt("a e1", "TP2", slot(T.TP, 2), sm("a"), sm("e1"), sub)
-        ts("ce", "TP0", slot(T.TP, 0), sm("ce"), 0.0, gt)
-        tt("TP0 e1", "TP3", slot(T.TP, 2, 8), slot(T.TP, 0), sm("e1"), mul)
-        tt("ce DW0 DW1", "cd", sm("cd"), sm("ce"), sm("DW"), mn)
-        tt("c cd", "cd", sm("cd"), sm("cd"), sm("c"), mx)
-        lin2("cd", "TP4", slot(T.TP, 1), sm("cd"))
-        tt("cd TP4", "TP5", slot(T.TP, 1, 8), sm("cd"), slot(T.TP, 1), sub)
-        turn(T.TP, "TP", T.T2, "T2")
-        to_list("T2", T.T2, 32, 16, "PD", 256)
-        cp("PD", "CU", su("CU"), T.PD[:, 256:272])
-        mm("T2 EZ IB BV", "PB", [(T.PB[:, 0:TR], T.IB[:], T.BV[:]), (T.PB[:, 0:TR], T.EZ[0:16, :], T.T2[0:16, :])])
-        to_list("T2", T.T2, 64, 16, "PE", 0, None, last)
-        zo, zon = T.zout[:, t, :], "zout%d" % t
+            bk, a, u = ("P0", "P1", "PB")[gq % 3], 32 * (gq // 2), gq % 2
+            blocks = ((0, 128), (128, 256))
+            mms("FE ONE RW0 LE%d" % u, bk, [[(T[bk][:, c0:c0 + n], mb("ONE", (a, a + 1)), T.RW[a:a + 1, 0:n]),
+                                             (T[bk][:, c0:c0 + n], LE[u][a:a + 32, 128 * h:128 * h + 128], T.FE[a:a + 32, 0:n])]
+                                            for h, (c0, n) in enumerate(blocks)])
+            for h, (c0, n) in enumerate(blocks):
+                k = 8 * h + gq
+                o, src = sm("ce", k, k + 1), T[bk][:, c0:c0 + n]
+                act(bk + " tx", "ce%d JNK%d ~ce" % (k, k), T.JNK[:, B * gq + c0:B * gq + c0 + n], src, ACT.Relu,
+                    bias=sm("tx", k, k + 1), scale=BIG, accum_out=o)
+        mms("FE Wp O2K NI af CF0", "PA", field(0, "PA", [(T.FE, wh("Wp"))], [cf(0), (mf("NI"), sm("af"))]))
+        mms("FE Wh", "PA", field(1, "PA", [(T.FE, wh("Wh"))]))
+        mms("FE Wn O2K CF%d" % (5 + t), "PA", field(2, "PA", [(T.FE, wh("Wn"))], [cf(5 + t)]))
+        mms("FE Wc O2K CF3", "PA", field(3, "PA", [(T.FE, wh("Wc"))], [cf(3)]))
+        ts("PA", "e1", sm("e1"), fld(0), 0.0, eq)
+        tt("PA e1", "e1", sm("e1"), sm("e1"), fld(1), mul)
+        tt("PA e1", "Y1", T.Y3[:, 16:32], sm("e1"), fld(2), add)
+        lin2("PA", "Y2", T.Y3[:, 32:48], fld(3))
+        act("XD", "AA", T.AA[:], T.XD[:], ACT.Abs, bias=-64.0 * U)
+        lin2("XD", "HB", T.HB[:], T.XD[:], 0.5, 127.75 * U)
+        mm("IB HB ONE C96 " + zn, "PB", [(T.PB[:, 0:TR], IB, Z), (T.PB[:, 0:TR], IB, T.HB[:]),
+                                         (T.PB[:, 0:TR], mb("ONE", (0, 1)), T.C96[0:1, :])], last=False)
+        ces = sm("ce").indirect(su("SPR"))
+        op([act_way(T.LS[:], ces, ACT.Sign, "g", {}), ts_way(T.LS[:], ces, 0.0, gt, None, None, "g")], "ce SPR", "LS")
+        tt("ce SP3 Y0 Y1 Y2", "T3", T.T3[:], sm("ce").indirect(sm("SP3", 0, 3, pool="SU")), T.Y3[:], add, "g")
+        son = "stout%d" % t
+        tt("T3 sq%d sx%d %s" % (t, t, stn), son, T.stout[:, 48 * t:48 * t + 48], T.T3[:], T.stin[:, 48 * t:48 * t + 48], mn)
+        lv, so, cd = [T.stout[:, 48 * t + 16 * k:48 * t + 16 * k + 16] for k in range(3)]
+        mm("LS N512", "PB", [(T.PB[:, 128 * h:128 * h + 128], T.LS[:, 128 * h:128 * h + 128], mb("N512")) for h in range(2)], first=False)
+        zo, zon = T.zout[:, TR * t:TR * t + TR], "zout%d" % t
         tt("PB AA", zon, zo, T.PB[:, 0:TR], T.AA[:], mx)
         if last:
-            cp(zon, "ZI", T.ZI[:], zo)
-            ts("ZI", "ZI", T.ZI[:], T.ZI[:], 63, band)
-            cp("ZI", zon, zo, T.ZI[:])
-            lin2("PE", "bfo", T.bfo[:], T.PE[:, 0:16])
-            send("bfo", "bfi", T.bfi[:], T.bfo[:], "ab%d" % t)
+            ts(zon, "INA", T.INA[:], zo, 64.0 * U, ge, -64.0 * U, mul)
+            mm("IU INA " + zon, "PB", [(T.PB[:, 0:TR], mb("IU"), zo), (T.PB[:, 0:TR], mb("IU"), T.INA[:])])
+            lin2("PB", zon, zo, T.PB[:, 0:TR])
         else:
-            cp("PE", "bout%d" % t, T.bout[:, t, :], T.PE[:, 0:16])
-            send("bout%d" % t, "bin%d" % (t + 1), T.bin[:, t + 1, :], T.bout[:, t, :], "ab%d" % t)
-        send(zon, "zin%d" % (t + 1), T.zin[:, t + 1, :], zo, "az%d" % t)
-
-        fields("FE FF FX AB BLK WF6 WF7 WF8 WF9",
-               [(7, [(T.FE, wf(6)), (T.FF, wf(7)), (T.FX, wf(8)), (T.FX, wf(9))]), (8, [(T.AB, BLK)])], "PK")
-        tt("PM SL0 SL1", "sp", sm("sp"), best, sm("SL"), ge)
-        lin2("sp", "sp", sm("sp"), sm("sp"), HELD)
-        tt("cb DB", "ad", sm("ad"), sm("cb"), sm("DB"), mn)
-        tt("a ad", "TQ1", slot(T.TQ, 1), sm("a"), sm("ad"), mx)
-        tt("cb sp", "m", sm("m"), sm("cb"), sm("sp"), mx)
-        jl, jln = (sm("L0"), "L00 L01") if t == 0 else (sm("JL"), "JL")
-        tt("PK " + jln, "j3", sm("j3"), fld(8, "PK"), jl, ge)
-        tt("j3 m", "m", sm("m"), sm("m"), sm("j3"), mx)
-        tt("PK m", "j", sm("j"), sm("m"), fld(7, "PK"), eq)
-        tt("j PM2", "j3", sm("j3"), sm("j"), best2, mul)
-        tt("j3 sp", "TZ", T.TZ[:, 0:TR:16], sm("j3"), sm("sp"), mx)
-        for h in range(2):
-            k = 2 * t + h
-            lin2("j VC VL", "TQ%d" % (2 + h), T.TQ[:, h, 64:72], sm("j", 8 * h, 8 * h + 8),
-                 sm("VL" if last else "VC", k, k + 1), 0.0 if last else NONE)
-        lin2("j", "TQ4", slot(T.TQ, 3), sm("j"))
-        scan("KEEP TZ", "TH", T.TH[:], T.KEEP[:], T.TZ[:], mul, add)
-        tt("PK TH", "SE", T.SE[:], T.PK[:, 0:TR], T.TH[:], le)
-        if t == 0:
-            homes(1)
-        turn(T.TQ, "TQ", T.T3, "T3", "P2")
-        mms("T3 EX SE IB", "P2", [[(T.P2[:, 0:TR], T.EX[64:72, :], T.T3[64:72, :])]]
-            + [[(T.P2[:, TR + 128 * h:TR + 128 * h + 128], T.SE[:, 128 * h:128 * h + 128], T.IB[:])] for h in range(2)])
-        to_list("T3", T.T3, 32, 8, "PK", 0)
-        tt("P2 JK", "W1", T.W1[:], T.P2[:, 0:TR], T.JK[:], sub)
-        tt("P2 W1", "W2", T.W2[:], T.P2[:, TR:], T.W1[:], mul)
-        cp("PK", "OB", su("OB"), T.PK[:, 0:16])
-        tt("W2 JK OB JH", "JH", T.JH[:].indirect(su("OB")), T.W2[:], T.JK[:], add, "s")
-        pv, pvn = (T.PV1, "PV1") if t == 1 else (T.PV0, "PV0")
-        half = [(T.P1[:, TR:], T.HIB[:], x[:]) for x in (T.XA, T.XB, T.AB)]
+            as_list(son, "SN", lv, 32, "MN")
+            cp("PE", "lout%d" % t, T.lout[:, 32 * t:32 * t + 16], T.PE[:, 32:48])
+            send("lout%d" % t, "lin%d" % (t + 1), T.lin[:, 32 * t + 32:32 * t + 48], T.lout[:, 32 * t:32 * t + 16], "al%d" % t)
+        send(zon, "zin%d" % (t + 1), T.zin[:, TR * t + TR:TR * t + 2 * TR], zo, "az%d" % t)
         if last:
-            mm("HIB XA XB AB", "P1", half)
-            lin2("P1", "NL", T.NL[:], T.P1[:, TR:], None, -128.0)
+            ts(son, "a", si("a"), so, 511, band)
+            spread("a MASK2a", "SN", T.SN, si("a"), "MASK2")
+            mm("SN OHH", "PE", [(T.PE[:, 32:48], T.SN[:, 128 * h:128 * h + 128], sh("OHH")) for h in range(2)])
+            lin2("PE", "bfo", T.bfo[:], T.PE[:, 32:48], None, 511.0)
+            send("bfo", "bfi", T.bfi[:], T.bfo[:], "as%d" % t)
         else:
-            mms("IB INJ HIB XA XB AB B0 S1 S2 FE FF " + zn, "P1",
-                [[(T.P1[:, 0:TR], T.IB[:], Z), (T.P1[:, 0:TR], T.INJ[:], T.FE[:])],
-                 half + [(T.P1[:, TR:], T.IB[:], T.B0[:, 0:TR]), (T.P1[:, TR:], T.S1[:], T.FE[:]), (T.P1[:, TR:], T.S2[:], T.FF[:])]])
-            lin2("P1", pvn, pv[:], T.P1[:, 0:TR])
-            lin2("P1 CBa", "NL", T.NL[:], T.P1[:, TR:], None, T.CB[:, t:t + 1])
-        mm("T3 EX", "P0", [(T.P0[:, 0:TR], T.EX[96:104, :], T.T3[96:104, :])])
+            send(son, "stin%d" % (t + 1), T.stin[:, 48 * t + 64:48 * t + 80], so, "as%d" % t)
+        spread(son, "SC", T.SC, cd)
+        to_list("SC", 64, T.W8F[:], "BLKF", bk="PA")
+        cp("PA", "CU", su("CU"), T.PA[:, 64:80])
+        if t == 1:
+            ts("PA", "UT", sm("UT"), T.PA[:, 64:80], float(V), lt)
+            tt("UT DM", "UT", sm("UT"), sm("UT"), sm("DM"), mul)
+            tt("UT PA", "UT", sm("UT"), sm("UT"), T.PA[:, 64:80], mx)
+            cp("UT", "UL", su("UL"), sm("UT"))
+
+        tt("PM SL0 SL1", "sp", sm("sp"), best, sm("SL"), ge)
+        mms("FE FF We Wf O2K CF4 NI3 af I4 nsw sp", "P2",
+            field(0, "P2", [(T.FE, wh("We")), (T.FF, wh("Wf"))],
+                  [cf(4), (mf("NI3"), sm("af")), (mf("I4"), sm("nsw")), (mf("I4"), sm("sp"))]))
+        mms("AB BLK IH L00 L01", "PD", field(1, "PD", [(T.AB, BLK)], [(mh("IH"), sh("L0"))]))
+        lin2("sp", "sh", sm("sh"), sm("sp"), HELD)
+        tt("sh PM2", "sh", sm("sh"), sm("sh"), best2, mx)
+        lin2("sh SPR", "TH", T.TH[:], sm("sh").indirect(su("SPR")), ind="g")
+        tt("PK TH", "SE", T.SE[:], T.PK[:, 0:TR], T.TH[:], le)
+        if t:
+            tt("PD AM", "j3", sm("j3"), fld(1, "PD"), si("AM"), ge)
+        else:
+            ts("PD", "j3", sm("j3"), fld(1, "PD"), 0.0, ge)
+        jn = "j%d" % t
+        jt = sh(jn)
+        tt("P2 j3", jn, jt, sm("j3"), fld(0, "P2"), eq)
+        tt(jn + " sp", "sg", sm("sg"), jt, sm("sp"), sub)
+        tt("sg SPR SE", "UU", T.UU[:], sm("sg").indirect(su("SPR")), T.SE[:], mul, "g")
+        mms("UU DG0 DG1 IT%d" % t, "P2", [[(T.P2[:, 128 * h:128 * h + 128], T.UU[:, 128 * h:128 * h + 128], x)
+                                           for x in (T.DG[:, 128 * h:128 * h + 128], mb("IT%d" % t))] for h in range(2)])
+        lin2("P2", "X", T.X[:], T.P2[:, 0:TR], None, -NONE)
+        tt("X JK OB JH", "JH", T.JH[:].indirect(su("OB")), T.X[:], T.JK[:], add, "s")
+        dma("y", "JH", "JF", T.JF[0:128:16, 0:16 * B], T.JH[:, 0:B], 100000)
+        if t == 0:
+            home_places()
+        o = T.P0[:, 0:TR]
+        items = [(o, mf("B1K"), T.X[:]), (o, T.RW[0:1, 512:640], T.RW[0:1, 0:TR]),
+                 (o, T.RW[0:1, 640 + 128 * t:768 + 128 * t], T.RW[0:1, TR:2 * TR]),
+                 (o, mb("HIB"), T.XD[:]), (o, mb("HIB"), T.XF[:]), (o, mb("UH"), T.AB[:]), (o, IB, Z)]
+        rd = "B1K X RW HIB XD XF UH AB IB " + zn
 
         def pass1(u, n):
             sl = slice(n * u, n * u + n)
-            tt("JH HEL KM0 KM1 KM2 KM3 KM4 KM5", "R1%d" % u, T.R1[:, sl],
-               T.JH[:, 0:B].indirect(T.HEL[:, n // 16 * u:n // 16 * (u + 1)]), T.KM[:, sl], mul, "g")
+            lin2("JF HS", "R1%d" % u, T.R1[:, sl], T.JF[:].indirect(T.HS[:, n // 16 * u:n // 16 * (u + 1)]), ind="g")
 
         if last:
+            mm(rd, "P0", items)
+            act("P0", "YL", T.YL[:], o, ACT.Relu, scale=1.0 / U, bias=-64.0)
+            dma("y", "YL", "", T.yx[:, WD - TR:WD], T.YL[:], 65536)
+            op([("g", 300.0, 8000.0, lambda: g.dma_start(T.YO[:, 0:V], T.W[:, 0:V]), "d")], "Ws", "YO0 YO1 YO2")
             for u in range(3):
-                for x in range(3):
-                    sl = slice(1536 * u + 512 * x, 1536 * u + 512 * x + 512)
-                    nm = "Y%d%d" % (u, x)
-                    act("W", nm, T.YO[:, sl], T.W[:, sl], ACT.Abs)
-                    op([ts_way(T.YO[:, sl], T.YO[:, sl], -128.0, add, 0.0, mx, None),
-                        act_way(T.YO[:, sl], T.YO[:, sl], ACT.Relu, None, {"bias": -128.0})], nm, nm)
-            ally = " ".join("Y%d%d" % (u, x) for u in range(3) for x in range(3))
-            tt("P0 NL Y02", "Y02", T.YO[:, TR * t:TR * t + TR], T.P0[:, 0:TR], T.NL[:], mul)
-            cp("YOd CU %s %s" % (ally, zn), ally, T.YO[:].indirect(su("CU")), Z, "s")
-            dma("y", ally, "", T.yx[:, 0:V], T.YO[:, LG:WD], 800000)
-            dma("y", ally, "", T.yx[:, V:WD], T.YO[:, 0:LG], 1200000)
+                sl = slice(1024 * u, 1024 * u + 1024)
+                lin2("YO%d" % u, "YO%d" % u, T.YO[:, sl], T.YO[:, sl], 1.0 / U, -64.0)
+            for u in range(2):
+                sl = slice(V + 640 * u, V + 640 * u + 640)
+                act("Wl", "YO%d" % (3 + u), T.YO[:, sl], T.W[:, sl], ACT.Abs, scale=1.0 / U)
+                relu2("YO%d" % (3 + u), "YO%d" % (3 + u), T.YO[:, sl], T.YO[:, sl], -64.0)
+            lin2(zn, "ZM", T.ZM[:], Z, 1.0 / U)
+            cp("YO CU ZM", "YO", T.YO[:].indirect(su("CU")), T.ZM[:], "s")
+            dma("y", "YO", "", T.yx[:, 0:2176], T.YO[:, 0:2176], 600000)
+            dma("s", "YO", "", T.yx[:, 2176:WD - TR], T.YO[:, 2176:WD - TR], 1100000)
             for u in range(4):
                 pass1(u, 768)
-                mm("ZH R1%d" % u, "PB", [(T.PB[:, 0:192], T.ZH[:, 15 - r:143 - r], T.R1[:, 192 * r:192 * r + 192])
-                                         for r in range(4 * u, 4 * u + 4)], first=u == 0, last=u == 3)
-            ts("PB", "YT", T.YT[:], T.PB[:, 0:192], 4096.0, mul, float(V - 1), mn)
-            tt("PB YT", "YT", T.YT[:], T.PB[:, 0:192], T.YT[:], add)
-            tt("YT YJ", "YJ", T.YJ[:], T.YJ[:], T.YT[:], mx)
+                mm("ZH ONEH C3K R1%d" % u, "PB", ([(T.PB[:, 0:192], mh("ONEH", (0, 1)), T.C3K[0:1, :])] if u == 0 else [])
+                   + [(T.PB[:, 0:192], T.ZH[:, 15 - r:143 - r], T.R1[:, 192 * r:192 * r + 192]) for r in range(4 * u, 4 * u + 4)],
+                   first=u == 0, last=u == 3)
+            tt("PB SLI1", "YJ", T.YJ[:], T.PB[:, 0:192], T.SLI[:, 192:384], mx)
             dma("y", "YJ", "", T.yj[:], T.YJ[:], 98304)
             break
 
-        if t and DENSE:
-            for u in range(12):
-                sl = slice(LG + 256 * u, LG + 256 * u + 256)
-                act("W%d" % u, "W%d" % u, T.W[:, sl], T.W[:, sl], ACT.Abs)
-        tt("P0 NL", "Wl", T.W[:, TR * t:TR * t + TR], T.P0[:, 0:TR], T.NL[:], mul)
+        mm(rd, "P0", items[:3], last=False)
+        mm(rd, "P0", items[3:], first=False, last=False)
+        mm("IB B8 S1 S2 FE FF", "P0", [(o, IB, T.B8[:]), (o, mh("S1"), T.FE[:]), (o, mh("S2"), T.FF[:])], first=False)
+        relu2("P0 CBa", "Wl", T.W[:, V + TR * t:V + TR * t + TR], o, T.CB[:, 12 + t:13 + t])
+        pv, pvn = (T.PV1, "PV1") if t == 1 else (T.PV0, "PV0")
+        mms("IB IH FE S12 " + zn, "P1", [[(T.P1[:, 0:TR], IB, Z), (T.P1[:, 0:TR], mh("IH"), T.FE[:])]]
+            + ([[(T.P1[:, TR:], mh("S12"), T.FE[:])]] if t else []))
+        lin2("P1", pvn, pv[:], T.P1[:, 0:TR], -1.0, -64.0 * U)
+        if t:
+            lin2("P1", "SG", T.SG[:], T.P1[:, TR:])
         if t == 4:
-            ts("PV1 UL W", "W", T.W[:].indirect(su("UL")), T.PV1[:], 1.0, mul, 128.0, add, "s")
-        ts(pvn + " CU W", "W", T.W[:].indirect(su("CU")), pv[:], -1.0, mul, -128.0, add, "s")
-        for nm, cmp_, when in (("US", lt, () if DENSE else (1, 2, 3)), ("UL", ge, (1,))):
-            if t in when:
-                ts("PD", "UT", sm("UT"), T.PD[:, 256:272], float(LG), cmp_)
-                tt("UT DM", "UT", sm("UT"), sm("UT"), sm("DM"), mul)
-                tt("UT PD", "UT", sm("UT"), sm("UT"), T.PD[:, 256:272], mx)
-                cp("UT", nm, su(nm), sm("UT"))
-        for u, bk in enumerate(("P2", "PK", "P2")):
-            pass1(u, 1024)
-            sl = slice(64 * u, 64 * u + 64)
-            o = T[bk][:, 0:64]
-            mm("ZH IH HAS R1%d" % u, bk, [(o, T.IH[:], T.HAS[:, sl])]
-               + [(o, T.ZH[:, 15 - r:143 - r], T.R1[:, 1024 * u + r:1024 * u + 1024:16]) for r in range(16)])
-            tt(bk + " SLI", "JO%d" % u, T.JO[:, sl], o, T.SLI[:, sl], mn)
+            ts("PV1 UL W", "W", T.W[:].indirect(su("UL")), T.PV1[:], -1.0, mul, 0.0, add, "s")
+        cp(pvn + " CU W", "W", T.W[:].indirect(su("CU")), pv[:], "s")
+        for u, (bk, x0, x1) in enumerate(PARTS):
+            for x in range(x0, x1):
+                pass1(x, 512)
+            sl = slice(32 * x0, 32 * x1)
+            o = T[bk][:, 256:256 + 32 * (x1 - x0)]
+            mm("ZH ONEH C3K " + many("R1", x1, x0), bk, [(o, mh("ONEH", (0, 1)), T.C3K[0:1, sl])]
+               + [(o, T.ZH[:, 15 - r:143 - r], T.R1[:, 512 * x0 + r:512 * x1:16]) for r in range(16)])
+            tt(bk + " SLI0", "JO%d" % u, T.JO[:, sl], o, T.SLI[:, sl], mx)
             cp("JO%d" % u, "JU%d" % u, T.JU[:, sl], T.JO[:, sl])
-            for x in range(2 * u, 2 * u + 2):
+            for x in range(x0, x1):
                 lin2("W JU%d" % u, "XE%d" % x, T.XE[:, 512 * x:512 * x + 512],
                      T.W[:, 0:WD].indirect(T.JU[:, 32 * x:32 * x + 32]), ind="g")
-        if t < 4 and not DENSE:
-            us = "US" if t else "CU"
-            ts("%s %s W" % (pvn, us), "W", T.W[:].indirect(su(us)), pv[:], 1.0, mul, 128.0, add, "s")
-        mms("O8 TQ4", "PA", [[(T.PA[:, 400 + 8 * u:408 + 8 * u], T.O8[:], T.TQ[:, h, 96:104]) for h in range(2)] for u in range(2)])
-        tt("PA AI", "AI", si("AI"), fld(9), si("AI"), add)
-        ts("AI", "AM", si("AM"), si("AI"), 248, band)
-        tt("AM L00 L01", "JL", sm("JL"), si("AM"), sm("L0"), add)
+        if t:
+            tt(pvn + " SG CU W", "W", T.W[:].indirect(su("CU")), pv[:], T.SG[:], mul, "s")
+        else:
+            ts(pvn + " CU W", "W", T.W[:].indirect(su("CU")), pv[:], -1.0, mul, 0.0, add, "s")
+        mms("O8 " + many("j", t + 1), "PA",
+            [[(T.PA[:, 96 + 8 * u:104 + 8 * u], mh("O8"), sh("j%d" % x, 8 * h, 8 * h + 8)) for x in range(t + 1) for h in range(2)]
+             for u in range(2)])
+        cp("PA", "AM", si("AM"), T.PA[:, 96:112])
+        ts("AM", "AM", si("AM"), si("AM"), 248, band)
 
     dma("y", "bfi", "", T.yb[:], T.bfi[:])
-    dma("y", "zin6", "", T.yz[:], T.zin[:, S, :], 65536)
+    dma("y", "zin6", "", T.yz[:], T.zin[:, S * TR:S * TR + TR], 65536)
 
     count, seen, token, nd = {}, {}, {}, 0
     for n, (q, c0, c1, fn, kind), deps in put_in_order(ops):
         want = {}
         for d in deps:
             sem, val = token[d]
-            if not (q == "p" and sem == "sp"):
+            if sem != own.get(q) or (q != "p" and (d, n) not in PLACED["soft"]):
                 want[sem] = max(want.get(sem, 0), val)
         for sem, val in want.items():
             if seen.get((q, sem), 0) < val:

@@ -10,6 +10,7 @@ BW = 392
 BIG = 8192.0
 CYC, GAT, SCA, FIX, PEC, PEF, LAT, DMA, HOP = 1.04, 1.3, 3.15, 60.0, 0.52, 15.0, 80.0, 2200.0, 3300.0
 ROUNDS, SEED = 8000, 1
+ROWS = ((0, 2), (2, 4), (4, 6), (6, 8), (8, 10), (10, 12), (12, 14), (14, 15), (15, 16))
 PARTS = (("P2", 0, 2), ("PK", 2, 4), ("P2", 4, 6))
 PLACED = {}
 
@@ -19,24 +20,24 @@ for _n, _c, _d in [
     ("xsb", V, BF), ("sb3", 3 * BW, I32), ("pq", 384, I32), ("pqh", 384, F16), ("pqr", V, F16),
     ("bxi", TR, I32), ("bxh", TR, F16), ("limi", 16, I32), ("limb", 16, I32),
     ("W", WD + TR, F32), ("XE", V, F32), ("DP", 17 * TR, F32), ("RL", 4096, BF),
-    ("R1", V, F16), ("KM", V, F16), ("IOS", V, I32), ("HEL", 192, U16), ("HS", 192, U16), ("C3K", 192, F16), ("SLI", 384, F32),
+    ("R1", V, F16), ("KM", V, F16), ("IOS", V, I32), ("HEL", 192, U16), ("HS", 192, U16), ("C3K", 192, BF), ("SLI", 384, F32),
     ("JF", 17 * B, F32), ("ZK", 144, F16),
     ("JO", 192, F32), ("JU", 192, U16), ("JH", 648, F32), ("YO", WD + TR, BF), ("YL", TR, BF), ("YJ", 192, F32),
     ("COL", TR, F32), ("D3", 400, F32), ("D2", 400, F32), ("FBT", 400, F32), ("GV", 128, F32), ("GW", 200, F32),
     ("PI", 8, I32), ("PF", 8, F32), ("PC", 96, F32), ("PH", 16, BF), ("OH", 16, F32),
-    ("MB", 128 * 17, BF), ("MH", 128 * 14, F16), ("EG", 1024, F16), ("GW8", 1024, BF), ("D8", 128, BF), ("MF", 128 * 5, F32), ("W8", 48, BF), ("W8H", 96, F16), ("W8F", 8, F32),
+    ("MB", 128 * 18, BF), ("MH", 128 * 16, F16), ("EG", 240, F16), ("sbf", 3 * BW, F32), ("D8", 128, BF), ("MF", 128 * 5, F32), ("W8", 48, BF), ("W8H", 96, F16), ("W8F", 8, F32),
     ("ZH", 144, F16), ("ZB", 144, F16), ("EH", 328, F16), ("CL", 200, F32), ("CLH", 200, F16), ("BIG", 200, BF),
-    ("RW", 1408, BF), ("CF", 16 * 12, F32), ("C17", TR, BF), ("C1", TR, BF), ("C96", TR, BF), ("DG", TR, BF),
-    ("RST", TR + 16, F32), ("KEEP", TR, F32), ("MASK", TR, BF), ("MASK2", TR, BF), ("BI", 288, I32), ("BC", 288, F32),
+    ("RW", 1408, BF), ("CF", 16 * 7, F32), ("CH", 16 * 7, F16), ("C17", TR, BF), ("DG", TR, BF), ("HH", 384, F16), ("ZA", 144, F16),
+    ("RST", TR + 16, F32), ("MASK", TR, BF), ("MASK2", TR, BF), ("BI", 288, I32), ("BC", 288, F32),
     ("B8", TR, BF), ("CB", 32, F32),
-    ("OT", TR, I32), ("OU", TR, I32), ("OFF", TR, U16), ("INA", TR, BF), ("ZC", TR, F32), ("JK", TR, F32), ("FX", TR, F16),
+    ("OT", TR, F32), ("OU", TR, F32), ("OFF", TR, U16), ("INA", TR, BF), ("JK", TR, F32), ("FX", TR, F16),
     ("H", 656, BF), ("MS", 200, F32), ("LK", TR, BF), ("PM", TR, I32), ("M2", TR, F32), ("PM2", TR, I32),
     ("SK", TR, F16), ("SF", TR, F16), ("SN", TR, F16), ("SO", TR, F16), ("SC", TR, F32), ("LS", TR, BF),
     ("XD", TR, BF), ("XF", TR, BF), ("FE", TR, F16), ("FF", TR, F16), ("LE0", TR, F16), ("LE1", TR, F16),
-    ("JNK", 8 * B, BF), ("AA", TR, BF), ("HB", TR, BF), ("AB", TR, BF), ("TZ", TR, F32), ("TH", TR, F32),
+    ("JNK", 8 * B, BF), ("AA", TR, BF), ("HB", TR, BF), ("AB", TR, BF), ("TH", TR, F32),
     ("SE", TR, BF), ("UU", TR, BF), ("X", TR, F32), ("PV0", TR, F32), ("PV1", TR, F32), ("SG", TR, F32), ("ZM", TR, BF),
-    ("SM", 16 * 40, F32), ("SI", 16 * 8, I32), ("SU", 16 * 10, U16), ("SH", 16 * 12, F16),
-    ("zin", (S + 1) * TR, BF), ("zout", S * TR, BF), ("lin", S * 32, U16), ("lout", S * 32, U16),
+    ("SM", 16 * 40, F32), ("SI", 16 * 8, I32), ("SU", 16 * 10, U16), ("SH", 16 * 16, F16),
+    ("zin", (2 * S + 1) * TR, BF), ("zout", S * TR, BF), ("lin", S * 32, U16), ("lout", S * 32, U16),
     ("stin", S * 48, I32), ("stout", S * 48, I32), ("Y3", 48, F32), ("T3", 48, F32), ("bfi", 16, F32), ("bfo", 16, F32),
 ]:
     SCRATCH[_n] = ("sbuf", [128, _c], _d)
@@ -45,7 +46,7 @@ for _n in BANKS:
     SCRATCH[_n] = ("psum", [128, 512], F32)
 
 SEMAPHORES = (["sv", "ss", "sp", "sg", "sent"] + ["d%d" % k for k in range(40)]
-              + ["a%s%d" % (x, k) for x in "zlsp" for k in range(S)])
+              + ["a%s%d" % (x, k) for x in "zylsp" for k in range(S)])
 
 
 def many(x, n, lo=0):
@@ -66,7 +67,7 @@ def put_in_order(ops):
     soft = PLACED.setdefault("soft", set())
     for n, (ways, R, Wr) in enumerate(ops):
         d = set()
-        fed = {wrote[r] for r in R + Wr if r in wrote and r[0] != "~"}
+        fed = {wrote[r] for r in R + Wr if r in wrote and r[0] != "~"} | {x for r in Wr for x in read.get(r, ())}
         for r in R:
             if r in wrote:
                 d.add(wrote[r])
@@ -358,7 +359,7 @@ def rank_program(g, core, T, topo):
     dma("y", "", "zraw ZM", T.ZM[:], T.zs[:], 65536)
     dma("y", "", "limi", T.limi[0:1, :], T.lim[:])
     for k in range(3):
-        ms("sb%d" % (5 + k), T.sb3[:, BW * k + B:BW * k + BW], 0)
+        iota("sb%d" % (5 + k), T.sb3[:, BW * k + B:BW * k + BW], [[0, BW - B]], 0, 0, False)
 
     iota("PI0", T.PI[:, 0:1], [[0, 1]], 0, 1, False)
     iota("COL", T.COL[:], [[1, TR]], 0, 0)
@@ -366,10 +367,9 @@ def rank_program(g, core, T, topo):
     iota("ONE", mb("ONE"), [[0, 128]], 1, 0)
     iota("D3", T.D3[:], [[0, 25], [1, 16]], 0, 0)
     iota("D8", T.D8[:], [[0, 16], [1, 8]], 0, 0)
-    iota("GW8", T.GW8[:], [[-16, 8], [1, 128]], 0, 0)
-    for k, c in ((0, 192), (3, 3583.5), (4, 192.0 * (5.0 + 5.0 / 512) + 3840.0)):
-        iota("CF%d" % k, T.CF[0:1, 16 * k:16 * k + 16], [[0, 16]], int(8 * c), 0)
-    iota(many("CF", 5 + S, 5), T.CF[0:1, 80:80 + 16 * S], [[-4096, S], [0, 16]], int(8 * (BIG - 1 - 192 - 512 * 3)), 0)
+    iota("CF0", T.CF[0:1, 0:16], [[0, 16]], 1536, 0)
+    iota("CF1", T.CF[0:1, 16:16 + 16 * S], [[-512, S], [0, 16]], int(BIG - 1 - 191 - 512 * 3), 0)
+    lin2("CF0 CF1", "CH", T.CH[0:1, :], T.CF[0:1, :])
     iota("D2", T.D2[:], [[1, 25], [0, 16]], 1024, 0)
     iota("BC1", T.BC[:, TR:TR + 12], [[256, 12]], 0, 0)
     iota("BC2", T.BC[:, TR + 12:TR + 32], [[256, 20]], 0, 0)
@@ -381,16 +381,17 @@ def rank_program(g, core, T, topo):
     for k in range(1, 4):
         dma("y", "JF0", "JF%d" % k, T.JF[:, 1632 * k:1632 * k + 1632], T.JF[:, 0:1632], 840000 * k)
     iota("RST", T.RST[:], [[0, TR + 16]], 0, 0)
-    iota("IOS", T.IOS[:], [[1, V]], 0, 0, False)
+    iota("RST", T.RST[:, 0:TR + 16:16], [[0, 17]], int(CAP), 0)
+    iota("JH", T.JH[:, B:B + 1], [[0, 1]], 0, 0)
+    iota("Y0", T.Y3[:, 0:16], [[0, 16]], -B, 0)
+    iota("C3K", T.C3K[0:1, :], [[0, 192]], V, 0)
+    iota("BIG", T.BIG[0:1, :], [[0, 200]], 0, 0)
+    for u in range(6):
+        iota("IOS%d" % u, T.IOS[:, 512 * u:512 * u + 512], [[1, 512]], 512 * u, 0, False)
     iota("RW0", T.RW[:, 0:TR], [[-1, TR]], 0, 0)
-    iota("RW1", T.RW[0:1, TR:2 * TR], [[0, TR]], 256, 0)
-    iota("RW2", T.RW[0:1, 512:640], [[0, 128]], 2048, 0)
+    iota("RW1", T.RW[0:1, TR:2 * TR], [[0, TR]], 512, 0)
+    iota("RW2", T.RW[0:1, 512:640], [[0, 128]], 4096, 0)
     iota("RW3", T.RW[0:1, 640:1408], [[-2048, S], [0, 128]], 224 * 2048, 0)
-    iota("Wl", T.W[:, V:WD], [[0, WD - V]], 0, 0)
-    iota("Wd", T.W[:, WD:WD + TR], [[0, TR]], 0, 0)
-    iota("YOd", T.YO[:, WD - TR:WD + TR], [[0, 2 * TR]], 0, 0)
-    ms("JH", T.JH[:, B:B + 1], 0.0)
-    ms("RST", T.RST[:, 0:TR + 16:16], CAP)
     for k, (sh_, mk) in enumerate(((0, 15), (0, 112), (4, 7), (0, 7), (4, 1), (3, 1))):
         ts("PI0", "PI%d" % (k + 1), T.PI[:, k + 1:k + 2], T.PI[:, 0:1], sh_, shr, mk, band)
     cp(many("PI", 7), "PF", T.PF[:, 0:7], T.PI[:, 0:7])
@@ -424,17 +425,25 @@ def rank_program(g, core, T, topo):
 
     IB, ONE = mb("IB"), mb("ONE")
     ts("COL PF", "IB", IB, T.COL[:, 0:128], pc, eq)
-    for nm, w in (("UI", U), ("NIB", -1.0), ("N64", 64.0 * U), ("HIB", 0.5), ("UH", U / 2), ("N512", -512.0 * U),
-                  ("IU", 1.0 / U)):
-        lin2("IB", nm, mb(nm), IB, w)
+    def put_way(out, src, step, base, c):
+        return way("g", 170 + 2 * nel(out) * CYC,
+                   lambda: g.affine_select(out, src, [[step, nel(out)]], ALU.not_equal, float(c), base, 1))
+
+    def diag(nm, out, c):
+        op([put_way(out, mb("NIL"), -1, 0, c), act_way(out, IB, ACT.Identity, None, {"scale": c})], "NIL IB", nm)
+
+    iota("NIL", mb("NIL"), [[0, 128]], 0, 0)
+    lin2("IB", "UI", mb("UI"), IB, U)
+    for nm, w in (("NIB", -1.0), ("N64", 80.0 * U), ("HIB", 0.5), ("UH", U / 2), ("N512", -512.0 * U), ("IU", 1.0 / U)):
+        diag(nm, mb(nm), w)
     for t in range(S):
-        lin2("IB", "IT%d" % t, mb("IT%d" % t), IB, NONE + 256.0 * t)
+        diag("IT%d" % t, mb("IT%d" % t), NONE + 256.0 * t)
     lin2("IB", "IH", mh("IH"), IB)
     lin2("ONE", "ONEH", mh("ONEH"), ONE)
-    for nm, w in (("I4", 4.0), ("NI", 1.0), ("NI3", 5.0 + 5.0 / 512)):
-        lin2("IB", nm, mf(nm), IB, w)
-    ts("GV PF", "B1K", mf("B1K"), T.GV[:], gc, eq, 1024.0, mul)
-    lin2("ONE", "O2K", mf("O2K", (0, 1)), mb("ONE", (0, 1)), 0.125)
+    diag("I4", mf("I4"), 4.0)
+    diag("NI3", mh("NI3"), 2.0 + 1.0 / 512)
+    diag("I4K", mh("I4K"), 4096.0)
+    ts("GV PF", "B1K", mf("B1K"), T.GV[:], gc, eq, 2048.0, mul)
     ts("GV PF", "BLK", w8("BLK"), T.GV[:, 0:128:16], gc, eq)
     BLK = w8("BLK")
     lin2("BLK", "W8A", w8("W8A"), BLK, 32.0 / U)
@@ -447,8 +456,8 @@ def rank_program(g, core, T, topo):
     npar, nparn = lin(par, "PF", -1.0, 1.0)
     lin2("IB " + nparn, "P00", mh("P00"), IB, npar)
     lin2("IB PF", "P11", mh("P11"), IB, par)
-    up, upn = lin(pc, "PF", 1.0, 16.0)
-    dn, dnn = lin(pc, "PF", 1.0, -16.0)
+    iota("PX", T.PC[:, 92:95], [[16, 3]], -16, 1)
+    (up, upn), (dn, dnn) = (T.PC[:, 94:95], "PX"), (T.PC[:, 92:93], "PX")
     ts("COL %s %s" % (upn, nparn), "P10", mh("P10"), T.COL[:, 0:128], up, eq, npar, mul)
     ts("COL PF " + dnn, "P01", mh("P01"), T.COL[:, 0:128], dn, eq, par, mul)
     ts("ONE PF", "VO0", sh("VO", 0, 16, 2), T.MB[:, 0:8], par, mul, float(BW), mul)
@@ -468,9 +477,10 @@ def rank_program(g, core, T, topo):
         tt("%s SP8 %s" % (R, mask), sn, T[sn][:, 0:128], src.indirect(sm("SP8", 0, 8, pool="SU")), mh(mask), mul, "g")
         o = T[bk][:, c0:c0 + 16]
         mm("%s EG IH %s" % (sn, extra or ""), bk, ([(o, mh("IH"), sh(extra))] if extra else [])
-           + [(o, T.EG[:, 128 * q:128 * q + 128], T[sn][:, 16 * q:16 * q + 16]) for q in range(8)])
+           + [(o, T.EG[:, 112 - 16 * q:240 - 16 * q], T[sn][:, 16 * q:16 * q + 16]) for q in range(8)])
 
-    ts("GW8 PF", "EG", T.EG[:], T.GW8[:], rc, eq)
+    r112, r112n = lin(rc, "PF", 1.0, 112.0)
+    ts("COL " + r112n, "EG", T.EG[:], T.COL[:, 0:240], r112, eq)
     lin2("PI7 COL", "UT", sm("UT", 0, 8), T.COL[:, 0:8], None, T.PF[:, 7:8])
     cp("UT", "SP8", sm("SP8", 0, 8, pool="SU"), sm("UT", 0, 8))
     ts("D8 PF", "MN", mh("MN"), T.D8[:], xg, eq, -1.0, mul)
@@ -489,10 +499,10 @@ def rank_program(g, core, T, topo):
     lin2("PA", "af", sm("af"), T.PA[:, 0:16], -1.0)
     pair_lists(T.lin[:, 0:32], "lin0 pin0", True)
     lin2("zraw", "zin0", T.zin[:, 0:TR], T.ZM[:], U)
+    lin2("zraw", "yin0", T.zin[:, TR:2 * TR], T.ZM[:], U)
     ts("ONE PF", "SP3", su("SP3"), T.MB[:, 0:16], rc, mul)
     for t in range(S):
         iota("sx%d" % t, T.stin[:, 48 * t + 32:48 * t + 48], [[128, 2], [0, 8]], WD, 1, False)
-    ms("Y0", T.Y3[:, 0:16], -float(B))
 
     LN2 = 0.6931471805599453
     act("PF", "PH0", T.PH[:, 0:1], rc, ACT.Exp, scale=-LN2)
@@ -501,6 +511,7 @@ def rank_program(g, core, T, topo):
     act("TI", "PH2", T.PH[:, 2:4], sm("TI", 0, 2), ACT.Exp, scale=-0.4 * LN2, bias=51.2 * LN2)
     for h in range(2):
         ts("ONE PH2", "TB%d" % h, sm("THB", 8 * h, 8 * h + 8), T.MB[:, 0:8], T.PH[:, 2 + h:3 + h], mul, T.PH[:, 2 + h:3 + h], mul)
+    lin2("PH2", "WT", sm("WT", 0, 2), T.PH[:, 2:4])
     lin2("TB0 TB1", "THB", sm("THB"), sm("THB"), 2.57 * 1024)
     sr, srn = lin(T.PH[:, 0:1], "PH0", 1.0, 0.0)
     sb_, sbn = lin(T.PH[:, 0:1], "PH0", 0.5, -0.5)
@@ -512,7 +523,7 @@ def rank_program(g, core, T, topo):
     ts("BI %s %s" % (a2n, a1n), "B8", T.B8[:], T.BI[:, 0:TR], a2, mul, a1, add)
     b2, b2n = test(rc, 12.0, lt, 2.0)
     lin2("%s %s" % (b2n, a2n), b2n, b2, a2, -1.0, b2)
-    bs_, bsn = rows([(12, -1.0), (13, -192.0), (14, -192.0)], lin(b2, b2n, -0.5, 64.0 * U))
+    bs_, bsn = rows([(12, -1.0), (13, -191.0), (14, -191.0)], lin(b2, b2n, -0.5, 64.0 * U))
     bl_, bln = rows([(12, 1.0)], lin(b2, b2n, -0.5, 0.0))
     ts("BI %s %s" % (b2n, bsn), "CB", T.CB[:, 0:12], T.BI[:, TR:TR + 12], b2, mul, bs_, add)
     ts("BI %s %s" % (b2n, bln), "CBa", T.CB[:, 12:18], T.BI[:, TR + 12:TR + 18], b2, mul, bl_, add)
@@ -537,33 +548,35 @@ def rank_program(g, core, T, topo):
     lin2("S12 OH EH0", "S12", mh("S12"), mh("S12"), T.OH[:, 12:13])
     ts("GW PF", "EH1", T.EH[:, 128:328], T.GW[:], gc, eq)
     lin2("CL", "CLH", T.CLH[0:1, :], T.CL[0:1, :])
-    ms("BIG", T.BIG[0:1, :], 0.0)
-    ms("BIG", T.BIG[0:1, 24:200:25], 2.0 ** 55)
-    ms("BIGR", mb("BIGR", (0, 1)), 2.0 ** 55)
+    op([put_way(T.BIG[0:1, 24:200:25], sm("NIL", 0, 8, pool="MB", w=128, rows=(0, 1)), 0, 0, 2.0 ** 55)], "NIL", "BIG")
+    op([put_way(mb("BIGR", (0, 1)), mb("NIL", (0, 1)), 0, 0, 2.0 ** 55)], "NIL", "BIGR")
     lo_, lon = lin(xg, "PF", 25.0, -0.46875)
     spc, spcn = rows([(11, -1.0)], lin(T.OH[:, 12:13], "OH", 1.0, 64.0 * U))
+    sp8, sp8n = lin(spc, spcn, 1.0, 80.0 * U)
     rq, rqn = lin(rc, "PF", 1.0, -0.25)
     for h in range(2):
         lin2("IB " + rqn, "C17%d" % h, T.C17[:, 128 * h:128 * h + 128], IB, rq)
         lin2("IB TI", "DG%d" % h, T.DG[:, 128 * h:128 * h + 128], IB, sm("TI", h, h + 1))
-    ms("C96", T.C96[0:1, :], -96.0 * U)
     l13, l13n = test(rc, 13.0, lt, 256.0)
     LS_ = [lin(l13, l13n, pp, 0.0, ppn) for pp, ppn in ((npar, nparn), (par, "PF"))]
 
-    def weights(nm, spec, prev=None):
-        c, n = rows(spec, prev)
-        lin2("BLK " + n, nm, wh(nm), BLK, c)
+    def weights(nm, spec, made=False):
+        for r, w in spec:
+            op([put_way(wh(nm), wh(nm) if made else sm("NIL", 0, 8, pool="MB", w=128), -16, -r, w)], nm if made else "NIL", nm)
+            made = True
 
     w12, w12n = test(rc, 12.0, lt, 1.0)
-    weights("Wc", [(12, 1536.0)], lin(T.PH[:, 1:2], "PH1", w12, 0.0, w12n))
+    tt("PH1 " + w12n, w12n, w12, w12, T.PH[:, 1:2], mul)
+    lin2("BLK " + w12n, "Wc", wh("Wc"), BLK, w12)
+    weights("Wc", [(12, 1536.0)], True)
     weights("Wp", [(13, 1.0)])
     weights("Wh", [(13, 1.0), (14, -1.0)])
     weights("Wn", [(13, -1.0), (12, -512.0)])
-    weights("We", [(14, 5.0 / 512), (12, 1280.0)])
-    weights("Wf", [(14, 5.0), (12, 2560.0)])
-    lin2("IB OH", "S1", mh("S1"), IB, T.OH[:, 13:14])
-    p1, p1n = lin(pc, "PF", 1.0, 1.0)
-    ts("COL OH " + p1n, "S2", mh("S2"), T.COL[:, 0:128], p1, eq, T.OH[:, 13:14], mul)
+    weights("We", [(14, 1.0 / 512), (12, 512.0)])
+    weights("Wf", [(14, 2.0), (12, 1024.0)])
+    for nm, c in (("S1", 13), ("S2", 14)):
+        op([put_way(mh(nm), mb("NIL"), 0, 1, 0.0)], "NIL", nm)
+        op([put_way(sm(nm, c, 128, 16, "MH", 128), sm("NIL", 0, 8, pool="MB", w=128), -16, -13, 1.0)], "NIL", nm)
     lin2("ONE", "O8", mh("O8"), ONE, 8.0)
     for h in range(2):
         lin2("ONE TI", "DB%d" % h, sm("DB", 8 * h, 8 * h + 8), T.MB[:, 0:8], sm("TI", h, h + 1), -3328.0)
@@ -577,9 +590,9 @@ def rank_program(g, core, T, topo):
     ts("COL PF " + z7n, "ZB", T.ZB[:], T.COL[:, 0:144], z7, eq, q8, mul)
     g15, g15n = lin(gc, "PF", 1.0, 15.0)
     ts("COL OH " + g15n, "ZH", T.ZH[:], T.COL[:, 0:144], g15, eq, T.OH[:, 0:1], mul)
+    ts("COL " + g15n, "ZA", T.ZA[:], T.COL[:, 0:144], g15, eq)
     kb, kbn = lin(rc, "PF", float(B), -16.0 * B)
     ts("COL %s %s" % (g15n, kbn), "ZK", T.ZK[:], T.COL[:, 0:144], g15, eq, kb, mul)
-    ms("C3K", T.C3K[0:1, :], float(V))
     lin2("COL PF", "SLI0", T.SLI[:, 0:192], T.COL[:, 0:192], 16.0, rc)
     r192, r192n = lin(rc, "PF", 192.0, 0.0)
     lin2("COL " + r192n, "SLI1", T.SLI[:, 192:384], T.COL[:, 0:192], None, r192)
@@ -592,12 +605,21 @@ def rank_program(g, core, T, topo):
     cp("PE", "HEL", T.HEL[:], T.PE[:, 256:448])
     for u in range(6):
         sl = slice(512 * u, 512 * u + 512)
-        tt("sb0 HEL IOS", "KM%d" % u, T.KM[:, sl], T.sb3[:, 0:B].indirect(T.HEL[:, 32 * u:32 * u + 32]), T.IOS[:, sl], eq, "g")
+        tt("sb0 HEL IOS%d" % u, "KM%d" % u, T.KM[:, sl], T.sb3[:, 0:B].indirect(T.HEL[:, 32 * u:32 * u + 32]), T.IOS[:, sl], eq, "g")
 
     def home_places():
-        mm("ZK KM ZB pqr", "P2", [(T.P2[:, 256:448], T.ZK[:, 15 - r:143 - r], T.KM[:, r:V:16]) for r in range(16)]
-           + [(T.P2[:, 256:448], T.ZB[0:16, 15 - r:143 - r], T.pqr[0:16, r:V:16]) for r in range(16)])
-        ts("P2", "HS", T.HS[:], T.P2[:, 256:448], 16.0 * B, add)
+        cp("HEL", "HH0", T.HH[:, 0:192], T.HEL[:])
+        mm("IH HH0", "PE", [(T.PE[:, 256:448], mh("IH"), T.HH[:, 0:192])], last=False)
+        for q in range(4):
+            mm("ZK KM", "PE", [(T.PE[:, 256:448], T.ZK[:, 15 - r:143 - r], T.KM[:, r:V:16]) for r in range(4 * q, 4 * q + 4)],
+               first=False, last=q == 3)
+        ts("PE", "HS", T.HS[:], T.PE[:, 256:448], 16.0 * B, add)
+
+    def has_home():
+        mm("ZA KM", "PD", [(T.PD[:, 256:448], T.ZA[:, 15 - r:143 - r], T.KM[:, 192 * r:192 * r + 192]) for r in range(8)])
+        hb, hbn = test(rc, 8.0, ge, V + 1.0)
+        lin2(hbn, hbn, hb, hb, None, -1.0)
+        lin2("PD " + hbn, "HH1", T.HH[:, 192:384], T.PD[:, 256:448], V + 1.0, hb)
 
     def fld(n, bk="PA"):
         return T[bk][:, 16 * n:16 * n + 16]
@@ -614,32 +636,38 @@ def rank_program(g, core, T, topo):
         return out
 
     def cf(k):
-        return (mf("O2K", (0, 1)), T.CF[0:1, 16 * k:16 * k + 16])
+        return (mh("ONEH", (0, 1)), T.CH[0:1, 16 * k:16 * k + 16])
 
     LE = (T.LE0, T.LE1)
     best, best2 = T.PM[:, 15:TR:16], T.PM2[:, 15:TR:16]
 
     for t in range(S):
         last = t == S - 1
-        Z, zn = T.zin[:, TR * t:TR * t + TR], "zin%d" % t
+        Z, zn = T.zin[:, 2 * TR * t:2 * TR * t + TR], "zin%d" % t
         BL, B2, ln_ = T.lin[:, 32 * t:32 * t + 16], T.lin[:, 32 * t + 16:32 * t + 32], "lin%d" % t
         st, stn = T.stin[:, 48 * t + 16:48 * t + 32], "stin%d" % t
         win, wn = (T.W[:, 0:V], "Ws") if t == 0 else (T.XE[:], "XE")
-        cp("sb3 sb3a pin%d" % t, "OT", T.OT[:], T.sb3[:].indirect(B2), "g")
+        if t:
+            lin2("sbf0 sbf1 sbf2 pin%d" % t, "OT", T.OT[:], T.sbf[:].indirect(B2), ind="g")
+        else:
+            cp("sb3 sb3a pin0", "OT", T.OT[:], T.sb3[:].indirect(B2), "g")
+            for k in range(3):
+                act("sb3 sb3a", "sbf%d" % k, T.sbf[:, BW * k:BW * k + BW], T.sb3[:, BW * k:BW * k + BW], ACT.Copy)
         op([way("v", plain(TR), lambda: g.vector.transpose(T.OU[:], T.OT[:]))], "OT", "OU")
         cp("OU PERM", "OFF", T.OFF[:], T.OU[:].indirect(su("PERM")), "g")
         if t:
-            ts(zn, "INA", T.INA[:], Z, 64.0 * U, ge)
+            act(zn, "INA", T.INA[:], Z, ACT.Sign, bias=-100.0 * U)
             mm("NIB N64 INA " + zn, "PD", [(T.PD[:, 0:TR], mb("NIB"), Z), (T.PD[:, 0:TR], mb("N64"), T.INA[:])])
-            lin2("PD " + spcn, "DP16", T.DP[:, 4096:4352], T.PD[:, 0:TR], None, spc)
+            lin2("PD " + sp8n, "DP16", T.DP[:, 4096:4352], T.PD[:, 0:TR], None, sp8)
         else:
             lin2(zn + " " + spcn, "DP16", T.DP[:, 4096:4352], Z, -1.0, spc)
         relu2("JH " + ln_, "JK", T.JK[:], T.JH[:, 0:BW].indirect(BL), NONE, "g")
         mm("ONE C170 C171 JK I4", "PK", [(T.PK[:, 0:TR], ONE, T.C17[:])]
            + [(T.PK[:, 128 * h:128 * h + 128], T.JK[:, 128 * h:128 * h + 128], mf("I4")) for h in range(2)], last=False)
-        for k in range(16):
-            tt("OFF %s %s" % (zn, wn), "DP%d ~DP" % k, T.DP[:, TR * k:TR * k + TR], win.indirect(T.OFF[:, 16 * k:16 * k + 16]), Z, sub, "g")
-        for lo, hi in ((0, 2), (2, 4), (4, 6), (6, 8), (8, 10), (10, 12), (12, 14), (14, 15), (15, 16)):
+        for lo, hi in ROWS:
+            tt("OFF %s %s%s" % (zn, wn, " yin%d" % t if hi > lo + 1 else ""), many("DP", hi, lo) + " ~DP", T.DP[:, TR * lo:TR * hi],
+               win.indirect(T.OFF[:, 16 * lo:16 * hi]), T.zin[:, 2 * TR * t:2 * TR * t + TR * (hi - lo)], sub, "g")
+        for lo, hi in ROWS:
             act(many("DP", hi, lo), many("RL", hi, lo) + " ~RL", T.RL[:, TR * lo:TR * hi], T.DP[:, TR * lo:TR * hi], ACT.Abs, bias=-64.0 * U)
             mm(many("RL", hi, lo) + " W8A", "PK",
                [(T.PK[:, 128 * h + k:128 * h + 128:16], T.RL[:, TR * k + 128 * h:TR * k + 128 * h + 128], w8("W8A"))
@@ -656,14 +684,19 @@ def rank_program(g, core, T, topo):
         for h, bk in enumerate(("P0", "P1")):
             mm("FX EH0 EH1 ONEH CLH", bk, [(T[bk][:, 0:328], T.FX[:, 128 * h:128 * h + 128], T.EH[:]),
                                            (T[bk][:, 128:328], mh("ONEH", (0, 1)), T.CLH[0:1, :])])
-            ts(bk + " PH2", "H%d" % h, T.H[:, 328 * h:328 * h + 328], T[bk][:, 0:328], 0.0, eq, T.PH[:, 2 + h:3 + h], mul)
-        mm("H0 H1 BIG BIGR", "P0", [(T.P0[:, 0:200], mb("BIGR", (0, 1)), T.BIG[0:1, :])]
+            w_ = sm("WT", h, h + 1)
+            ts(bk + " WT", "H%d" % h, T.H[:, 328 * h + 128:328 * h + 328], T[bk][:, 128:328], 0.0, eq, w_, mul)
+            o, src = T.H[:, 328 * h:328 * h + 128], T[bk][:, 0:128]
+            op([act_way(o, src, ACT.Relu, None, {"scale": w_, "bias": w_}), ts_way(o, src, 0.0, eq, w_, mul, None)],
+               bk + " WT", "G%d" % h)
+        mm("H0 H1 G0 G1 BIG BIGR", "P0", [(T.P0[:, 0:200], mb("BIGR", (0, 1)), T.BIG[0:1, :])]
            + [(T.P0[:, 0:200], T.H[:, 328 * h:328 * h + 128], T.H[:, 328 * h + 128:328 * h + 328]) for h in range(2)])
         lin2("P0", "MS", T.MS[:], T.P0[:, 0:200])
         tt("MS LO FX", "LK", T.LK[:], T.MS[:].indirect(su("LO")), T.FX[:], mul, "g")
         mms("LK BLK", "P1", field(0, "P1", [(T.LK, BLK)]))
-        tt("P1 THB", "nsw", sm("nsw"), fld(0, "P1"), sm("THB"), ge)
-        tt("nsw DB0 DB1", "ob", sm("ob"), sm("nsw"), sm("DB"), mul)
+        tt("P1 THB", "nsw", sh("nsw"), fld(0, "P1"), sm("THB"), ge)
+        lin2("af", "ah", sh("ah"), sm("af"), None, 191.0)
+        tt("nsw DB0 DB1", "ob", sm("ob"), sh("nsw"), sm("DB"), mul)
         tt("ob af", "ob", sm("ob"), sm("ob"), sm("af"), mn)
         as_list("ob", "SO", sm("ob"), 64, "MN", bk="P2")
         cp("P2", "OB", su("OB"), T.P2[:, 64:80])
@@ -691,26 +724,24 @@ def rank_program(g, core, T, topo):
         for gq in range(8):
             bk, a, u = ("P0", "P1", "PB")[gq % 3], 32 * (gq // 2), gq % 2
             blocks = ((0, 128), (128, 256))
-            mms("FE ONE RW0 LE%d" % u, bk, [[(T[bk][:, c0:c0 + n], mb("ONE", (a, a + 1)), T.RW[a:a + 1, 0:n]),
-                                             (T[bk][:, c0:c0 + n], LE[u][a:a + 32, 128 * h:128 * h + 128], T.FE[a:a + 32, 0:n])]
-                                            for h, (c0, n) in enumerate(blocks)])
+            mms("FE ONE RW0 LE%d" % u, bk,
+                [[(T[bk][:, c0:c0 + n], LE[u][a:a + 32, 128 * h:128 * h + 128], T.FE[a:a + 32, 0:n]),
+                  (T[bk][:, 256 * h:256 * h + 128], mb("ONE", (a, a + 1)), T.RW[a:a + 1, 128 * h:128 * h + 128])]
+                 for h, (c0, n) in enumerate(blocks)])
             for h, (c0, n) in enumerate(blocks):
                 k = 8 * h + gq
                 o, src = sm("ce", k, k + 1), T[bk][:, c0:c0 + n]
                 act(bk + " tx", "ce%d JNK%d ~ce" % (k, k), T.JNK[:, B * gq + c0:B * gq + c0 + n], src, ACT.Relu,
                     bias=sm("tx", k, k + 1), scale=BIG, accum_out=o)
-        mms("FE Wp O2K NI af CF0", "PA", field(0, "PA", [(T.FE, wh("Wp"))], [cf(0), (mf("NI"), sm("af"))]))
-        mms("FE Wh", "PA", field(1, "PA", [(T.FE, wh("Wh"))]))
-        mms("FE Wn O2K CF%d" % (5 + t), "PA", field(2, "PA", [(T.FE, wh("Wn"))], [cf(5 + t)]))
-        mms("FE Wc O2K CF3", "PA", field(3, "PA", [(T.FE, wh("Wc"))], [cf(3)]))
+        mms("FE Wp IH ah Wh", "PA", field(0, "PA", [(T.FE, wh("Wp"))], [(mh("IH"), sh("ah"))]) + field(1, "PA", [(T.FE, wh("Wh"))]))
+        mms("FE Wn ONEH CH Wc", "PA", field(2, "PA", [(T.FE, wh("Wn"))], [cf(1 + t)]) + field(3, "PA", [(T.FE, wh("Wc"))]))
         ts("PA", "e1", sm("e1"), fld(0), 0.0, eq)
         tt("PA e1", "e1", sm("e1"), sm("e1"), fld(1), mul)
         tt("PA e1", "Y1", T.Y3[:, 16:32], sm("e1"), fld(2), add)
-        lin2("PA", "Y2", T.Y3[:, 32:48], fld(3))
+        lin2("PA", "Y2", T.Y3[:, 32:48], fld(3), None, 3583.5)
         act("XD", "AA", T.AA[:], T.XD[:], ACT.Abs, bias=-64.0 * U)
         lin2("XD", "HB", T.HB[:], T.XD[:], 0.5, 127.75 * U)
-        mm("IB HB ONE C96 " + zn, "PB", [(T.PB[:, 0:TR], IB, Z), (T.PB[:, 0:TR], IB, T.HB[:]),
-                                         (T.PB[:, 0:TR], mb("ONE", (0, 1)), T.C96[0:1, :])], last=False)
+        mm("IB HB " + zn, "PB", [(T.PB[:, 0:TR], IB, Z), (T.PB[:, 0:TR], IB, T.HB[:])], last=False)
         ces = sm("ce").indirect(su("SPR"))
         op([act_way(T.LS[:], ces, ACT.Sign, "g", {}), ts_way(T.LS[:], ces, 0.0, gt, None, None, "g")], "ce SPR", "LS")
         tt("ce SP3 Y0 Y1 Y2", "T3", T.T3[:], sm("ce").indirect(sm("SP3", 0, 3, pool="SU")), T.Y3[:], add, "g")
@@ -721,14 +752,17 @@ def rank_program(g, core, T, topo):
         zo, zon = T.zout[:, TR * t:TR * t + TR], "zout%d" % t
         tt("PB AA", zon, zo, T.PB[:, 0:TR], T.AA[:], mx)
         if last:
-            ts(zon, "INA", T.INA[:], zo, 64.0 * U, ge, -64.0 * U, mul)
+            ts(zon, "INA", T.INA[:], zo, 64.0 * U, ge, -160.0 * U, mul)
             mm("IU INA " + zon, "PB", [(T.PB[:, 0:TR], mb("IU"), zo), (T.PB[:, 0:TR], mb("IU"), T.INA[:])])
             lin2("PB", zon, zo, T.PB[:, 0:TR])
         else:
             as_list(son, "SN", lv, 32, "MN")
             cp("PE", "lout%d" % t, T.lout[:, 32 * t:32 * t + 16], T.PE[:, 32:48])
             send("lout%d" % t, "lin%d" % (t + 1), T.lin[:, 32 * t + 32:32 * t + 48], T.lout[:, 32 * t:32 * t + 16], "al%d" % t)
-        send(zon, "zin%d" % (t + 1), T.zin[:, TR * t + TR:TR * t + 2 * TR], zo, "az%d" % t)
+        z1 = 2 * TR * (t + 1)
+        send(zon, "zin%d" % (t + 1), T.zin[:, z1:z1 + TR], zo, "az%d" % t)
+        if not last:
+            send(zon, "yin%d" % (t + 1), T.zin[:, z1 + TR:z1 + 2 * TR], zo, "ay%d" % t)
         if last:
             ts(son, "a", si("a"), so, 511, band)
             spread("a MASK2a", "SN", T.SN, si("a"), "MASK2")
@@ -746,12 +780,12 @@ def rank_program(g, core, T, topo):
             tt("UT PA", "UT", sm("UT"), sm("UT"), T.PA[:, 64:80], mx)
             cp("UT", "UL", su("UL"), sm("UT"))
 
-        tt("PM SL0 SL1", "sp", sm("sp"), best, sm("SL"), ge)
-        mms("FE FF We Wf O2K CF4 NI3 af I4 nsw sp", "P2",
+        tt("PM SL0 SL1", "sp", sh("sp"), best, sm("SL"), ge)
+        mms("FE FF We Wf ONEH CH NI3 ah I4K nsw sp", "P2",
             field(0, "P2", [(T.FE, wh("We")), (T.FF, wh("Wf"))],
-                  [cf(4), (mf("NI3"), sm("af")), (mf("I4"), sm("nsw")), (mf("I4"), sm("sp"))]))
+                  [cf(0), (mh("NI3"), sh("ah")), (mh("I4K"), sh("nsw")), (mh("I4K"), sh("sp"))]))
         mms("AB BLK IH L00 L01", "PD", field(1, "PD", [(T.AB, BLK)], [(mh("IH"), sh("L0"))]))
-        lin2("sp", "sh", sm("sh"), sm("sp"), HELD)
+        lin2("sp", "sh", sm("sh"), sh("sp"), HELD)
         tt("sh PM2", "sh", sm("sh"), sm("sh"), best2, mx)
         lin2("sh SPR", "TH", T.TH[:], sm("sh").indirect(su("SPR")), ind="g")
         tt("PK TH", "SE", T.SE[:], T.PK[:, 0:TR], T.TH[:], le)
@@ -762,7 +796,7 @@ def rank_program(g, core, T, topo):
         jn = "j%d" % t
         jt = sh(jn)
         tt("P2 j3", jn, jt, sm("j3"), fld(0, "P2"), eq)
-        tt(jn + " sp", "sg", sm("sg"), jt, sm("sp"), sub)
+        tt(jn + " sp", "sg", sm("sg"), jt, sh("sp"), sub)
         tt("sg SPR SE", "UU", T.UU[:], sm("sg").indirect(su("SPR")), T.SE[:], mul, "g")
         mms("UU DG0 DG1 IT%d" % t, "P2", [[(T.P2[:, 128 * h:128 * h + 128], T.UU[:, 128 * h:128 * h + 128], x)
                                            for x in (T.DG[:, 128 * h:128 * h + 128], mb("IT%d" % t))] for h in range(2)])
@@ -771,6 +805,8 @@ def rank_program(g, core, T, topo):
         dma("y", "JH", "JF", T.JF[0:128:16, 0:16 * B], T.JH[:, 0:B], 100000)
         if t == 0:
             home_places()
+        if t == 3:
+            has_home()
         o = T.P0[:, 0:TR]
         items = [(o, mf("B1K"), T.X[:]), (o, T.RW[0:1, 512:640], T.RW[0:1, 0:TR]),
                  (o, T.RW[0:1, 640 + 128 * t:768 + 128 * t], T.RW[0:1, TR:2 * TR]),
@@ -798,11 +834,15 @@ def rank_program(g, core, T, topo):
             dma("y", "YO", "", T.yx[:, 0:2176], T.YO[:, 0:2176], 600000)
             dma("s", "YO", "", T.yx[:, 2176:WD - TR], T.YO[:, 2176:WD - TR], 1100000)
             for u in range(4):
-                pass1(u, 768)
-                mm("ZH ONEH C3K R1%d" % u, "PB", ([(T.PB[:, 0:192], mh("ONEH", (0, 1)), T.C3K[0:1, :])] if u == 0 else [])
-                   + [(T.PB[:, 0:192], T.ZH[:, 15 - r:143 - r], T.R1[:, 192 * r:192 * r + 192]) for r in range(4 * u, 4 * u + 4)],
-                   first=u == 0, last=u == 3)
-            tt("PB SLI1", "YJ", T.YJ[:], T.PB[:, 0:192], T.SLI[:, 192:384], mx)
+                if u < 2:
+                    sl = slice(768 * u, 768 * u + 768)
+                    tt("JH HEL KM", "R1%d" % u, T.R1[:, sl], T.JH[:, 0:B].indirect(T.HEL[:, 48 * u:48 * u + 48]), T.KM[:, sl], mul, "g")
+                else:
+                    pass1(u, 768)
+                mm("ZH ZA IH HH1 R1%d" % u, "P1", ([(T.P1[:, 0:192], mh("IH"), T.HH[:, 192:384])] if u == 0 else [])
+                   + [(T.P1[:, 0:192], (T.ZA if u < 2 else T.ZH)[:, 15 - r:143 - r], T.R1[:, 192 * r:192 * r + 192])
+                      for r in range(4 * u, 4 * u + 4)], first=u == 0, last=u == 3)
+            tt("P1 SLI1", "YJ", T.YJ[:], T.P1[:, 0:192], T.SLI[:, 192:384], mx)
             dma("y", "YJ", "", T.yj[:], T.YJ[:], 98304)
             break
 
@@ -824,13 +864,13 @@ def rank_program(g, core, T, topo):
                 pass1(x, 512)
             sl = slice(32 * x0, 32 * x1)
             o = T[bk][:, 256:256 + 32 * (x1 - x0)]
-            mm("ZH ONEH C3K " + many("R1", x1, x0), bk, [(o, mh("ONEH", (0, 1)), T.C3K[0:1, sl])]
+            mm("ZH ONE C3K " + many("R1", x1, x0), bk, [(o, mb("ONE", (0, 1)), T.C3K[0:1, sl])]
                + [(o, T.ZH[:, 15 - r:143 - r], T.R1[:, 512 * x0 + r:512 * x1:16]) for r in range(16)])
             tt(bk + " SLI0", "JO%d" % u, T.JO[:, sl], o, T.SLI[:, sl], mx)
             cp("JO%d" % u, "JU%d" % u, T.JU[:, sl], T.JO[:, sl])
             for x in range(x0, x1):
                 lin2("W JU%d" % u, "XE%d" % x, T.XE[:, 512 * x:512 * x + 512],
-                     T.W[:, 0:WD].indirect(T.JU[:, 32 * x:32 * x + 32]), ind="g")
+                     T.W[:, 0:V + TR * t + TR].indirect(T.JU[:, 32 * x:32 * x + 32]), ind="g")
         if t:
             tt(pvn + " SG CU W", "W", T.W[:].indirect(su("CU")), pv[:], T.SG[:], mul, "s")
         else:
@@ -842,7 +882,7 @@ def rank_program(g, core, T, topo):
         ts("AM", "AM", si("AM"), si("AM"), 248, band)
 
     dma("y", "bfi", "", T.yb[:], T.bfi[:])
-    dma("y", "zin6", "", T.yz[:], T.zin[:, S * TR:S * TR + TR], 65536)
+    dma("y", "zin6", "", T.yz[:], T.zin[:, 2 * S * TR:2 * S * TR + TR], 65536)
 
     count, seen, token, nd = {}, {}, {}, 0
     for n, (q, c0, c1, fn, kind), deps in put_in_order(ops):

from concourse.mybir import AluOpType as ALU, AxisListType, ActivationFunctionType as ACT

N, V, B, TR, S = 6, 3072, 384, 256, 6
WD = V + TR * S
U = 131072.0
CAP = 32304.0
HELD = 85000.0
NONE = 8192.0
BW = 392
BIG = 8192.0
CYC, GAT, SCA, FIX, PEC, PEF, LAT, DMA, HOP = 1.04, 1.3, 3.15, 60.0, 0.52, 15.0, 80.0, 2200.0, 3300.0
ROUNDS, SEED = 8000, 1
ROWS = ((0, 2), (2, 4), (4, 6), (6, 8), (8, 10), (10, 12), (12, 14), (14, 15), (15, 16))
PARTS = (("P2", 0, 2), ("PK", 2, 4), ("P2", 4, 6))
PLACED = {}

F32, BF, F16, I32, U16 = "float32", "bfloat16", "float16", "int32", "uint16"
SCRATCH = {}
for _n, _c, _d in [
    ("xsb", V, BF), ("sb3", 3 * BW, I32), ("pq", 384, I32), ("pqh", 384, F16), ("pqr", V, F16),
    ("bxi", TR, I32), ("bxh", TR, F16), ("limi", 16, I32), ("limb", 16, I32),
    ("W", WD + TR, F32), ("XE", V, F32), ("DP", 17 * TR, F32), ("RL", 4096, BF),
    ("R1", V, F16), ("KM", V, F16), ("IOS", V, I32), ("HEL", 192, U16), ("HS", 192, U16), ("C3K", 192, BF), ("SLI", 384, F32),
    ("JF", 17 * B, F32), ("ZK", 144, F16),
    ("JO", 192, F32), ("JU", 192, U16), ("JH", 648, F32), ("YO", WD + TR, BF), ("YL", TR, BF), ("YJ", 192, F32),
    ("COL", TR, F32), ("D3", 400, F32), ("D2", 400, F32), ("FBT", 400, F32), ("GV", 128, F32), ("GW", 200, F32),
    ("PI", 8, I32), ("PF", 8, F32), ("PC", 96, F32), ("PH", 16, BF), ("OH", 16, F32),
    ("MB", 128 * 18, BF), ("MH", 128 * 16, F16), ("EG", 240, F16), ("sbf", 3 * BW, F32), ("D8", 128, BF), ("MF", 128 * 5, F32), ("W8", 48, BF), ("W8H", 96, F16), ("W8F", 8, F32),
    ("ZH", 144, F16), ("ZB", 144, F16), ("EH", 328, F16), ("CL", 200, F32), ("CLH", 200, F16), ("BIG", 200, BF),
    ("RW", 1408, BF), ("CF", 16 * 7, F32), ("CH", 16 * 7, F16), ("C17", TR, BF), ("DG", TR, BF), ("HH", 384, F16), ("ZA", 144, F16),
    ("RST", TR + 16, F32), ("MASK", TR, BF), ("MASK2", TR, BF), ("BI", 288, I32), ("BC", 288, F32),
    ("B8", TR, BF), ("CB", 32, F32),
    ("OT", TR, F32), ("OU", TR, F32), ("OFF", TR, U16), ("INA", TR, BF), ("JK", TR, F32), ("FX", TR, F16),
    ("H", 656, BF), ("MS", 200, F32), ("LK", TR, BF), ("PM", TR, I32), ("M2", TR, F32), ("PM2", TR, I32),
    ("SK", TR, F16), ("SF", TR, F16), ("SN", TR, F16), ("SO", TR, F16), ("SC", TR, F32), ("LS", TR, BF),
    ("XD", TR, BF), ("XF", TR, BF), ("FE", TR, F16), ("FF", TR, F16), ("LE0", TR, F16), ("LE1", TR, F16),
    ("JNK", 8 * B, BF), ("AA", TR, BF), ("HB", TR, BF), ("AB", TR, BF), ("TH", TR, F32),
    ("SE", TR, BF), ("UU", TR, BF), ("X", TR, F32), ("PV0", TR, F32), ("PV1", TR, F32), ("SG", TR, F32), ("ZM", TR, BF),
    ("SM", 16 * 40, F32), ("SI", 16 * 8, I32), ("SU", 16 * 10, U16), ("SH", 16 * 16, F16),
    ("zin", (2 * S + 1) * TR, BF), ("zout", S * TR, BF), ("lin", S * 32, U16), ("lout", S * 32, U16),
    ("stin", S * 48, I32), ("stout", S * 48, I32), ("Y3", 48, F32), ("T3", 48, F32), ("bfi", 16, F32), ("bfo", 16, F32),
]:
    SCRATCH[_n] = ("sbuf", [128, _c], _d)
BANKS = ("P0", "P1", "P2", "PK", "PA", "PB", "PE", "PD")
for _n in BANKS:
    SCRATCH[_n] = ("psum", [128, 512], F32)

SEMAPHORES = (["sv", "ss", "sp", "sg", "sent"] + ["d%d" % k for k in range(40)]
              + ["a%s%d" % (x, k) for x in "zylsp" for k in range(S)])


def many(x, n, lo=0):
    return " ".join("%s%d" % (x, k) for k in range(lo, n))


WHOLE = {"Ws": many("W", 12), "W": "Wl Wd " + many("W", 12), "DP": many("DP", 17), "ce": many("ce", 16), "XE": many("XE", 6),
         "KM": many("KM", 6), "sb3": many("sb", 8), "pqr": "pqr0 pqr1", "YO": many("YO", 5) + " YOd", "PF": many("PF", 1),
         "JF": many("JF", 4), "RW": many("RW", 4)}


def names(text):
    return " ".join(WHOLE.get(x, x) for x in text.split()).split()


def put_in_order(ops):
    wrote, read, deps = {}, {}, []
    soft = PLACED.setdefault("soft", set())
    for n, (ways, R, Wr) in enumerate(ops):
        d = set()
        fed = {wrote[r] for r in R + Wr if r in wrote and r[0] != "~"} | {x for r in Wr for x in read.get(r, ())}
        for r in R:
            if r in wrote:
                d.add(wrote[r])
            if r in BANKS:
                d.update(read.get(r, ()))
        for r in Wr:
            if r in wrote:
                d.add(wrote[r])
            d.update(read.get(r, ()))
        d.discard(n)
        deps.append(d)
        soft.update((x, n) for x in d if x not in fed and ways[0][4] == "c" and ops[x][0][0][4] == "c")
        for r in R:
            read.setdefault(r, []).append(n)
        for r in Wr:
            wrote[r] = n
            read[r] = []
    if "place" not in PLACED:
        PLACED["place"] = shorten([[w[:3] for w in o[0]] for o in ops], [sorted(d) for d in deps], [kind_of(o) for o in ops], None, ROUNDS)
        PLACED["ops"] = [(o[1], o[2], [w[:3] for w in o[0]], sorted(d)) for o, d in zip(ops, deps)]
    place = PLACED["place"]
    return [(n, ops[n][0][place[n][0]], deps[n]) for n in sorted(range(len(ops)), key=lambda k: (place[k][1], k))]


def kind_of(o):
    return "".join(x for x in (o[2] or ["out"])[0] + "<" + (o[1] or [""])[0] if not x.isdigit())


def place_calls(ops, deps, order, fixed, back):
    busy, place, soft = {q: [] for q in "vspgy"}, [None] * len(ops), PLACED["soft"]
    for n in order:
        best = None
        for k in (range(len(ops[n])) if fixed[n] is None else (fixed[n],)):
            w = ops[n][k]
            t = 0.0
            for d in deps[n]:
                e = place[d][2]
                if w[0] != ops[d][place[d][0]][0] or (w[0] != "p" and ((n, d) if back else (d, n)) not in soft):
                    e += LAT
                if e > t:
                    t = e
            if back:
                t += w[2] - w[1]
            lst = busy[w[0]]
            lo, hi = 0, len(lst)
            while lo < hi:
                mid = (lo + hi) // 2
                if lst[mid][1] <= t:
                    lo = mid + 1
                else:
                    hi = mid
            while lo < len(lst) and t + w[1] > lst[lo][0]:
                t = max(t, lst[lo][1])
                lo += 1
            e = t + (w[1] if back else w[2])
            if best is None or e < best[2]:
                best = (k, t, e, lo)
        place[n] = best
        w = ops[n][best[0]]
        busy[w[0]].insert(best[3], (best[1], best[1] + w[1]))
    return place


def shorten(ops, deps, kinds, cur=None, ROUNDS=None, SEED=1):
    n_ = len(ops)
    succ = [[] for _ in ops]
    level = [0.0] * n_
    for n in range(n_ - 1, -1, -1):
        level[n] += min(w[2] for w in ops[n]) + LAT
        for d in deps[n]:
            succ[d].append(n)
            level[d] = max(level[d], level[n])
    seed = [SEED]

    def draw(k):
        seed[0] = (seed[0] * 1103515245 + 12345) % 2147483648
        return (seed[0] >> 8) % k

    free = [n for n in range(n_) if len(ops[n]) > 1]
    cur = cur or place_calls(ops, deps, sorted(range(n_), key=lambda k: (-level[k], k)), [None] * n_, False)
    best, cs = cur, max(x[2] for x in cur)
    bs = cs
    for it in range(ROUNDS):
        fixed = [x[0] for x in cur]
        if draw(4):
            ends = {(ops[n][x[0]][0], round(x[1] + ops[n][x[0]][1])): n for n, x in enumerate(cur)}
            n = max(range(n_), key=lambda k: cur[k][2])
            waits = []
            while n is not None:
                m = ends.get((ops[n][cur[n][0]][0], round(cur[n][1])))
                if m is not None and m not in deps[n]:
                    waits.append((n, m))
                    n = m
                else:
                    n = max(deps[n], key=lambda k: cur[k][2]) if deps[n] else None
            key = [x[1] for x in cur]
            for _ in range(1 + draw(2)):
                n, m = waits[draw(len(waits))]
                way_ = draw(4)
                if way_ == 0 and len(ops[m]) > 1:
                    fixed[m] = 1 - fixed[m]
                elif way_ == 1 and len(ops[n]) > 1:
                    fixed[n] = 1 - fixed[n]
                elif way_ == 2:
                    key[m] = min([key[d] for d in succ[m]] + [key[n] + 1.0 + draw(1500)]) - 0.5
                else:
                    key[n] = max([key[d] for d in deps[n]] + [key[m] - 1.0 - draw(1500)]) + 0.5
            for n in range(n_):
                for d in deps[n]:
                    key[n] = max(key[n], key[d])
            new = place_calls(ops, deps, sorted(range(n_), key=lambda k: (key[k], k)), fixed, False)
            s_ = max(x[2] for x in new)
            if s_ < cs + 150.0 * (1.0 - it / ROUNDS):
                cur, cs = new, s_
                if s_ < bs:
                    best, bs = new, s_
            continue
        if draw(4) == 0:
            kind, k = kinds[free[draw(len(free))]], draw(2)
            for n in free:
                if kinds[n] == kind:
                    fixed[n] = k
        else:
            for _ in range((0, 1, 3, 8)[draw(4)]):
                fixed[free[draw(len(free))]] = draw(2)
        b = place_calls(ops, succ, sorted(range(n_), key=lambda k: (-cur[k][2], -k)), fixed, True)
        key = [-x[2] for x in b]
        for _ in range((0, 5, 30)[draw(3)]):
            n = draw(n_)
            lo = max([key[d] for d in deps[n]] or [key[n] - 2000.0])
            hi = min([key[d] for d in succ[n]] or [key[n] + 2000.0])
            key[n] = lo + (hi - lo) * (1 + draw(999)) / 1001.0
        new = place_calls(ops, deps, sorted(range(n_), key=lambda k: (key[k], k)), fixed, False)
        s_ = max(x[2] for x in new)
        if s_ < cs + 400.0 * (1.0 - it / ROUNDS):
            cur, cs = new, s_
            if s_ < bs:
                best, bs = new, s_
    return best


def rank_program(g, core, T, topo):
    rank = T.rank_of(core)
    if rank is None:
        return
    Q = {"v": g.vector, "s": g.scalar, "p": g.tensor, "g": g, "y": g.sync}
    own = {"v": "sv", "s": "ss", "p": "sp", "g": "sg"}
    ops = []

    def nel(ap):
        n = 1
        for x in list(ap.shape)[1:]:
            n *= int(x)
        return n

    def two(*aps):
        return all("16" in str(x.dtype) for x in aps)

    def op(ways, R, Wr):
        ops.append((ways, names(R), names(Wr)))

    def way(q, c, fn):
        return (q, c, c, fn, "c")

    def plain(n, k=1.0):
        return FIX + max(64.0, n * k) * CYC

    def vtime(out, a, ind, k):
        if ind == "g":
            return 55 + nel(out) * GAT
        if ind == "s":
            return 50 + nel(a) * SCA
        return plain(nel(a), k)

    def dma(q, R, Wr, out, in_, nbytes=0):
        op([(q, 100.0, DMA + nbytes / 200.0, lambda: Q[q].dma_start(out, in_), "d")], R, Wr)

    def mms(R, Wr, groups, first=True, last=True):
        def fn():
            for items in groups:
                for n, (o, l, r) in enumerate(items):
                    ins = g.tensor.matmul(o, l, r, first and n == 0, last and n == len(items) - 1)
            return ins
        op([way("p", sum(PEF + max(min(64, nel(l)), nel(r)) * PEC * (1 if two(l) else 4) for it in groups for o, l, r in it), fn)], R, Wr)

    def mm(R, Wr, items, first=True, last=True):
        mms(R, Wr, [items], first, last)

    def ts_way(out, a, s1, o1, s2, o2, ind):
        c = vtime(out, a, ind, 0.5 if ind is None and two(out, a) else 1.0)
        if o2 is None:
            return way("v", c, lambda: g.vector.tensor_scalar(out, a, s1, None, o1))
        return way("v", c, lambda: g.vector.tensor_scalar(out, a, s1, s2, o1, o2))

    def ts(R, Wr, out, a, s1, o1, s2=None, o2=None, ind=None):
        op([ts_way(out, a, s1, o1, s2, o2, ind)], R, Wr)

    def tt(R, Wr, out, a, b, o, ind=None):
        k = 1.0 if any(x in BANKS for x in R.split()) else 2.0
        op([way("v", vtime(out, a, ind, k), lambda: g.vector.tensor_tensor(out, a, b, o))], R, Wr)

    def cp_way(out, a, ind):
        return way("v", vtime(out, a, ind, 0.5 if ind is None and two(out, a) else 1.0), lambda: g.vector.tensor_copy(out, a))

    def cp(R, Wr, out, a, ind=None):
        op([cp_way(out, a, ind)], R, Wr)

    def ms(Wr, out, c):
        op([way("v", plain(nel(out), 0.5 if two(out) else 1.0), lambda: g.vector.memset(out, c))], "", Wr)

    def act_way(out, a, f, ind, kw):
        return way("s", vtime(out, a, ind, 1.0) + 20 * ("accum_out" in kw), lambda: g.scalar.activation(out, a, f, **kw))

    def act(R, Wr, out, a, f, ind=None, **kw):
        op([act_way(out, a, f, ind, kw)], R, Wr)

    add, sub, mul, mx, mn = ALU.add, ALU.subtract, ALU.mult, ALU.max, ALU.min
    eq, ge, gt, le, lt = ALU.is_equal, ALU.is_ge, ALU.is_gt, ALU.is_le, ALU.is_lt
    band, shr = ALU.bitwise_and, ALU.arith_shift_right

    def lin2(R, Wr, out, a, scale=None, bias=None, ind=None):
        if scale is None and bias is None:
            op([act_way(out, a, ACT.Copy, ind, {}), cp_way(out, a, ind)], R, Wr)
            return
        s_, b_ = 1.0 if scale is None else scale, 0.0 if bias is None else bias
        op([act_way(out, a, ACT.Identity, ind, {"scale": s_, "bias": b_}), ts_way(out, a, s_, mul, b_, add, ind)], R, Wr)

    def relu2(R, Wr, out, a, bias, ind=None):
        op([act_way(out, a, ACT.Relu, ind, {"bias": bias}), ts_way(out, a, bias, add, 0.0, mx, ind)], R, Wr)

    def scan(R, Wr, out, d0, d1, o0, o1):
        op([way("v", plain(nel(d0)), lambda: g.vector.tensor_tensor_scan(out, d0, d1, 0.0, o0, o1))], R, Wr)

    def iota(Wr, out, pat, base, cm, flt=True):
        kw = {"allow_small_or_imprecise_dtypes": True} if flt else {}
        op([way("g", 130 + 2 * nel(out) * CYC, lambda: g.iota(out, pat, base, cm, **kw))], "", Wr)

    slots = {}

    def sm(name, a=0, b=16, st=1, pool="SM", w=16, rows=None):
        d = slots.setdefault(pool, {})
        k = d.setdefault(name, len(d))
        if rows is not None:
            return T[pool][rows[0]:rows[1], w * k + a:w * k + b:st]
        return T[pool][:, w * k + a:w * k + b:st]

    def si(name):
        return sm(name, pool="SI")

    def su(name):
        return sm(name, pool="SU")

    def sh(name, a=0, b=16, st=1):
        return sm(name, a, b, st, pool="SH")

    def mb(name, rows=None):
        return sm(name, 0, 128, pool="MB", w=128, rows=rows)

    def mh(name, rows=None, b=128):
        return sm(name, 0, b, pool="MH", w=128, rows=rows)

    def mf(name, rows=None):
        return sm(name, 0, 128, pool="MF", w=128, rows=rows)

    def w8(name):
        return sm(name, 0, 8, pool="W8", w=8)

    def wh(name):
        return sm(name, 0, 8, pool="W8H", w=8)

    nxt = T.cores[(rank + 1) % N]
    rid, pid = topo.addr(nxt)[:2]
    emask = topo.mask(core, nxt)
    neng = len(topo.engines(core, nxt))

    def send(R, Wr, out, in_, sem):
        op([("g", 600.0, HOP + 4.0 * nel(out), lambda: g.remote_dma(out, in_, T.sem[sem], T.sem.sent, pid, rid, emask), sem)], R, Wr)

    dma("y", "", "pq0", T.pq[:, 0:192], T.pe[:], 98304)
    dma("s", "", "pq1", T.pq[:, 192:384], T.he[:], 98304)
    dma("y", "", "xsb0", T.xsb[:, 0:1536], T.xs[:, 0:1536], 600000)
    dma("s", "", "bxi", T.bxi[0:8, :], T.bx[:])
    dma("y", "", "xsb1", T.xsb[:, 1536:V], T.xs[:, 1536:V], 800000)
    dma("s", "", "sb0", T.sb3[:, 0:B], T.sb[:], 196608)
    dma("y", "", "sb1", T.sb3[16:128, BW:BW + B], T.sb[0:112, :], 196608)
    dma("y", "", "sb2", T.sb3[0:112, 2 * BW:2 * BW + B], T.sb[16:128, :], 196608)
    dma("y", "", "sb3a", T.sb3[0:16, BW:BW + B], T.sb[0:16, :])
    dma("y", "", "sb4", T.sb3[112:128, 2 * BW:2 * BW + B], T.sb[0:16, :])
    dma("y", "", "zraw ZM", T.ZM[:], T.zs[:], 65536)
    dma("y", "", "limi", T.limi[0:1, :], T.lim[:])
    for k in range(3):
        iota("sb%d" % (5 + k), T.sb3[:, BW * k + B:BW * k + BW], [[0, BW - B]], 0, 0, False)

    iota("PI0", T.PI[:, 0:1], [[0, 1]], 0, 1, False)
    iota("COL", T.COL[:], [[1, TR]], 0, 0)
    iota("GV", T.GV[:], [[16, 8], [0, 16]], 0, 0)
    iota("ONE", mb("ONE"), [[0, 128]], 1, 0)
    iota("D3", T.D3[:], [[0, 25], [1, 16]], 0, 0)
    iota("D8", T.D8[:], [[0, 16], [1, 8]], 0, 0)
    iota("CF0", T.CF[0:1, 0:16], [[0, 16]], 1536, 0)
    iota("CF1", T.CF[0:1, 16:16 + 16 * S], [[-512, S], [0, 16]], int(BIG - 1 - 191 - 512 * 3), 0)
    lin2("CF0 CF1", "CH", T.CH[0:1, :], T.CF[0:1, :])
    iota("D2", T.D2[:], [[1, 25], [0, 16]], 1024, 0)
    iota("BC1", T.BC[:, TR:TR + 12], [[256, 12]], 0, 0)
    iota("BC2", T.BC[:, TR + 12:TR + 32], [[256, 20]], 0, 0)
    iota("GW", T.GW[:], [[16, 8], [0, 25]], 0, 0)
    iota("CL", T.CL[0:1, :], [[0, 8], [-1, 25]], -1024, 0)
    op([way("g", 300.0, lambda: g.partition_broadcast(T.limb[:], T.limi[0:1, :], 128))], "limi", "limb")
    iota("JH", T.JH[:], [[0, 648]], -int(NONE), 0)
    iota("JF0", T.JF[:, 0:1632], [[0, 1632]], -int(NONE), 0)
    for k in range(1, 4):
        dma("y", "JF0", "JF%d" % k, T.JF[:, 1632 * k:1632 * k + 1632], T.JF[:, 0:1632], 840000 * k)
    iota("RST", T.RST[:], [[0, TR + 16]], 0, 0)
    iota("RST", T.RST[:, 0:TR + 16:16], [[0, 17]], int(CAP), 0)
    iota("JH", T.JH[:, B:B + 1], [[0, 1]], 0, 0)
    iota("Y0", T.Y3[:, 0:16], [[0, 16]], -B, 0)
    iota("C3K", T.C3K[0:1, :], [[0, 192]], V, 0)
    iota("BIG", T.BIG[0:1, :], [[0, 200]], 0, 0)
    for u in range(6):
        iota("IOS%d" % u, T.IOS[:, 512 * u:512 * u + 512], [[1, 512]], 512 * u, 0, False)
    iota("RW0", T.RW[:, 0:TR], [[-1, TR]], 0, 0)
    iota("RW1", T.RW[0:1, TR:2 * TR], [[0, TR]], 512, 0)
    iota("RW2", T.RW[0:1, 512:640], [[0, 128]], 4096, 0)
    iota("RW3", T.RW[0:1, 640:1408], [[-2048, S], [0, 128]], 224 * 2048, 0)
    for k, (sh_, mk) in enumerate(((0, 15), (0, 112), (4, 7), (0, 7), (4, 1), (3, 1))):
        ts("PI0", "PI%d" % (k + 1), T.PI[:, k + 1:k + 2], T.PI[:, 0:1], sh_, shr, mk, band)
    cp(many("PI", 7), "PF", T.PF[:, 0:7], T.PI[:, 0:7])
    pc, rc, gc, xg, q7, par, q8 = [T.PF[:, k:k + 1] for k in range(7)]
    lin2("PF", "PI7", T.PF[:, 7:8], q8, 8.0)
    ts("COL PF", "OH", T.OH[:], T.COL[:, 0:16], rc, eq)
    cp("pq0 pq1", "pqh", T.pqh[:], T.pq[:])
    for f in range(2):
        dma("ys"[f], "pqh", "pqr%d" % f, T.pqr[8 * f:8 * f + 8, :], T.pqh[:, 192 * f:192 * f + 192], 49152)

    pcn = [0]

    def col():
        pcn[0] += 1
        return T.PC[:, pcn[0] - 1:pcn[0]], "pc%d" % pcn[0]

    def lin(a, an, s, b, bn=""):
        c, n = col()
        lin2(an + " " + bn, n, c, a, s, b)
        return c, n

    def test(a, c, o, s):
        x, n = col()
        ts("PF", n, x, a, c, o, s, mul)
        return x, n

    def rows(spec, prev=None):
        for r, w in spec:
            prev = lin(T.OH[:, r:r + 1], "OH", float(w), 0.0 if prev is None else prev[0], "" if prev is None else prev[1])
        return prev

    IB, ONE = mb("IB"), mb("ONE")
    ts("COL PF", "IB", IB, T.COL[:, 0:128], pc, eq)
    def put_way(out, src, step, base, c):
        return way("g", 170 + 2 * nel(out) * CYC,
                   lambda: g.affine_select(out, src, [[step, nel(out)]], ALU.not_equal, float(c), base, 1))

    def diag(nm, out, c):
        op([put_way(out, mb("NIL"), -1, 0, c), act_way(out, IB, ACT.Identity, None, {"scale": c})], "NIL IB", nm)

    iota("NIL", mb("NIL"), [[0, 128]], 0, 0)
    lin2("IB", "UI", mb("UI"), IB, U)
    for nm, w in (("NIB", -1.0), ("N64", 80.0 * U), ("HIB", 0.5), ("UH", U / 2), ("N512", -512.0 * U), ("IU", 1.0 / U)):
        diag(nm, mb(nm), w)
    for t in range(S):
        diag("IT%d" % t, mb("IT%d" % t), NONE + 256.0 * t)
    lin2("IB", "IH", mh("IH"), IB)
    lin2("ONE", "ONEH", mh("ONEH"), ONE)
    diag("I4", mf("I4"), 4.0)
    diag("NI3", mh("NI3"), 2.0 + 1.0 / 512)
    diag("I4K", mh("I4K"), 4096.0)
    ts("GV PF", "B1K", mf("B1K"), T.GV[:], gc, eq, 2048.0, mul)
    ts("GV PF", "BLK", w8("BLK"), T.GV[:, 0:128:16], gc, eq)
    BLK = w8("BLK")
    lin2("BLK", "W8A", w8("W8A"), BLK, 32.0 / U)
    lin2("BLK", "BLKF", T.W8F[:], BLK)
    ts("D3 PF", "MASK", T.MASK[:], T.D3[:, 0:TR], rc, eq)
    cp("COL", "SPR", su("SPR"), T.COL[:, 0:16])
    r16, r16n = lin(rc, "PF", 16.0, 0.0)
    ts("COL " + r16n, "PERM", su("PERM"), T.COL[:, 0:16], r16, add)
    lin2("COL PF", "J16", sh("J16"), T.COL[:, 0:16], 16.0, rc)
    npar, nparn = lin(par, "PF", -1.0, 1.0)
    lin2("IB " + nparn, "P00", mh("P00"), IB, npar)
    lin2("IB PF", "P11", mh("P11"), IB, par)
    iota("PX", T.PC[:, 92:95], [[16, 3]], -16, 1)
    (up, upn), (dn, dnn) = (T.PC[:, 94:95], "PX"), (T.PC[:, 92:93], "PX")
    ts("COL %s %s" % (upn, nparn), "P10", mh("P10"), T.COL[:, 0:128], up, eq, npar, mul)
    ts("COL PF " + dnn, "P01", mh("P01"), T.COL[:, 0:128], dn, eq, par, mul)
    ts("ONE PF", "VO0", sh("VO", 0, 16, 2), T.MB[:, 0:8], par, mul, float(BW), mul)
    ts("ONE " + nparn, "VO1", sh("VO", 1, 16, 2), T.MB[:, 0:8], npar, mul, 2.0 * BW, mul)

    def spread(R, Wr, out, src, mask="MASK"):
        tt(R + " SPR " + mask, Wr, out[:], src.indirect(su("SPR")), T[mask][:], mul, "g")

    def to_list(sn, c0, blk, bn, extra=None, bk="PE"):
        its = [(T[bk][:, c0 + 8 * h:c0 + 8 * h + 8], T[sn][:, 128 * h:128 * h + 128], blk) for h in range(2)]
        if extra is None:
            mms(sn + " " + bn, bk, [[x] for x in its])
        else:
            mm("%s %s IH %s" % (sn, bn, extra), bk, [(T[bk][:, c0:c0 + 16], mh("IH"), sh(extra))] + its)

    def as_list(R, sn, src, c0, mask, extra=None, bk="PE"):
        tt("%s SP8 %s" % (R, mask), sn, T[sn][:, 0:128], src.indirect(sm("SP8", 0, 8, pool="SU")), mh(mask), mul, "g")
        o = T[bk][:, c0:c0 + 16]
        mm("%s EG IH %s" % (sn, extra or ""), bk, ([(o, mh("IH"), sh(extra))] if extra else [])
           + [(o, T.EG[:, 112 - 16 * q:240 - 16 * q], T[sn][:, 16 * q:16 * q + 16]) for q in range(8)])

    r112, r112n = lin(rc, "PF", 1.0, 112.0)
    ts("COL " + r112n, "EG", T.EG[:], T.COL[:, 0:240], r112, eq)
    lin2("PI7 COL", "UT", sm("UT", 0, 8), T.COL[:, 0:8], None, T.PF[:, 7:8])
    cp("UT", "SP8", sm("SP8", 0, 8, pool="SU"), sm("UT", 0, 8))
    ts("D8 PF", "MN", mh("MN"), T.D8[:], xg, eq, -1.0, mul)
    ts("D8 PF", "M256", mh("M256"), T.D8[:], xg, eq, 256.0, mul)

    def pair_lists(out, on, both=False):
        as_list("af", "SN", sm("af"), 32, "MN")
        lin2("PE", "BH", sh("BH"), T.PE[:, 32:48])
        mm("BH IH VO0 VO1 P00 P01 P10 P11", "PE", [(T.PE[:, 48:64], mh("IH"), sh("VO"))]
           + [(T.PE[:, 48 + v:64:2], mh("P%d%d" % (u, v)), sh("BH", u, 16, 2)) for u in range(2) for v in range(2)])
        cp("PE", on, out, T.PE[:, 32 if both else 48:64])

    cp("bxi", "bxh", T.bxh[0:8, :], T.bxi[0:8, :])
    mms("bxh IH", "PA", [[(T.PA[:, 8 * h:8 * h + 8], T.bxh[0:8, 128 * h:128 * h + 128], mh("IH", (0, 8), 8))] for h in range(2)])
    ts("PA", "stin0", T.stin[:, 16:32], T.PA[:, 0:16], -1.0, mul, BIG - 1, add)
    lin2("PA", "af", sm("af"), T.PA[:, 0:16], -1.0)
    pair_lists(T.lin[:, 0:32], "lin0 pin0", True)
    lin2("zraw", "zin0", T.zin[:, 0:TR], T.ZM[:], U)
    lin2("zraw", "yin0", T.zin[:, TR:2 * TR], T.ZM[:], U)
    ts("ONE PF", "SP3", su("SP3"), T.MB[:, 0:16], rc, mul)
    for t in range(S):
        iota("sx%d" % t, T.stin[:, 48 * t + 32:48 * t + 48], [[128, 2], [0, 8]], WD, 1, False)

    LN2 = 0.6931471805599453
    act("PF", "PH0", T.PH[:, 0:1], rc, ACT.Exp, scale=-LN2)
    act("PF", "PH1", T.PH[:, 1:2], rc, ACT.Exp, scale=LN2, bias=-LN2)
    lin2("COL PF", "TI", sm("TI", 0, 2), T.COL[:, 0:2], 128.0, pc)
    act("TI", "PH2", T.PH[:, 2:4], sm("TI", 0, 2), ACT.Exp, scale=-0.4 * LN2, bias=51.2 * LN2)
    for h in range(2):
        ts("ONE PH2", "TB%d" % h, sm("THB", 8 * h, 8 * h + 8), T.MB[:, 0:8], T.PH[:, 2 + h:3 + h], mul, T.PH[:, 2 + h:3 + h], mul)
    lin2("PH2", "WT", sm("WT", 0, 2), T.PH[:, 2:4])
    lin2("TB0 TB1", "THB", sm("THB"), sm("THB"), 2.57 * 1024)
    sr, srn = lin(T.PH[:, 0:1], "PH0", 1.0, 0.0)
    sb_, sbn = lin(T.PH[:, 0:1], "PH0", 0.5, -0.5)
    lin2("COL", "BC0", T.BC[:, 0:TR], T.COL[:])
    ts("BC0 BC1 BC2 %s %s" % (srn, sbn), "BI", T.BI[:], T.BC[:], sr, mul, sb_, add)
    ts("BI", "BI", T.BI[:], T.BI[:], 1, band)
    a2, a2n = test(rc, 8.0, lt, 2.0)
    a1, a1n = test(rc, 8.0, lt, -1.0)
    ts("BI %s %s" % (a2n, a1n), "B8", T.B8[:], T.BI[:, 0:TR], a2, mul, a1, add)
    b2, b2n = test(rc, 12.0, lt, 2.0)
    lin2("%s %s" % (b2n, a2n), b2n, b2, a2, -1.0, b2)
    bs_, bsn = rows([(12, -1.0), (13, -191.0), (14, -191.0)], lin(b2, b2n, -0.5, 64.0 * U))
    bl_, bln = rows([(12, 1.0)], lin(b2, b2n, -0.5, 0.0))
    ts("BI %s %s" % (b2n, bsn), "CB", T.CB[:, 0:12], T.BI[:, TR:TR + 12], b2, mul, bs_, add)
    ts("BI %s %s" % (b2n, bln), "CBa", T.CB[:, 12:18], T.BI[:, TR + 12:TR + 18], b2, mul, bl_, add)
    s7, s7n = lin(q7, "PF", 16.0, 13.0)
    s8, s8n = lin(q8, "PF", 1.0, s7, s7n)
    ts("COL " + s8n, "SEL", mh("SEL"), T.COL[:, 0:128], s8, eq)

    for m, bk in enumerate(("P0", "P1", "P2", "PB", "PD", "PK")):
        sl = slice(512 * m, 512 * m + 512)
        mm("UI IB xsb%d B8" % (m // 3), bk, [(T[bk][:], mb("UI"), T.xsb[:, sl])]
           + [(T[bk][:, TR * u:TR * u + TR], IB, T.B8[:]) for u in range(2)], last=False)
        mm("SEL pqr", bk, [(T[bk][:], mh("SEL", (0, 16)), T.pqr[0:16, sl])], first=False)
        for u in range(2):
            c0 = 512 * m + TR * u
            lin2(bk + " CB", "W%d" % (2 * m + u), T.W[:, c0:c0 + TR], T[bk][:, TR * u:TR * u + TR], None,
                 T.CB[:, 2 * m + u:2 * m + u + 1])

    ts("D3 PF", "FBT", T.FBT[:], T.D3[:], rc, eq)
    tt("FBT D2", "FBT", T.FBT[:], T.FBT[:], T.D2[:], mul)
    ts("GV PF", "S12", mh("S12"), T.GV[:], gc, eq)
    tt("IB S12", "EH0", T.EH[:, 0:128], IB, mh("S12"), sub)
    lin2("S12 OH EH0", "S12", mh("S12"), mh("S12"), T.OH[:, 12:13])
    ts("GW PF", "EH1", T.EH[:, 128:328], T.GW[:], gc, eq)
    lin2("CL", "CLH", T.CLH[0:1, :], T.CL[0:1, :])
    op([put_way(T.BIG[0:1, 24:200:25], sm("NIL", 0, 8, pool="MB", w=128, rows=(0, 1)), 0, 0, 2.0 ** 55)], "NIL", "BIG")
    op([put_way(mb("BIGR", (0, 1)), mb("NIL", (0, 1)), 0, 0, 2.0 ** 55)], "NIL", "BIGR")
    lo_, lon = lin(xg, "PF", 25.0, -0.46875)
    spc, spcn = rows([(11, -1.0)], lin(T.OH[:, 12:13], "OH", 1.0, 64.0 * U))
    sp8, sp8n = lin(spc, spcn, 1.0, 80.0 * U)
    rq, rqn = lin(rc, "PF", 1.0, -0.25)
    for h in range(2):
        lin2("IB " + rqn, "C17%d" % h, T.C17[:, 128 * h:128 * h + 128], IB, rq)
        lin2("IB TI", "DG%d" % h, T.DG[:, 128 * h:128 * h + 128], IB, sm("TI", h, h + 1))
    l13, l13n = test(rc, 13.0, lt, 256.0)
    LS_ = [lin(l13, l13n, pp, 0.0, ppn) for pp, ppn in ((npar, nparn), (par, "PF"))]

    def weights(nm, spec, made=False):
        for r, w in spec:
            op([put_way(wh(nm), wh(nm) if made else sm("NIL", 0, 8, pool="MB", w=128), -16, -r, w)], nm if made else "NIL", nm)
            made = True

    w12, w12n = test(rc, 12.0, lt, 1.0)
    tt("PH1 " + w12n, w12n, w12, w12, T.PH[:, 1:2], mul)
    lin2("BLK " + w12n, "Wc", wh("Wc"), BLK, w12)
    weights("Wc", [(12, 1536.0)], True)
    weights("Wp", [(13, 1.0)])
    weights("Wh", [(13, 1.0), (14, -1.0)])
    weights("Wn", [(13, -1.0), (12, -512.0)])
    weights("We", [(14, 1.0 / 512), (12, 512.0)])
    weights("Wf", [(14, 2.0), (12, 1024.0)])
    for nm, c in (("S1", 13), ("S2", 14)):
        op([put_way(mh(nm), mb("NIL"), 0, 1, 0.0)], "NIL", nm)
        op([put_way(sm(nm, c, 128, 16, "MH", 128), sm("NIL", 0, 8, pool="MB", w=128), -16, -13, 1.0)], "NIL", nm)
    lin2("ONE", "O8", mh("O8"), ONE, 8.0)
    for h in range(2):
        lin2("ONE TI", "DB%d" % h, sm("DB", 8 * h, 8 * h + 8), T.MB[:, 0:8], sm("TI", h, h + 1), -3328.0)
        ts("limb", "L0%d" % h, sh("L0", 8 * h, 8 * h + 8), T.limb[:, 0:16:2], -1.0, mul)
        ts("limb", "SL%d" % h, sm("SL", 8 * h, 8 * h + 8), T.limb[:, 1:16:2], 32.0, mul, 32.0, add)
    ts("SL0 SL1", "SL0 SL1", sm("SL"), sm("SL"), CAP, mn)
    lin2("DB0 DB1", "TX", sm("TX"), sm("DB"), BIG)
    lin2("DB0 DB1", "DB0 DB1", sm("DB"), sm("DB"), -1.0, -3328.0 - B - 1)
    lin2("J16", "DM", sm("DM"), sh("J16"), None, float(WD))
    z7, z7n = lin(q7, "PF", 16.0, 15.0)
    ts("COL PF " + z7n, "ZB", T.ZB[:], T.COL[:, 0:144], z7, eq, q8, mul)
    g15, g15n = lin(gc, "PF", 1.0, 15.0)
    ts("COL OH " + g15n, "ZH", T.ZH[:], T.COL[:, 0:144], g15, eq, T.OH[:, 0:1], mul)
    ts("COL " + g15n, "ZA", T.ZA[:], T.COL[:, 0:144], g15, eq)
    kb, kbn = lin(rc, "PF", float(B), -16.0 * B)
    ts("COL %s %s" % (g15n, kbn), "ZK", T.ZK[:], T.COL[:, 0:144], g15, eq, kb, mul)
    lin2("COL PF", "SLI0", T.SLI[:, 0:192], T.COL[:, 0:192], 16.0, rc)
    r192, r192n = lin(rc, "PF", 192.0, 0.0)
    lin2("COL " + r192n, "SLI1", T.SLI[:, 192:384], T.COL[:, 0:192], None, r192)
    x8, x8n = lin(xg, "PF", 1.0, 8.0)
    for h, (c, cn) in enumerate(((xg, "PF"), (x8, x8n))):
        ts("D3 " + cn, "MASK2" if h else "MASK2a", T.MASK2[:, 128 * h:128 * h + 128], T.D3[:, 0:128], c, eq)
    lin2("OH", "OHH", sh("OHH"), T.OH[:], -1.0)

    mm("ZB pqr", "PE", [(T.PE[:, 256:448], T.ZB[0:16, 15 - r:143 - r], T.pqr[0:16, r:V:16]) for r in range(16)])
    cp("PE", "HEL", T.HEL[:], T.PE[:, 256:448])
    for u in range(6):
        sl = slice(512 * u, 512 * u + 512)
        tt("sb0 HEL IOS%d" % u, "KM%d" % u, T.KM[:, sl], T.sb3[:, 0:B].indirect(T.HEL[:, 32 * u:32 * u + 32]), T.IOS[:, sl], eq, "g")

    def home_places():
        cp("HEL", "HH0", T.HH[:, 0:192], T.HEL[:])
        mm("IH HH0", "PE", [(T.PE[:, 256:448], mh("IH"), T.HH[:, 0:192])], last=False)
        for q in range(4):
            mm("ZK KM", "PE", [(T.PE[:, 256:448], T.ZK[:, 15 - r:143 - r], T.KM[:, r:V:16]) for r in range(4 * q, 4 * q + 4)],
               first=False, last=q == 3)
        ts("PE", "HS", T.HS[:], T.PE[:, 256:448], 16.0 * B, add)

    def has_home():
        mm("ZA KM", "PD", [(T.PD[:, 256:448], T.ZA[:, 15 - r:143 - r], T.KM[:, 192 * r:192 * r + 192]) for r in range(8)])
        hb, hbn = test(rc, 8.0, ge, V + 1.0)
        lin2(hbn, hbn, hb, hb, None, -1.0)
        lin2("PD " + hbn, "HH1", T.HH[:, 192:384], T.PD[:, 256:448], V + 1.0, hb)

    def fld(n, bk="PA"):
        return T[bk][:, 16 * n:16 * n + 16]

    def field(n, bk, parts, whole=()):
        its = [(fld(n, bk), l, r) for l, r in whole]
        out = [] if not its else [its]
        for h in range(2):
            half = [(T[bk][:, 16 * n + 8 * h:16 * n + 8 * h + 8], src[:, 128 * h:128 * h + 128], w) for src, w in parts]
            if its:
                its += half
            else:
                out.append(half)
        return out

    def cf(k):
        return (mh("ONEH", (0, 1)), T.CH[0:1, 16 * k:16 * k + 16])

    LE = (T.LE0, T.LE1)
    best, best2 = T.PM[:, 15:TR:16], T.PM2[:, 15:TR:16]

    for t in range(S):
        last = t == S - 1
        Z, zn = T.zin[:, 2 * TR * t:2 * TR * t + TR], "zin%d" % t
        BL, B2, ln_ = T.lin[:, 32 * t:32 * t + 16], T.lin[:, 32 * t + 16:32 * t + 32], "lin%d" % t
        st, stn = T.stin[:, 48 * t + 16:48 * t + 32], "stin%d" % t
        win, wn = (T.W[:, 0:V], "Ws") if t == 0 else (T.XE[:], "XE")
        if t:
            lin2("sbf0 sbf1 sbf2 pin%d" % t, "OT", T.OT[:], T.sbf[:].indirect(B2), ind="g")
        else:
            cp("sb3 sb3a pin0", "OT", T.OT[:], T.sb3[:].indirect(B2), "g")
            for k in range(3):
                act("sb3 sb3a", "sbf%d" % k, T.sbf[:, BW * k:BW * k + BW], T.sb3[:, BW * k:BW * k + BW], ACT.Copy)
        op([way("v", plain(TR), lambda: g.vector.transpose(T.OU[:], T.OT[:]))], "OT", "OU")
        cp("OU PERM", "OFF", T.OFF[:], T.OU[:].indirect(su("PERM")), "g")
        if t:
            act(zn, "INA", T.INA[:], Z, ACT.Sign, bias=-100.0 * U)
            mm("NIB N64 INA " + zn, "PD", [(T.PD[:, 0:TR], mb("NIB"), Z), (T.PD[:, 0:TR], mb("N64"), T.INA[:])])
            lin2("PD " + sp8n, "DP16", T.DP[:, 4096:4352], T.PD[:, 0:TR], None, sp8)
        else:
            lin2(zn + " " + spcn, "DP16", T.DP[:, 4096:4352], Z, -1.0, spc)
        relu2("JH " + ln_, "JK", T.JK[:], T.JH[:, 0:BW].indirect(BL), NONE, "g")
        mm("ONE C170 C171 JK I4", "PK", [(T.PK[:, 0:TR], ONE, T.C17[:])]
           + [(T.PK[:, 128 * h:128 * h + 128], T.JK[:, 128 * h:128 * h + 128], mf("I4")) for h in range(2)], last=False)
        for lo, hi in ROWS:
            tt("OFF %s %s%s" % (zn, wn, " yin%d" % t if hi > lo + 1 else ""), many("DP", hi, lo) + " ~DP", T.DP[:, TR * lo:TR * hi],
               win.indirect(T.OFF[:, 16 * lo:16 * hi]), T.zin[:, 2 * TR * t:2 * TR * t + TR * (hi - lo)], sub, "g")
        for lo, hi in ROWS:
            act(many("DP", hi, lo), many("RL", hi, lo) + " ~RL", T.RL[:, TR * lo:TR * hi], T.DP[:, TR * lo:TR * hi], ACT.Abs, bias=-64.0 * U)
            mm(many("RL", hi, lo) + " W8A", "PK",
               [(T.PK[:, 128 * h + k:128 * h + 128:16], T.RL[:, TR * k + 128 * h:TR * k + 128 * h + 128], w8("W8A"))
                for k in range(lo, hi) for h in range(2)], first=False, last=hi == 16)
        if t:
            ts(stn, "a", si("a"), st, 511, band)
            ts("a", "af", sm("af"), si("a"), -511.0, add)
        if not last:
            po = T.lout[:, 32 * t + 16:32 * t + 32]
            pair_lists(po, "pout%d" % t)
            send("pout%d" % t, "pin%d" % (t + 1), T.lin[:, 32 * t + 48:32 * t + 64], po, "ap%d" % t)
        lin2("FBT " + ln_, "FX", T.FX[:], T.FBT[:].indirect(BL), ind="g")
        ts("%s %s" % (ln_, lon), "LO", su("LO"), BL, 0.0625, mul, lo_, add)
        for h, bk in enumerate(("P0", "P1")):
            mm("FX EH0 EH1 ONEH CLH", bk, [(T[bk][:, 0:328], T.FX[:, 128 * h:128 * h + 128], T.EH[:]),
                                           (T[bk][:, 128:328], mh("ONEH", (0, 1)), T.CLH[0:1, :])])
            w_ = sm("WT", h, h + 1)
            ts(bk + " WT", "H%d" % h, T.H[:, 328 * h + 128:328 * h + 328], T[bk][:, 128:328], 0.0, eq, w_, mul)
            o, src = T.H[:, 328 * h:328 * h + 128], T[bk][:, 0:128]
            op([act_way(o, src, ACT.Relu, None, {"scale": w_, "bias": w_}), ts_way(o, src, 0.0, eq, w_, mul, None)],
               bk + " WT", "G%d" % h)
        mm("H0 H1 G0 G1 BIG BIGR", "P0", [(T.P0[:, 0:200], mb("BIGR", (0, 1)), T.BIG[0:1, :])]
           + [(T.P0[:, 0:200], T.H[:, 328 * h:328 * h + 128], T.H[:, 328 * h + 128:328 * h + 328]) for h in range(2)])
        lin2("P0", "MS", T.MS[:], T.P0[:, 0:200])
        tt("MS LO FX", "LK", T.LK[:], T.MS[:].indirect(su("LO")), T.FX[:], mul, "g")
        mms("LK BLK", "P1", field(0, "P1", [(T.LK, BLK)]))
        tt("P1 THB", "nsw", sh("nsw"), fld(0, "P1"), sm("THB"), ge)
        lin2("af", "ah", sh("ah"), sm("af"), None, 191.0)
        tt("nsw DB0 DB1", "ob", sm("ob"), sh("nsw"), sm("DB"), mul)
        tt("ob af", "ob", sm("ob"), sm("ob"), sm("af"), mn)
        as_list("ob", "SO", sm("ob"), 64, "MN", bk="P2")
        cp("P2", "OB", su("OB"), T.P2[:, 64:80])
        ts(stn, "q", sm("q"), st, BIG - 1 - 512 * (t + 2), le, -float(B), mul)
        tt("q af", "sq%d" % t, T.stin[:, 48 * t:48 * t + 16], sm("q"), sm("af"), mn)
        scan("RST PK", "PM", T.PM[:], T.RST[:, 0:TR], T.PK[:, 0:TR], mx, mn)
        ts("PM", "K1", si("K1"), best, 31, band)
        as_list("K1", "SK", si("K1"), 0, "M256", "J16")
        cp("PE", "OE", su("OE"), T.PE[:, 0:16])
        lin2("DP OE", "XD", T.XD[:], T.DP[:].indirect(su("OE")), ind="g")
        tt("DP OE XD", "FE", T.FE[:], T.DP[:].indirect(su("OE")), T.XD[:], sub, "g")
        tt("PK PM", "M2", T.M2[:, 1:TR], T.PK[:, 1:TR], T.PM[:, 0:TR - 1], mx)
        scan("RST M2", "PM2", T.PM2[:, 1:TR], T.RST[:, 16:TR + 15], T.M2[:, 1:TR], mx, mn)
        ts("PM2", "K2", si("K2"), best2, 31, band)
        as_list("K2", "SF", si("K2"), 16, "M256", "J16")
        cp("PE", "OF", su("OF"), T.PE[:, 16:32])
        lin2("DP OF", "XF", T.XF[:], T.DP[:].indirect(su("OF")), ind="g")
        tt("DP OF XF", "FF", T.FF[:], T.DP[:].indirect(su("OF")), T.XF[:], sub, "g")
        mm("IB NIB XD XF", "PD", [(T.PD[:, TR:], IB, T.XD[:]), (T.PD[:, TR:], mb("NIB"), T.XF[:])])
        act("PD", "AB", T.AB[:], T.PD[:, TR:], ACT.Abs, scale=1.0 / U)
        for u in range(2):
            lin2("FE " + LS_[u][1], "LE%d" % u, LE[u][:], T.FE[:], LS_[u][0])
        ts("K1", "tx", sm("tx"), si("K1"), 16.0, ge, 4096.0 * BIG, mul)
        tt("tx TX", "tx", sm("tx"), sm("tx"), sm("TX"), add)
        for gq in range(8):
            bk, a, u = ("P0", "P1", "PB")[gq % 3], 32 * (gq // 2), gq % 2
            blocks = ((0, 128), (128, 256))
            mms("FE ONE RW0 LE%d" % u, bk,
                [[(T[bk][:, c0:c0 + n], LE[u][a:a + 32, 128 * h:128 * h + 128], T.FE[a:a + 32, 0:n]),
                  (T[bk][:, 256 * h:256 * h + 128], mb("ONE", (a, a + 1)), T.RW[a:a + 1, 128 * h:128 * h + 128])]
                 for h, (c0, n) in enumerate(blocks)])
            for h, (c0, n) in enumerate(blocks):
                k = 8 * h + gq
                o, src = sm("ce", k, k + 1), T[bk][:, c0:c0 + n]
                act(bk + " tx", "ce%d JNK%d ~ce" % (k, k), T.JNK[:, B * gq + c0:B * gq + c0 + n], src, ACT.Relu,
                    bias=sm("tx", k, k + 1), scale=BIG, accum_out=o)
        mms("FE Wp IH ah Wh", "PA", field(0, "PA", [(T.FE, wh("Wp"))], [(mh("IH"), sh("ah"))]) + field(1, "PA", [(T.FE, wh("Wh"))]))
        mms("FE Wn ONEH CH Wc", "PA", field(2, "PA", [(T.FE, wh("Wn"))], [cf(1 + t)]) + field(3, "PA", [(T.FE, wh("Wc"))]))
        ts("PA", "e1", sm("e1"), fld(0), 0.0, eq)
        tt("PA e1", "e1", sm("e1"), sm("e1"), fld(1), mul)
        tt("PA e1", "Y1", T.Y3[:, 16:32], sm("e1"), fld(2), add)
        lin2("PA", "Y2", T.Y3[:, 32:48], fld(3), None, 3583.5)
        act("XD", "AA", T.AA[:], T.XD[:], ACT.Abs, bias=-64.0 * U)
        lin2("XD", "HB", T.HB[:], T.XD[:], 0.5, 127.75 * U)
        mm("IB HB " + zn, "PB", [(T.PB[:, 0:TR], IB, Z), (T.PB[:, 0:TR], IB, T.HB[:])], last=False)
        ces = sm("ce").indirect(su("SPR"))
        op([act_way(T.LS[:], ces, ACT.Sign, "g", {}), ts_way(T.LS[:], ces, 0.0, gt, None, None, "g")], "ce SPR", "LS")
        tt("ce SP3 Y0 Y1 Y2", "T3", T.T3[:], sm("ce").indirect(sm("SP3", 0, 3, pool="SU")), T.Y3[:], add, "g")
        son = "stout%d" % t
        tt("T3 sq%d sx%d %s" % (t, t, stn), son, T.stout[:, 48 * t:48 * t + 48], T.T3[:], T.stin[:, 48 * t:48 * t + 48], mn)
        lv, so, cd = [T.stout[:, 48 * t + 16 * k:48 * t + 16 * k + 16] for k in range(3)]
        mm("LS N512", "PB", [(T.PB[:, 128 * h:128 * h + 128], T.LS[:, 128 * h:128 * h + 128], mb("N512")) for h in range(2)], first=False)
        zo, zon = T.zout[:, TR * t:TR * t + TR], "zout%d" % t
        tt("PB AA", zon, zo, T.PB[:, 0:TR], T.AA[:], mx)
        if last:
            ts(zon, "INA", T.INA[:], zo, 64.0 * U, ge, -160.0 * U, mul)
            mm("IU INA " + zon, "PB", [(T.PB[:, 0:TR], mb("IU"), zo), (T.PB[:, 0:TR], mb("IU"), T.INA[:])])
            lin2("PB", zon, zo, T.PB[:, 0:TR])
        else:
            as_list(son, "SN", lv, 32, "MN")
            cp("PE", "lout%d" % t, T.lout[:, 32 * t:32 * t + 16], T.PE[:, 32:48])
            send("lout%d" % t, "lin%d" % (t + 1), T.lin[:, 32 * t + 32:32 * t + 48], T.lout[:, 32 * t:32 * t + 16], "al%d" % t)
        z1 = 2 * TR * (t + 1)
        send(zon, "zin%d" % (t + 1), T.zin[:, z1:z1 + TR], zo, "az%d" % t)
        if not last:
            send(zon, "yin%d" % (t + 1), T.zin[:, z1 + TR:z1 + 2 * TR], zo, "ay%d" % t)
        if last:
            ts(son, "a", si("a"), so, 511, band)
            spread("a MASK2a", "SN", T.SN, si("a"), "MASK2")
            mm("SN OHH", "PE", [(T.PE[:, 32:48], T.SN[:, 128 * h:128 * h + 128], sh("OHH")) for h in range(2)])
            lin2("PE", "bfo", T.bfo[:], T.PE[:, 32:48], None, 511.0)
            send("bfo", "bfi", T.bfi[:], T.bfo[:], "as%d" % t)
        else:
            send(son, "stin%d" % (t + 1), T.stin[:, 48 * t + 64:48 * t + 80], so, "as%d" % t)
        spread(son, "SC", T.SC, cd)
        to_list("SC", 64, T.W8F[:], "BLKF", bk="PA")
        cp("PA", "CU", su("CU"), T.PA[:, 64:80])
        if t == 1:
            ts("PA", "UT", sm("UT"), T.PA[:, 64:80], float(V), lt)
            tt("UT DM", "UT", sm("UT"), sm("UT"), sm("DM"), mul)
            tt("UT PA", "UT", sm("UT"), sm("UT"), T.PA[:, 64:80], mx)
            cp("UT", "UL", su("UL"), sm("UT"))

        tt("PM SL0 SL1", "sp", sh("sp"), best, sm("SL"), ge)
        mms("FE FF We Wf ONEH CH NI3 ah I4K nsw sp", "P2",
            field(0, "P2", [(T.FE, wh("We")), (T.FF, wh("Wf"))],
                  [cf(0), (mh("NI3"), sh("ah")), (mh("I4K"), sh("nsw")), (mh("I4K"), sh("sp"))]))
        mms("AB BLK IH L00 L01", "PD", field(1, "PD", [(T.AB, BLK)], [(mh("IH"), sh("L0"))]))
        lin2("sp", "sh", sm("sh"), sh("sp"), HELD)
        tt("sh PM2", "sh", sm("sh"), sm("sh"), best2, mx)
        lin2("sh SPR", "TH", T.TH[:], sm("sh").indirect(su("SPR")), ind="g")
        tt("PK TH", "SE", T.SE[:], T.PK[:, 0:TR], T.TH[:], le)
        if t:
            tt("PD AM", "j3", sm("j3"), fld(1, "PD"), si("AM"), ge)
        else:
            ts("PD", "j3", sm("j3"), fld(1, "PD"), 0.0, ge)
        jn = "j%d" % t
        jt = sh(jn)
        tt("P2 j3", jn, jt, sm("j3"), fld(0, "P2"), eq)
        tt(jn + " sp", "sg", sm("sg"), jt, sh("sp"), sub)
        tt("sg SPR SE", "UU", T.UU[:], sm("sg").indirect(su("SPR")), T.SE[:], mul, "g")
        mms("UU DG0 DG1 IT%d" % t, "P2", [[(T.P2[:, 128 * h:128 * h + 128], T.UU[:, 128 * h:128 * h + 128], x)
                                           for x in (T.DG[:, 128 * h:128 * h + 128], mb("IT%d" % t))] for h in range(2)])
        lin2("P2", "X", T.X[:], T.P2[:, 0:TR], None, -NONE)
        tt("X JK OB JH", "JH", T.JH[:].indirect(su("OB")), T.X[:], T.JK[:], add, "s")
        dma("y", "JH", "JF", T.JF[0:128:16, 0:16 * B], T.JH[:, 0:B], 100000)
        if t == 0:
            home_places()
        if t == 3:
            has_home()
        o = T.P0[:, 0:TR]
        items = [(o, mf("B1K"), T.X[:]), (o, T.RW[0:1, 512:640], T.RW[0:1, 0:TR]),
                 (o, T.RW[0:1, 640 + 128 * t:768 + 128 * t], T.RW[0:1, TR:2 * TR]),
                 (o, mb("HIB"), T.XD[:]), (o, mb("HIB"), T.XF[:]), (o, mb("UH"), T.AB[:]), (o, IB, Z)]
        rd = "B1K X RW HIB XD XF UH AB IB " + zn

        def pass1(u, n):
            sl = slice(n * u, n * u + n)
            lin2("JF HS", "R1%d" % u, T.R1[:, sl], T.JF[:].indirect(T.HS[:, n // 16 * u:n // 16 * (u + 1)]), ind="g")

        if last:
            mm(rd, "P0", items)
            act("P0", "YL", T.YL[:], o, ACT.Relu, scale=1.0 / U, bias=-64.0)
            dma("y", "YL", "", T.yx[:, WD - TR:WD], T.YL[:], 65536)
            op([("g", 300.0, 8000.0, lambda: g.dma_start(T.YO[:, 0:V], T.W[:, 0:V]), "d")], "Ws", "YO0 YO1 YO2")
            for u in range(3):
                sl = slice(1024 * u, 1024 * u + 1024)
                lin2("YO%d" % u, "YO%d" % u, T.YO[:, sl], T.YO[:, sl], 1.0 / U, -64.0)
            for u in range(2):
                sl = slice(V + 640 * u, V + 640 * u + 640)
                act("Wl", "YO%d" % (3 + u), T.YO[:, sl], T.W[:, sl], ACT.Abs, scale=1.0 / U)
                relu2("YO%d" % (3 + u), "YO%d" % (3 + u), T.YO[:, sl], T.YO[:, sl], -64.0)
            lin2(zn, "ZM", T.ZM[:], Z, 1.0 / U)
            cp("YO CU ZM", "YO", T.YO[:].indirect(su("CU")), T.ZM[:], "s")
            dma("y", "YO", "", T.yx[:, 0:2176], T.YO[:, 0:2176], 600000)
            dma("s", "YO", "", T.yx[:, 2176:WD - TR], T.YO[:, 2176:WD - TR], 1100000)
            for u in range(4):
                if u < 2:
                    sl = slice(768 * u, 768 * u + 768)
                    tt("JH HEL KM", "R1%d" % u, T.R1[:, sl], T.JH[:, 0:B].indirect(T.HEL[:, 48 * u:48 * u + 48]), T.KM[:, sl], mul, "g")
                else:
                    pass1(u, 768)
                mm("ZH ZA IH HH1 R1%d" % u, "P1", ([(T.P1[:, 0:192], mh("IH"), T.HH[:, 192:384])] if u == 0 else [])
                   + [(T.P1[:, 0:192], (T.ZA if u < 2 else T.ZH)[:, 15 - r:143 - r], T.R1[:, 192 * r:192 * r + 192])
                      for r in range(4 * u, 4 * u + 4)], first=u == 0, last=u == 3)
            tt("P1 SLI1", "YJ", T.YJ[:], T.P1[:, 0:192], T.SLI[:, 192:384], mx)
            dma("y", "YJ", "", T.yj[:], T.YJ[:], 98304)
            break

        mm(rd, "P0", items[:3], last=False)
        mm(rd, "P0", items[3:], first=False, last=False)
        mm("IB B8 S1 S2 FE FF", "P0", [(o, IB, T.B8[:]), (o, mh("S1"), T.FE[:]), (o, mh("S2"), T.FF[:])], first=False)
        relu2("P0 CBa", "Wl", T.W[:, V + TR * t:V + TR * t + TR], o, T.CB[:, 12 + t:13 + t])
        pv, pvn = (T.PV1, "PV1") if t == 1 else (T.PV0, "PV0")
        mms("IB IH FE S12 " + zn, "P1", [[(T.P1[:, 0:TR], IB, Z), (T.P1[:, 0:TR], mh("IH"), T.FE[:])]]
            + ([[(T.P1[:, TR:], mh("S12"), T.FE[:])]] if t else []))
        lin2("P1", pvn, pv[:], T.P1[:, 0:TR], -1.0, -64.0 * U)
        if t:
            lin2("P1", "SG", T.SG[:], T.P1[:, TR:])
        if t == 4:
            ts("PV1 UL W", "W", T.W[:].indirect(su("UL")), T.PV1[:], -1.0, mul, 0.0, add, "s")
        cp(pvn + " CU W", "W", T.W[:].indirect(su("CU")), pv[:], "s")
        for u, (bk, x0, x1) in enumerate(PARTS):
            for x in range(x0, x1):
                pass1(x, 512)
            sl = slice(32 * x0, 32 * x1)
            o = T[bk][:, 256:256 + 32 * (x1 - x0)]
            mm("ZH ONE C3K " + many("R1", x1, x0), bk, [(o, mb("ONE", (0, 1)), T.C3K[0:1, sl])]
               + [(o, T.ZH[:, 15 - r:143 - r], T.R1[:, 512 * x0 + r:512 * x1:16]) for r in range(16)])
            tt(bk + " SLI0", "JO%d" % u, T.JO[:, sl], o, T.SLI[:, sl], mx)
            cp("JO%d" % u, "JU%d" % u, T.JU[:, sl], T.JO[:, sl])
            for x in range(x0, x1):
                lin2("W JU%d" % u, "XE%d" % x, T.XE[:, 512 * x:512 * x + 512],
                     T.W[:, 0:V + TR * t + TR].indirect(T.JU[:, 32 * x:32 * x + 32]), ind="g")
        if t:
            tt(pvn + " SG CU W", "W", T.W[:].indirect(su("CU")), pv[:], T.SG[:], mul, "s")
        else:
            ts(pvn + " CU W", "W", T.W[:].indirect(su("CU")), pv[:], -1.0, mul, 0.0, add, "s")
        mms("O8 " + many("j", t + 1), "PA",
            [[(T.PA[:, 96 + 8 * u:104 + 8 * u], mh("O8"), sh("j%d" % x, 8 * h, 8 * h + 8)) for x in range(t + 1) for h in range(2)]
             for u in range(2)])
        cp("PA", "AM", si("AM"), T.PA[:, 96:112])
        ts("AM", "AM", si("AM"), si("AM"), 248, band)

    dma("y", "bfi", "", T.yb[:], T.bfi[:])
    dma("y", "zin6", "", T.yz[:], T.zin[:, 2 * S * TR:2 * S * TR + TR], 65536)

    count, seen, token, nd = {}, {}, {}, 0
    for n, (q, c0, c1, fn, kind), deps in put_in_order(ops):
        want = {}
        for d in deps:
            sem, val = token[d]
            if sem != own.get(q) or (q != "p" and (d, n) not in PLACED["soft"]):
                want[sem] = max(want.get(sem, 0), val)
        for sem, val in want.items():
            if seen.get((q, sem), 0) < val:
                Q[q].wait_ge(T.sem[sem], val)
                seen[(q, sem)] = val
        ins = fn()
        if kind == "c":
            sem, inc = own[q], 1
        elif kind == "d":
            sem, inc = "d%d" % nd, 16
            nd += 1
        else:
            sem, inc = kind, neng
            count["sent"] = count.get("sent", 0) + neng
        if kind in ("c", "d"):
            ins.then_inc(T.sem[sem], inc)
        count[sem] = count.get(sem, 0) + inc
        token[n] = (sem, count[sem])
    for sem, val in count.items():
        g.wait_ge(T.sem[sem], val)
